import numpy as np
import ml_dtypes


def mxq(x, axis, fmt="e4m3"):
    dtype, down = {"e4m3": (ml_dtypes.float8_e4m3fn, 7), "e5m2": (ml_dtypes.float8_e5m2, 14)}[fmt]
    v = np.moveaxis(np.asarray(x, np.float32).astype(ml_dtypes.bfloat16).astype(np.float64), axis, -1)
    blocks = v.reshape(v.shape[:-1] + (-1, 32))
    amax = np.abs(blocks).max(-1, keepdims=True)
    byte = np.maximum(np.where(amax > 0, np.frexp(amax)[1] - 1 + 127, 0) - down, 1)
    scale = np.exp2(byte - 127.0)
    codes = (blocks / scale).astype(np.float32).astype(dtype).astype(np.float64)
    return np.moveaxis((codes * scale).reshape(v.shape), -1, axis)


WIDE = False


def mx_kscale(k):
    if not WIDE:
        return np.ones(k)
    levels = np.array([10, -10, 5, -5, 0])
    if k % 512:
        return np.exp2(np.random.permutation(np.resize(levels, k // 32))).repeat(32)
    a = np.empty((k // 512, 16))
    for p in range(k // 512):
        a[p, :8] = np.random.permutation(np.resize(levels, 8))
        for g in range(8):
            far = levels[np.abs(levels - a[p, g]) >= 10]
            a[p, g + 8] = far[np.random.randint(len(far))]
    return np.exp2(a.ravel()).repeat(32)


BF16 = ml_dtypes.bfloat16


def bf(x):
    return np.asarray(x, np.float32).astype(BF16)


def f64(x):
    return np.asarray(x).astype(np.float64)


N, G, C = 256, 6, 512

GC = G * C

K = (
    (0, 1, 2, 3, 4, 5),
    (2, 0, 1, 5, 3, 4),
    (1, 2, 0, 4, 5, 3),
    (3, 5, 4, 0, 2, 1),
    (4, 3, 5, 1, 0, 2),
    (5, 4, 3, 2, 1, 0),
)


def draw0():
    s = mx_kscale(C)
    t = mx_kscale(C)
    x = np.random.standard_normal((N, G, C)) * s[None, None, :]
    w1 = np.random.standard_normal((G, C, C)) / np.sqrt(GC) / s[None, :, None]
    b1 = 0.4 * np.random.standard_normal(C)
    ls = (1.0 + 0.1 * np.random.standard_normal(C)) * t
    w2 = np.random.standard_normal((G, C, C)) / np.sqrt(GC) / t[None, :, None]
    return {"x": bf(x), "w1": bf(w1), "b1": bf(b1), "ls": bf(ls), "w2": bf(w2)}


def sigmoid(v):
    return 1.0 / (1.0 + np.exp(-v))


def all_products(a, w):
    n, g, c = a.shape
    j, _, d = w.shape
    rows = np.reshape(a, (n * g, c))
    cols = np.reshape(np.transpose(w, (1, 0, 2)), (c, j * d))
    return np.reshape(mxq(rows, 1, "e4m3") @ mxq(cols, 0, "e4m3"), (n, g, j, d))


def gather_sum(p, g):
    total = p[:, 0, K[0][g], :]
    for h in range(1, G):
        total = total + p[:, h, K[h][g], :]
    return total


def group_combine(p):
    return np.stack([gather_sum(p, g) for g in range(G)], axis=1)


def core(x, w1, b1, ls, w2):
    p = all_products(f64(x), f64(w1))
    y = group_combine(p) + f64(b1)[None, None, :]

    m = np.max(y, axis=1)
    e = y * sigmoid(m)[:, None, :] * f64(ls)[None, None, :]

    q = all_products(e, f64(w2))
    z = group_combine(q)
    return z


def e4m3fn_bytes(y):
    return np.clip(np.asarray(y, np.float64), -448.0, 448.0).astype(np.float32).astype(ml_dtypes.float8_e4m3fn).view(np.uint8)


def e4m3fn_values(b):
    return np.asarray(b, np.uint8).view(ml_dtypes.float8_e4m3fn).astype(np.float64)


def setup_inputs():
    d = draw0()
    x0 = np.asarray(d['w2']).astype(np.float64)
    s = (np.max(np.abs(x0), axis=(0, 2), keepdims=True) / 448.0).astype(np.float32)
    out = {}
    for k, v in d.items():
        if k == 'w2':
            out['w2_bytes'] = e4m3fn_bytes(x0 / s.astype(np.float64))
            out['w2_scale'] = s
        else:
            out[k] = v
    return out


def reference(x, w1, b1, ls, w2_bytes, w2_scale):
    return core(x, w1, b1, ls, e4m3fn_values(w2_bytes) * w2_scale.astype(np.float64))

@@ -1,0 +1,747 @@
+from contextlib import ExitStack
+
+import concourse.mybir as mybir
+from concourse.masks import make_identity
+
+N, G, C = 256, 6, 512
+FLOPS = 2 * 2 * N * G * C * G * C
+
+K = (
+    (0, 1, 2, 3, 4, 5),
+    (2, 0, 1, 5, 3, 4),
+    (1, 2, 0, 4, 5, 3),
+    (3, 5, 4, 0, 2, 1),
+    (4, 3, 5, 1, 0, 2),
+    (5, 4, 3, 2, 1, 0),
+)
+PAIRS = ((0, 3), (1, 5), (2, 4))
+POS = (0, 3, 1, 5, 2, 4)
+
+PROGRAM = (
+    ('T', 0, 'P'),
+    ('T', 1, 'P'),
+    ('E', 0, 'S'),
+    ('T', 2, 'P'),
+    ('E', 1, 'S'),
+    ('Q', 0, 0, 'V'),
+    ('Q', 0, 1, 'V'),
+    ('T', 3, 'P'),
+    ('E', 2, 'V'),
+    ('T', 4, 'P'),
+    ('E', 3, 'S'),
+    ('Q', 2, 0, 'V'),
+    ('T', 5, 'P'),
+    ('E', 4, 'S'),
+    ('Q', 1, 0, 'V'),
+    ('Q', 2, 1, 'V'),
+    ('E', 5, 'S'),
+    ('I', 0, 0, 'V'),
+    ('I', 0, 1, 'S'),
+    ('Q', 5, 0, 'V'),
+    ('Q', 1, 1, 'V'),
+    ('Q', 3, 0, 'V'),
+    ('q', 0, 0, 'V'),
+    ('I', 1, 0, 'S'),
+    ('Q', 4, 0, 'V'),
+    ('A', 0, 0, 0, 'P'),
+    ('I', 2, 0, 'V'),
+    ('A', 0, 0, 1, 'P'),
+    ('A', 0, 1, 0, 'P'),
+    ('q', 0, 1, 'V'),
+    ('A', 0, 1, 1, 'P'),
+    ('I', 1, 1, 'S'),
+    ('q', 2, 0, 'V'),
+    ('A', 0, 2, 0, 'P'),
+    ('q', 1, 0, 'V'),
+    ('A', 0, 2, 1, 'P'),
+    ('I', 3, 0, 'V'),
+    ('A', 1, 0, 0, 'P'),
+    ('A', 1, 0, 1, 'P'),
+    ('I', 3, 1, 'S'),
+    ('I', 4, 1, 'V'),
+    ('A', 1, 1, 0, 'P'),
+    ('A', 1, 1, 1, 'P'),
+    ('A', 1, 2, 0, 'P'),
+    ('q', 3, 0, 'V'),
+    ('A', 1, 2, 1, 'P'),
+    ('I', 4, 0, 'V'),
+    ('A', 2, 0, 0, 'P'),
+    ('I', 2, 1, 'S'),
+    ('A', 2, 0, 1, 'P'),
+    ('W', 0, 0, 'V'),
+    ('A', 2, 1, 0, 'P'),
+    ('I', 5, 0, 'V'),
+    ('A', 2, 1, 1, 'P'),
+    ('A', 2, 2, 0, 'P'),
+    ('W', 0, 2, 'S'),
+    ('A', 2, 2, 1, 'P'),
+    ('W', 0, 1, 'V'),
+    ('A', 3, 0, 0, 'P'),
+    ('W', 1, 2, 'V'),
+    ('W', 1, 3, 'S'),
+    ('A', 3, 0, 1, 'P'),
+    ('q', 2, 1, 'V'),
+    ('A', 3, 1, 0, 'P'),
+    ('q', 4, 0, 'V'),
+    ('A', 3, 1, 1, 'P'),
+    ('I', 5, 1, 'S'),
+    ('W', 2, 0, 'V'),
+    ('A', 3, 2, 0, 'P'),
+    ('q', 5, 0, 'V'),
+    ('A', 3, 2, 1, 'P'),
+    ('q', 4, 1, 'V'),
+    ('A', 4, 0, 0, 'P'),
+    ('W', 1, 1, 'V'),
+    ('A', 4, 0, 1, 'P'),
+    ('W', 4, 3, 'S'),
+    ('W', 0, 3, 'V'),
+    ('A', 4, 1, 0, 'P'),
+    ('W', 2, 2, 'V'),
+    ('A', 4, 1, 1, 'P'),
+    ('I2', 0, 'S'),
+    ('W', 1, 0, 'V'),
+    ('A', 4, 2, 0, 'P'),
+    ('W', 2, 1, 'V'),
+    ('A', 4, 2, 1, 'P'),
+    ('q', 5, 1, 'V'),
+    ('A', 5, 0, 0, 'P'),
+    ('q', 1, 1, 'V'),
+    ('A', 5, 0, 1, 'P'),
+    ('q', 3, 1, 'V'),
+    ('A', 5, 1, 0, 'P'),
+    ('A', 5, 1, 1, 'P'),
+    ('W', 3, 1, 'V'),
+    ('A', 5, 2, 0, 'P'),
+    ('W', 3, 0, 'V'),
+    ('A', 5, 2, 1, 'P'),
+    ('W', 5, 1, 'V'),
+    ('B2', 0, 0, 0, 0, 'P'),
+    ('Y', 'A', 0, 1, 'V'),
+    ('B2', 0, 0, 0, 1, 'P'),
+    ('B2', 0, 0, 0, 2, 'P'),
+    ('Y', 'A', 2, 1, 'S'),
+    ('B2', 0, 0, 0, 3, 'P'),
+    ('B2', 0, 0, 0, 4, 'P'),
+    ('B2', 0, 0, 0, 5, 'P'),
+    ('B2', 0, 0, 1, 0, 'P'),
+    ('B2', 0, 0, 1, 1, 'P'),
+    ('I2', 1, 'V'),
+    ('B2', 0, 0, 1, 2, 'P'),
+    ('B2', 0, 0, 1, 3, 'P'),
+    ('B2', 0, 0, 1, 4, 'P'),
+    ('Y', 'A', 0, 0, 'S'),
+    ('B2', 0, 0, 1, 5, 'P'),
+    ('B2', 0, 0, 2, 0, 'P'),
+    ('B2', 0, 0, 2, 1, 'P'),
+    ('B2', 0, 0, 2, 2, 'P'),
+    ('B2', 0, 0, 2, 3, 'P'),
+    ('B2', 0, 0, 2, 4, 'P'),
+    ('B2', 0, 0, 2, 5, 'P'),
+    ('Y', 'A', 1, 0, 'S'),
+    ('B2', 0, 1, 0, 0, 'P'),
+    ('B2', 0, 1, 0, 1, 'P'),
+    ('B2', 0, 1, 0, 2, 'P'),
+    ('B2', 0, 1, 0, 3, 'P'),
+    ('B2', 0, 1, 0, 4, 'P'),
+    ('B2', 0, 1, 0, 5, 'P'),
+    ('B2', 0, 1, 1, 0, 'P'),
+    ('q2', 0, 'V'),
+    ('Y', 'A', 2, 0, 'S'),
+    ('B2', 0, 1, 1, 1, 'P'),
+    ('B2', 0, 1, 1, 2, 'P'),
+    ('B2', 0, 1, 1, 3, 'P'),
+    ('B2', 0, 1, 1, 4, 'P'),
+    ('B2', 0, 1, 1, 5, 'P'),
+    ('B2', 0, 1, 2, 0, 'P'),
+    ('B2', 0, 1, 2, 1, 'P'),
+    ('W', 2, 3, 'S'),
+    ('B2', 0, 1, 2, 2, 'P'),
+    ('q2', 1, 'V'),
+    ('B2', 0, 1, 2, 3, 'P'),
+    ('B2', 0, 1, 2, 4, 'P'),
+    ('B2', 0, 1, 2, 5, 'P'),
+    ('C', 0, 0, 0, 0, 'P'),
+    ('C', 0, 0, 0, 1, 'P'),
+    ('C', 0, 0, 0, 2, 'P'),
+    ('C', 0, 0, 0, 3, 'P'),
+    ('Y', 'A', 1, 1, 'S'),
+    ('M0', 0, 'V'),
+    ('C', 0, 0, 0, 4, 'P'),
+    ('C', 0, 0, 0, 5, 'P'),
+    ('C', 0, 0, 1, 0, 'P'),
+    ('C', 0, 0, 1, 1, 'P'),
+    ('C', 0, 0, 1, 2, 'P'),
+    ('C', 0, 0, 1, 3, 'P'),
+    ('C', 0, 0, 1, 4, 'P'),
+    ('Y', 'B2', 0, 1, 'S'),
+    ('C', 0, 0, 1, 5, 'P'),
+    ('C', 0, 0, 2, 0, 'P'),
+    ('C', 0, 0, 2, 1, 'P'),
+    ('C', 0, 0, 2, 2, 'P'),
+    ('M0', 1, 'V'),
+    ('C', 0, 0, 2, 3, 'P'),
+    ('Y', 'B2', 0, 0, 'S'),
+    ('C', 0, 0, 2, 4, 'P'),
+    ('C', 0, 0, 2, 5, 'P'),
+    ('C', 0, 1, 0, 0, 'P'),
+    ('C', 0, 1, 0, 1, 'P'),
+    ('C', 0, 1, 0, 2, 'P'),
+    ('C', 0, 1, 0, 3, 'P'),
+    ('Y', 'C', 0, 0, 'S'),
+    ('C', 0, 1, 0, 4, 'P'),
+    ('C', 0, 1, 0, 5, 'P'),
+    ('C', 0, 1, 1, 0, 'P'),
+    ('M0', 'B2', 0, 'V'),
+    ('C', 0, 1, 1, 1, 'P'),
+    ('C', 0, 1, 1, 2, 'P'),
+    ('I2', 2, 'S'),
+    ('C', 0, 1, 1, 3, 'P'),
+    ('C', 0, 1, 1, 4, 'P'),
+    ('C', 0, 1, 1, 5, 'P'),
+    ('C', 0, 1, 2, 0, 'P'),
+    ('M1', 'A', 'V'),
+    ('C', 0, 1, 2, 1, 'P'),
+    ('C', 0, 1, 2, 2, 'P'),
+    ('C', 0, 1, 2, 3, 'P'),
+    ('C', 0, 1, 2, 4, 'P'),
+    ('C', 0, 1, 2, 5, 'P'),
+    ('B2', 1, 0, 0, 0, 'P'),
+    ('B2', 1, 0, 0, 1, 'P'),
+    ('Y', 'C', 0, 1, 'V'),
+    ('B2', 1, 0, 0, 2, 'P'),
+    ('B2', 1, 0, 0, 3, 'P'),
+    ('B2', 1, 0, 0, 4, 'P'),
+    ('B2', 1, 0, 0, 5, 'P'),
+    ('B2', 1, 0, 1, 0, 'P'),
+    ('B2', 1, 0, 1, 1, 'P'),
+    ('W', 4, 0, 'V'),
+    ('B2', 1, 0, 1, 2, 'P'),
+    ('B2', 1, 0, 1, 3, 'P'),
+    ('B2', 1, 0, 1, 4, 'P'),
+    ('M0', 'C', 0, 'V'),
+    ('B2', 1, 0, 1, 5, 'P'),
+    ('B2', 1, 0, 2, 0, 'P'),
+    ('B2', 1, 0, 2, 1, 'P'),
+    ('B2', 1, 0, 2, 2, 'P'),
+    ('B2', 1, 0, 2, 3, 'P'),
+    ('B2', 1, 0, 2, 4, 'P'),
+    ('M2', 'A', 'V'),
+    ('B2', 1, 0, 2, 5, 'P'),
+    ('B2', 1, 1, 0, 0, 'P'),
+    ('B2', 1, 1, 0, 1, 'P'),
+    ('B2', 1, 1, 0, 2, 'P'),
+    ('B2', 1, 1, 0, 3, 'P'),
+    ('B2', 1, 1, 0, 4, 'P'),
+    ('B2', 1, 1, 0, 5, 'P'),
+    ('M1', 'C', 0, 'V'),
+    ('W', 4, 1, 'S'),
+    ('B2', 1, 1, 1, 0, 'P'),
+    ('B2', 1, 1, 1, 1, 'P'),
+    ('B2', 1, 1, 1, 2, 'P'),
+    ('B2', 1, 1, 1, 3, 'P'),
+    ('W', 3, 3, 'V'),
+    ('B2', 1, 1, 1, 4, 'P'),
+    ('B2', 1, 1, 1, 5, 'P'),
+    ('B2', 1, 1, 2, 0, 'P'),
+    ('M2', 'C', 0, 'V'),
+    ('g', 'A', 'S'),
+    ('B2', 1, 1, 2, 1, 'P'),
+    ('B2', 1, 1, 2, 2, 'P'),
+    ('B2', 1, 1, 2, 3, 'P'),
+    ('B2', 1, 1, 2, 4, 'P'),
+    ('q2', 2, 'V'),
+    ('B2', 1, 1, 2, 5, 'P'),
+    ('C', 1, 0, 0, 0, 'P'),
+    ('C', 1, 0, 0, 1, 'P'),
+    ('C', 1, 0, 0, 2, 'P'),
+    ('g', 'C', 0, 'S'),
+    ('C', 1, 0, 0, 3, 'P'),
+    ('C', 1, 0, 0, 4, 'P'),
+    ('C', 1, 0, 0, 5, 'P'),
+    ('Y', 'B2', 1, 1, 'S'),
+    ('n', 'A', 1, 'V'),
+    ('C', 1, 0, 1, 0, 'P'),
+    ('C', 1, 0, 1, 1, 'P'),
+    ('n', 'C', 0, 'V'),
+    ('C', 1, 0, 1, 2, 'P'),
+    ('C', 1, 0, 1, 3, 'P'),
+    ('n', 'A', 0, 'V'),
+    ('C', 1, 0, 1, 4, 'P'),
+    ('n', 'B2', 0, 'V'),
+    ('C', 1, 0, 1, 5, 'P'),
+    ('Y', 'B2', 1, 0, 'S'),
+    ('C', 1, 0, 2, 0, 'P'),
+    ('W', 3, 2, 'V'),
+    ('C', 1, 0, 2, 1, 'P'),
+    ('C', 1, 0, 2, 2, 'P'),
+    ('C', 1, 0, 2, 3, 'P'),
+    ('e', 0, 0, 'V'),
+    ('C', 1, 0, 2, 4, 'P'),
+    ('W', 4, 2, 'S'),
+    ('C', 1, 0, 2, 5, 'P'),
+    ('C', 1, 1, 0, 0, 'P'),
+    ('C', 1, 1, 0, 1, 'P'),
+    ('C', 1, 1, 0, 2, 'P'),
+    ('C', 1, 1, 0, 3, 'P'),
+    ('C', 1, 1, 0, 4, 'P'),
+    ('C', 1, 1, 0, 5, 'P'),
+    ('C', 1, 1, 1, 0, 'P'),
+    ('I2', 3, 'S'),
+    ('e', 0, 1, 'V'),
+    ('C', 1, 1, 1, 1, 'P'),
+    ('C', 1, 1, 1, 2, 'P'),
+    ('C', 1, 1, 1, 3, 'P'),
+    ('C', 1, 1, 1, 4, 'P'),
+    ('C', 1, 1, 1, 5, 'P'),
+    ('C', 1, 1, 2, 0, 'P'),
+    ('C', 1, 1, 2, 1, 'P'),
+    ('C', 1, 1, 2, 2, 'P'),
+    ('eq', 0, 0, 'V'),
+    ('C', 1, 1, 2, 3, 'P'),
+    ('C', 1, 1, 2, 4, 'P'),
+    ('e', 0, 2, 'V'),
+    ('C', 1, 1, 2, 5, 'P'),
+    ('D', 0, 0, 0, 'P'),
+    ('D', 0, 0, 1, 'P'),
+    ('eq', 0, 1, 'V'),
+    ('D', 0, 0, 2, 'P'),
+    ('e', 0, 3, 'V'),
+    ('D', 0, 1, 0, 'P'),
+    ('D', 0, 1, 1, 'P'),
+    ('eq', 0, 2, 'V'),
+    ('D', 0, 1, 2, 'P'),
+    ('eq', 0, 3, 'V'),
+    ('Y', 'C', 1, 0, 'S'),
+    ('D', 0, 2, 0, 'P'),
+    ('e', 0, 4, 'V'),
+    ('D', 0, 2, 1, 'P'),
+    ('Y', 'C', 1, 1, 'S'),
+    ('D', 0, 2, 2, 'P'),
+    ('e', 0, 5, 'V'),
+    ('I2', 4, 'S'),
+    ('D', 0, 3, 0, 'P'),
+    ('D', 0, 3, 1, 'P'),
+    ('eq', 0, 4, 'V'),
+    ('D', 0, 3, 2, 'P'),
+    ('eq', 0, 5, 'V'),
+    ('M0', 'B2', 1, 'V'),
+    ('D', 0, 4, 0, 'P'),
+    ('D', 0, 4, 1, 'P'),
+    ('M0', 'C', 1, 'V'),
+    ('D', 0, 4, 2, 'P'),
+    ('q2', 3, 'V'),
+    ('D', 0, 5, 0, 'P'),
+    ('D', 0, 5, 1, 'P'),
+    ('D', 0, 5, 2, 'P'),
+    ('W', 5, 0, 'V'),
+    ('W', 5, 3, 'S'),
+    ('D', 0, 0, 3, 'P'),
+    ('M1', 'C', 1, 'V'),
+    ('D', 0, 1, 3, 'P'),
+    ('q2', 4, 'V'),
+    ('W', 5, 2, 'S'),
+    ('D', 0, 2, 3, 'P'),
+    ('D', 0, 3, 3, 'P'),
+    ('M2', 'C', 1, 'V'),
+    ('D', 0, 4, 3, 'P'),
+    ('I2', 5, 'V'),
+    ('g', 'C', 1, 'S'),
+    ('D', 0, 5, 3, 'P'),
+    ('D', 0, 0, 4, 'P'),
+    ('D', 0, 1, 4, 'P'),
+    ('D', 0, 2, 4, 'P'),
+    ('D', 0, 3, 4, 'P'),
+    ('n', 'B2', 1, 'V'),
+    ('q2', 5, 'V'),
+    ('D', 0, 4, 4, 'P'),
+    ('D', 0, 5, 4, 'P'),
+    ('n', 'C', 1, 'V'),
+    ('D', 0, 0, 5, 'P'),
+    ('e', 1, 0, 'V'),
+    ('D', 0, 1, 5, 'P'),
+    ('O', 0, 5, 'S'),
+    ('D', 0, 2, 5, 'P'),
+    ('e', 1, 1, 'V'),
+    ('D', 0, 3, 5, 'P'),
+    ('O', 0, 1, 'S'),
+    ('D', 0, 4, 5, 'P'),
+    ('D', 0, 5, 5, 'P'),
+    ('eq', 1, 0, 'V'),
+    ('O', 0, 0, 'S'),
+    ('eq', 1, 1, 'V'),
+    ('D', 1, 0, 0, 'P'),
+    ('e', 1, 2, 'V'),
+    ('D', 1, 0, 1, 'P'),
+    ('O', 0, 2, 'S'),
+    ('D', 1, 0, 2, 'P'),
+    ('eq', 1, 2, 'V'),
+    ('D', 1, 1, 3, 'P'),
+    ('O', 0, 3, 'S'),
+    ('e', 1, 3, 'V'),
+    ('D', 1, 1, 5, 'P'),
+    ('D', 1, 1, 4, 'P'),
+    ('O', 0, 4, 'S'),
+    ('D', 1, 2, 2, 'P'),
+    ('eq', 1, 3, 'V'),
+    ('e', 1, 4, 'V'),
+    ('D', 1, 2, 0, 'P'),
+    ('D', 1, 2, 1, 'P'),
+    ('D', 1, 3, 5, 'P'),
+    ('eq', 1, 4, 'V'),
+    ('D', 1, 3, 4, 'P'),
+    ('e', 1, 5, 'V'),
+    ('D', 1, 3, 3, 'P'),
+    ('D', 1, 4, 1, 'P'),
+    ('D', 1, 4, 2, 'P'),
+    ('eq', 1, 5, 'V'),
+    ('D', 1, 4, 0, 'P'),
+    ('D', 1, 5, 4, 'P'),
+    ('D', 1, 5, 3, 'P'),
+    ('O', 1, 0, 'S'),
+    ('D', 1, 5, 5, 'P'),
+    ('O', 1, 1, 'V'),
+    ('D', 1, 0, 3, 'P'),
+    ('O', 1, 2, 'S'),
+    ('D', 1, 1, 0, 'P'),
+    ('D', 1, 2, 5, 'P'),
+    ('D', 1, 3, 2, 'P'),
+    ('D', 1, 4, 4, 'P'),
+    ('D', 1, 5, 1, 'P'),
+    ('D', 1, 0, 4, 'P'),
+    ('O', 1, 3, 'V'),
+    ('D', 1, 1, 2, 'P'),
+    ('D', 1, 2, 3, 'P'),
+    ('D', 1, 3, 1, 'P'),
+    ('D', 1, 4, 5, 'P'),
+    ('D', 1, 5, 0, 'P'),
+    ('D', 1, 0, 5, 'P'),
+    ('O', 1, 4, 'S'),
+    ('D', 1, 1, 1, 'P'),
+    ('D', 1, 2, 4, 'P'),
+    ('D', 1, 3, 0, 'P'),
+    ('D', 1, 4, 3, 'P'),
+    ('D', 1, 5, 2, 'P'),
+    ('O', 1, 5, 'V'),
+)
+
+P = 128
+XH = 2
+F32 = mybir.dt.float32
+BF16 = mybir.dt.bfloat16
+U32 = mybir.dt.uint32
+U8 = mybir.dt.uint8
+FP8X4 = mybir.dt.float8_e4m3fn_x4
+FP8 = mybir.dt.float8_e4m3fn
+ACT = mybir.ActivationFunctionType
+ALU = mybir.AluOpType
+
+
+def tile_dihedralthreegroupblock_kernel(tc, x, w1, b1, ls, w2_bytes, w2_scale, out):
+    nc = tc.nc
+    with ExitStack() as ctx:
+        keep = ctx.enter_context(tc.tile_pool(name="keep", bufs=1))
+        work = ctx.enter_context(tc.tile_pool(name="work", bufs=3))
+        psum = ctx.enter_context(tc.psum_pool(name="psum", bufs=8))
+        ctx.enter_context(tc.manual_schedule())
+
+        def bank(shape):
+            return psum.tile(shape, F32, name="bank")
+
+        b1_sb = keep.tile([P, 4], BF16, name="b1_sb")
+        ls_sb = keep.tile([P, 4], BF16, name="ls_sb")
+        sc_sb = keep.tile([P, 4], F32, name="sc_sb")
+        nc.scalar.dma_start(out=sc_sb[:], in_=w2_scale.rearrange("o (p t) z -> p (o t z)", t=4))
+        nc.scalar.dma_start(out=b1_sb[:], in_=b1.rearrange("(p t) -> p t", t=4))
+        nc.scalar.dma_start(out=ls_sb[:], in_=ls.rearrange("(p t) -> p t", t=4))
+
+        xs = []
+        for i in range(G // XH):
+            t = keep.tile([P, 2, XH, C], BF16, name="xs%d" % i, align_bytes=64)
+            nc.sync.dma_start(
+                out=t[:].rearrange("p a h c -> p a (h c)"),
+                in_=x[:, XH * i : XH * i + XH, :].rearrange("(a p) h c -> p a (h c)", p=P),
+            )
+            xs.append(t)
+        w1_raw = []
+        for j in range(G):
+            t = keep.tile([P, 4, C], BF16, name="w1_raw%d" % j, align_bytes=64)
+            nc.sync.dma_start(out=t[:], in_=w1[j].rearrange("(p t) d -> p t d", t=4))
+            w1_raw.append(t)
+        w2_raw = []
+        for j in range(G):
+            t = keep.tile([P, 4, C], U8, name="w2_raw%d" % j, align_bytes=64)
+            nc.sync.dma_start(out=t[:], in_=w2_bytes[j].rearrange("(p t) d -> p t d", t=4))
+            w2_raw.append(t)
+
+        ident = keep.tile([P, P], F32, name="ident")
+        make_identity(nc, ident[:])
+        warm = keep.tile([P, 1], F32, name="warm")
+        nc.gpsimd.memset(warm[:], 0.0)
+        nc.scalar.activation(out=warm[:], in_=warm[:], func=ACT.Sigmoid)
+
+        xc = [keep.tile([P, 3, N], U32, name="xc%d" % i, align_bytes=64) for i in range(3)]
+        xsc = [keep.tile([P, 3, N], U8, name="xsc%d" % i, align_bytes=64) for i in range(3)]
+        w1c = [keep.tile([P, C], U32, name="w1c%d" % j, align_bytes=64) for j in range(G)]
+        w1s = [keep.tile([P, C], U8, name="w1s%d" % j, align_bytes=64) for j in range(G)]
+        w2c = [keep.tile([P, C], U32, name="w2c%d" % j, align_bytes=64) for j in range(G)]
+        w2s = [keep.tile([P, C], U8, name="w2s%d" % j, align_bytes=64) for j in range(G)]
+        y_sb = keep.tile([P, 4, G, N], F32, name="y_sb", align_bytes=64)
+        m3 = keep.tile([P, 4, 3, N], F32, name="m3", align_bytes=64)
+        m_sb = keep.tile([P, 4, N], F32, name="m_sb", align_bytes=64)
+        s_sb = keep.tile([P, 4, N], F32, name="s_sb", align_bytes=64)
+        eg = {}
+        ec = [[keep.tile([P, 2, P], U32, name="ec%d_%d" % (a, q), align_bytes=64) for q in range(3)] for a in range(2)]
+        es = [[keep.tile([P, 2, P], U8, name="es%d_%d" % (a, q), align_bytes=64) for q in range(3)] for a in range(2)]
+        xg = [keep.tile([P, N, 4], BF16, name="xg", align_bytes=64, bufs=6) for h in range(G)]
+        tb = {}
+
+        def copy(eng, out, in_):
+            if eng == "S":
+                nc.scalar.copy(out=out, in_=in_)
+            else:
+                nc.vector.tensor_copy(out=out, in_=in_)
+
+        def x_transpose(h):
+            b = bank([P, 2, 2, P])
+            for a in range(2):
+                words = xs[h // XH][:, a, h % XH, :].bitcast(F32)
+                for u in range(2):
+                    nc.tensor.transpose(b[:, a, u, :], words[:, u : C // 2 : 2], ident[:])
+            tb[h] = b
+
+        def x_evac(h, eng):
+            copy(
+                eng,
+                xg[h][:].rearrange("p n t -> p (n t)").bitcast(F32).rearrange("p (a r u) -> p a r u", a=2, u=2),
+                tb[h][:].rearrange("p a u r -> p a r u"),
+            )
+
+        def x_quant(h, dup=False):
+            q = [i for i in range(3) if h in PAIRS[i]][0]
+            slot = 2 if dup else PAIRS[q].index(h)
+            nc.vector.quantize_mx(
+                out=xc[q][:, slot, :].bitcast(FP8X4),
+                scales=xsc[q][:, slot, :],
+                in_=xg[h][:].rearrange("p n t -> p (n t)"),
+            )
+
+        wg = {}
+
+        def w1_inter(j, th, eng):
+            g = work.tile([P, 2, P, 4], BF16, name="wg", align_bytes=64, bufs=8)
+            copy(
+                eng,
+                g[:],
+                w1_raw[j][:].rearrange("p j (m t) -> p t m j", t=4)[:, 2 * th : 2 * th + 2],
+            )
+            wg[j, th] = g
+
+        def w1_quant(j, th):
+            cols = slice(2 * th * P, 2 * (th + 1) * P)
+            nc.vector.quantize_mx(
+                out=w1c[j][:, cols].bitcast(FP8X4),
+                scales=w1s[j][:, cols],
+                in_=wg[j, th][:].rearrange("p t m j -> p (t m j)"),
+            )
+
+        wide = {}
+        grp = {}
+
+        def w2_widen(j, t, eng):
+            if j not in wide:
+                wide[j] = work.tile([P, 4, C], BF16, name="wide", align_bytes=64, bufs=6)
+            src = w2_raw[j][:, t, :].bitcast(FP8)
+            if eng == "S":
+                nc.scalar.activation(out=wide[j][:, t, :], in_=src, func=ACT.Copy, scale=sc_sb[:, t : t + 1])
+            else:
+                nc.vector.tensor_scalar(
+                    out=wide[j][:, t, :], in0=src, scalar1=sc_sb[:, t : t + 1], scalar2=None, op0=ALU.mult
+                )
+
+        def w2_inter(j, eng):
+            grp[j] = work.tile([P, C, 4], BF16, name="grp", align_bytes=64, bufs=6)
+            copy(
+                eng,
+                grp[j][:].rearrange("p (c i) t -> p c t i", i=4),
+                wide[j][:].rearrange("p t (c i) -> p c t i", i=4),
+            )
+
+        def w2_quant(j):
+            nc.vector.quantize_mx(
+                out=w2c[j][:].bitcast(FP8X4), scales=w2s[j][:], in_=grp[j][:].rearrange("p n t -> p (n t)")
+            )
+
+        def window(gp, j):
+            ha, hb = [[h for h in range(G) if K[h][g] == j][0] for g in PAIRS[gp]]
+            for q in range(3):
+                if PAIRS[q] == (ha, hb):
+                    return q, 0
+                if PAIRS[q] == (hb, ha):
+                    return q, 1
+            raise ValueError("no window")
+
+        def conv1_pair(acc, t, gp, j, first, last):
+            q, s0 = window(gp, j)
+            cols = slice(t * P, (t + 1) * P)
+            nc.tensor.matmul_mx(
+                out=acc[:],
+                lhsT=w1c[j][:, cols].bitcast(FP8X4),
+                lhsT_scale=w1s[j][:, cols],
+                rhs=xc[q][:, s0 : s0 + 2, :].rearrange("p s n -> p (s n)").bitcast(FP8X4),
+                rhs_scale=xsc[q][:, s0 : s0 + 2, :].rearrange("p s n -> p (s n)"),
+                start=first,
+                stop=last,
+            )
+
+        def conv1_half(acc, t, pos, a, i):
+            h = POS[i]
+            j = K[h][POS[pos]]
+            cols = slice(t * P, (t + 1) * P)
+            n = slice(a * P, (a + 1) * P)
+            nc.tensor.matmul_mx(
+                out=acc,
+                lhsT=w1c[j][:, cols].bitcast(FP8X4),
+                lhsT_scale=w1s[j][:, cols],
+                rhs=xc[i // 2][:, i % 2, n].bitcast(FP8X4),
+                rhs_scale=xsc[i // 2][:, i % 2, n],
+                start=(i == 0),
+                stop=(i == G - 1),
+            )
+
+        def y_evac(out, in_, t, eng):
+            if eng == "S":
+                nc.scalar.activation(out=out, in_=in_, func=ACT.Identity, bias=b1_sb[:, t : t + 1])
+            else:
+                nc.vector.tensor_scalar(out=out, in0=in_, scalar1=b1_sb[:, t : t + 1], scalar2=None, op0=ALU.add)
+
+        def pool_max0(t, n):
+            nc.vector.tensor_tensor(out=m3[:, t, :, n], in0=y_sb[:, t, 0:3, n], in1=y_sb[:, t, 3:6, n], op=ALU.max)
+
+        def pool_max1(t, n):
+            nc.vector.tensor_tensor(out=m_sb[:, t, n], in0=m3[:, t, 0, n], in1=m3[:, t, 1, n], op=ALU.max)
+
+        def pool_max2(t, n):
+            nc.vector.tensor_tensor(out=m_sb[:, t, n], in0=m_sb[:, t, n], in1=m3[:, t, 2, n], op=ALU.max)
+
+        def gate(t, n):
+            nc.scalar.activation(out=s_sb[:, t, n], in_=m_sb[:, t, n], func=ACT.Sigmoid)
+
+        def gain(t, n):
+            nc.vector.tensor_scalar(
+                out=s_sb[:, t, n], in0=s_sb[:, t, n], scalar1=ls_sb[:, t : t + 1], scalar2=None, op0=ALU.mult
+            )
+
+        def e_mult(a, pos):
+            n = slice(a * P, (a + 1) * P)
+            if (a, pos // 2) not in eg:
+                eg[a, pos // 2] = keep.tile([P, 2, P, 4], BF16, name="eg", tag="xg", align_bytes=64, bufs=6)
+            nc.vector.tensor_tensor(
+                out=eg[a, pos // 2][:, pos % 2].rearrange("p (c i) t -> p c t i", i=4),
+                in0=y_sb[:, :, pos, n].rearrange("p t (c i) -> p c t i", i=4),
+                in1=s_sb[:, :, n].rearrange("p t (c i) -> p c t i", i=4),
+                op=ALU.mult,
+            )
+
+        def e_quant(a, pos):
+            nc.vector.quantize_mx(
+                out=ec[a][pos // 2][:, pos % 2, :].bitcast(FP8X4),
+                scales=es[a][pos // 2][:, pos % 2, :],
+                in_=eg[a, pos // 2][:, pos % 2].rearrange("p n t -> p (n t)"),
+            )
+
+        def conv2(acc, a, h, j, first, last):
+            i = POS.index(h)
+            nc.tensor.matmul_mx(
+                out=acc[:],
+                lhsT=ec[a][i // 2][:, i % 2, :].bitcast(FP8X4),
+                lhsT_scale=es[a][i // 2][:, i % 2, :],
+                rhs=w2c[j][:].bitcast(FP8X4),
+                rhs_scale=w2s[j][:],
+                start=first,
+                stop=last,
+            )
+
+        def store(acc, a, g, eng):
+            o = work.tile([P, C], F32, name="o_sb", bufs=4)
+            copy(eng, o[:], acc[:])
+            nc.sync.dma_start(out=out[a * P : (a + 1) * P, g, :], in_=o[:])
+
+        ALL = slice(0, N)
+        HALF = (slice(0, P), slice(P, N))
+        accs = {}
+        count = {}
+
+        def group(key, shape):
+            if key not in accs:
+                accs[key] = bank(shape)
+            return accs[key]
+
+        def nth(key):
+            count[key] = count.get(key, 0) + 1
+            return count[key]
+
+        def flat(ap):
+            return ap.rearrange("p g n -> p (g n)")
+
+        for step in PROGRAM:
+            kind, arg, eng = step[0], step[1:-1], step[-1]
+            if kind == "T":
+                x_transpose(arg[0])
+            elif kind == "E":
+                x_evac(arg[0], eng)
+            elif kind == "Q":
+                x_quant(arg[0], dup=(arg[1] == 1))
+            elif kind == "I":
+                w1_inter(arg[0], arg[1], eng)
+            elif kind == "q":
+                w1_quant(arg[0], arg[1])
+            elif kind == "W":
+                w2_widen(arg[0], arg[1], eng)
+            elif kind == "I2":
+                w2_inter(arg[0], eng)
+            elif kind == "q2":
+                w2_quant(arg[0])
+            elif kind == "A":
+                j, gp, t = arg
+                n = nth(("A", gp, t))
+                conv1_pair(group(("A", gp, t), [P, C]), t, gp, j, n == 1, n == G)
+            elif kind in ("B2", "C"):
+                a, k, i, z = arg
+                t = 2 if kind == "B2" else 3
+                conv1_half(group((kind, a, k), [P, 3, P])[:, i, :], t, 3 * k + i, a, z)
+            elif kind == "Y":
+                if arg[0] == "A":
+                    gp, t = arg[1:]
+                    y_evac(flat(y_sb[:, t, 2 * gp : 2 * gp + 2, :]), accs["A", gp, t][:], t, eng)
+                else:
+                    t = 2 if arg[0] == "B2" else 3
+                    a, k = arg[1:]
+                    y_evac(y_sb[:, t, 3 * k : 3 * k + 3, HALF[a]], accs[arg[0], a, k][:], t, eng)
+            elif kind == "M0":
+                if arg[0] in (0, 1):
+                    pool_max0(arg[0], ALL)
+                else:
+                    pool_max0(2 if arg[0] == "B2" else 3, HALF[arg[1]])
+            elif kind in ("M1", "M2", "g"):
+                f = {"M1": pool_max1, "M2": pool_max2, "g": gate}[kind]
+                if arg[0] == "A":
+                    f(slice(0, 2), ALL)
+                else:
+                    f(slice(2, 4), HALF[arg[1]])
+            elif kind == "n":
+                if arg[0] == "A":
+                    gain(arg[1], ALL)
+                else:
+                    gain(2 if arg[0] == "B2" else 3, HALF[arg[1]])
+            elif kind == "e":
+                e_mult(arg[0], arg[1])
+            elif kind == "eq":
+                e_quant(arg[0], arg[1])
+            elif kind == "D":
+                a, pos, j = arg
+                h = POS[pos]
+                g = [gg for gg in range(G) if K[h][gg] == j][0]
+                n = nth(("D", a, g))
+                conv2(group(("D", a, g), [P, C]), a, h, j, n == 1, n == G)
+            elif kind == "O":
+                store(accs["D", arg[0], arg[1]], arg[0], arg[1], eng)

@@ -17,415 +17,579 @@ K = (
 PAIRS = ((0, 3), (1, 5), (2, 4))
 POS = (0, 3, 1, 5, 2, 4)
 
+LOADS = (('x', 0, 0), ('x', 0, 1), ('x', 0, 2), ('w1', 0), ('w1', 1), ('x', 1, 0), ('x', 1, 1), ('x', 1, 2), ('w1', 2), ('w1', 3), ('w1', 4), ('w1', 5), ('w2', 0), ('w2', 1), ('w2', 2), ('w2', 3), ('w2', 4), ('w2', 5))
+
+SLOTS = {
+    ('T', 0, 0): 0,
+    ('T', 0, 1): 1,
+    ('T', 0, 2): 2,
+    ('A', 0, 0, 0): 3,
+    ('A', 0, 1, 0): 4,
+    ('A', 0, 0, 1): 5,
+    ('A', 0, 1, 1): 6,
+    ('A', 0, 0, 2): 7,
+    ('A', 0, 1, 2): 0,
+    ('T', 1, 0): 1,
+    ('T', 1, 1): 2,
+    ('T', 1, 2): 1,
+    ('A', 1, 0, 0): 2,
+    ('A', 1, 0, 1): 1,
+    ('A', 0, 2, 0): 3,
+    ('A', 0, 2, 1): 4,
+    ('A', 0, 2, 2): 5,
+    ('A', 0, 3, 0): 6,
+    ('A', 0, 3, 1): 7,
+    ('A', 0, 3, 2): 0,
+    ('A', 1, 0, 2): 2,
+    ('A', 1, 1, 0): 1,
+    ('A', 1, 1, 1): 3,
+    ('A', 1, 1, 2): 4,
+    ('A', 1, 2, 0): 5,
+    ('A', 1, 2, 1): 6,
+    ('A', 1, 2, 2): 7,
+    ('A', 1, 3, 0): 0,
+    ('A', 1, 3, 1): 2,
+    ('A', 1, 3, 2): 1,
+    ('D', 0, 0, 0): 3,
+    ('D', 0, 0, 1): 4,
+    ('D', 0, 0, 2): 5,
+    ('D', 0, 0, 3): 6,
+    ('D', 0, 0, 4): 7,
+    ('D', 0, 0, 5): 0,
+    ('D', 1, 0, 0): 2,
+    ('D', 1, 0, 1): 1,
+    ('D', 1, 0, 2): 7,
+    ('D', 1, 0, 3): 6,
+    ('D', 1, 0, 4): 0,
+    ('D', 1, 0, 5): 4,
+    ('D', 0, 1, 0): 3,
+    ('D', 0, 1, 3): 5,
+    ('D', 0, 1, 1): 0,
+    ('D', 0, 1, 5): 6,
+    ('D', 0, 1, 2): 4,
+    ('D', 0, 1, 4): 1,
+    ('D', 1, 1, 0): 2,
+    ('D', 1, 1, 1): 7,
+    ('D', 1, 1, 2): 6,
+    ('D', 1, 1, 3): 0,
+    ('D', 1, 1, 4): 5,
+    ('D', 1, 1, 5): 3,
+}
+
 PROGRAM = (
-    ('T', 0, 'P'),
-    ('T', 1, 'P'),
-    ('E', 0, 'S'),
-    ('T', 2, 'P'),
-    ('E', 1, 'S'),
-    ('Q', 0, 0, 'V'),
-    ('Q', 0, 1, 'V'),
-    ('T', 3, 'P'),
-    ('E', 2, 'V'),
-    ('T', 4, 'P'),
-    ('E', 3, 'S'),
-    ('Q', 2, 0, 'V'),
-    ('T', 5, 'P'),
-    ('E', 4, 'S'),
-    ('Q', 1, 0, 'V'),
-    ('Q', 2, 1, 'V'),
-    ('E', 5, 'S'),
+    ('T', 0, 0, 'P'),
+    ('T', 0, 1, 'P'),
+    ('E', 0, 0, 'S'),
+    ('T', 0, 2, 'P'),
+    ('E', 0, 1, 'S'),
+    ('Q', 0, 0, 1, 'V'),
+    ('Q', 0, 1, 1, 'V'),
+    ('Q', 0, 0, 0, 'V'),
+    ('E', 0, 2, 'S'),
+    ('Q', 0, 1, 0, 'V'),
+    ('Q', 0, 3, 0, 'V'),
     ('I', 0, 0, 'V'),
     ('I', 0, 1, 'S'),
-    ('Q', 5, 0, 'V'),
-    ('Q', 1, 1, 'V'),
-    ('Q', 3, 0, 'V'),
+    ('Q', 0, 4, 0, 'V'),
     ('q', 0, 0, 'V'),
-    ('I', 1, 0, 'S'),
-    ('Q', 4, 0, 'V'),
-    ('A', 0, 0, 0, 'P'),
-    ('I', 2, 0, 'V'),
-    ('A', 0, 0, 1, 'P'),
-    ('A', 0, 1, 0, 'P'),
-    ('q', 0, 1, 'V'),
-    ('A', 0, 1, 1, 'P'),
+    ('Q', 0, 5, 0, 'V'),
+    ('A', 0, 0, 0, 0, 'P'),
+    ('Q', 0, 2, 0, 'V'),
     ('I', 1, 1, 'S'),
-    ('q', 2, 0, 'V'),
-    ('A', 0, 2, 0, 'P'),
+    ('I', 1, 0, 'V'),
+    ('A', 0, 1, 0, 0, 'P'),
+    ('A', 0, 0, 1, 0, 'P'),
+    ('A', 0, 1, 1, 0, 'P'),
+    ('A', 0, 0, 2, 0, 'P'),
+    ('A', 0, 1, 2, 0, 'P'),
+    ('Q', 0, 2, 1, 'V'),
+    ('T', 1, 0, 'P'),
     ('q', 1, 0, 'V'),
-    ('A', 0, 2, 1, 'P'),
-    ('I', 3, 0, 'V'),
-    ('A', 1, 0, 0, 'P'),
-    ('A', 1, 0, 1, 'P'),
-    ('I', 3, 1, 'S'),
-    ('I', 4, 1, 'V'),
-    ('A', 1, 1, 0, 'P'),
-    ('A', 1, 1, 1, 'P'),
-    ('A', 1, 2, 0, 'P'),
-    ('q', 3, 0, 'V'),
-    ('A', 1, 2, 1, 'P'),
-    ('I', 4, 0, 'V'),
-    ('A', 2, 0, 0, 'P'),
+    ('A', 0, 0, 0, 1, 'P'),
+    ('E', 1, 0, 'S'),
+    ('A', 0, 1, 0, 1, 'P'),
+    ('A', 0, 0, 1, 1, 'P'),
+    ('A', 0, 1, 1, 1, 'P'),
+    ('A', 0, 0, 2, 1, 'P'),
+    ('A', 0, 1, 2, 1, 'P'),
+    ('T', 1, 1, 'P'),
     ('I', 2, 1, 'S'),
-    ('A', 2, 0, 1, 'P'),
-    ('W', 0, 0, 'V'),
-    ('A', 2, 1, 0, 'P'),
-    ('I', 5, 0, 'V'),
-    ('A', 2, 1, 1, 'P'),
-    ('A', 2, 2, 0, 'P'),
-    ('W', 0, 2, 'S'),
-    ('A', 2, 2, 1, 'P'),
-    ('W', 0, 1, 'V'),
-    ('A', 3, 0, 0, 'P'),
-    ('W', 1, 2, 'V'),
-    ('W', 1, 3, 'S'),
-    ('A', 3, 0, 1, 'P'),
+    ('I', 2, 0, 'V'),
+    ('T', 1, 2, 'P'),
+    ('q', 0, 1, 'V'),
+    ('q', 2, 0, 'V'),
+    ('Q', 1, 0, 0, 'V'),
+    ('I', 3, 0, 'S'),
+    ('A', 0, 0, 0, 2, 'P'),
     ('q', 2, 1, 'V'),
-    ('A', 3, 1, 0, 'P'),
-    ('q', 4, 0, 'V'),
-    ('A', 3, 1, 1, 'P'),
-    ('I', 5, 1, 'S'),
-    ('W', 2, 0, 'V'),
-    ('A', 3, 2, 0, 'P'),
-    ('q', 5, 0, 'V'),
-    ('A', 3, 2, 1, 'P'),
-    ('q', 4, 1, 'V'),
-    ('A', 4, 0, 0, 'P'),
-    ('W', 1, 1, 'V'),
-    ('A', 4, 0, 1, 'P'),
-    ('W', 4, 3, 'S'),
-    ('W', 0, 3, 'V'),
-    ('A', 4, 1, 0, 'P'),
-    ('W', 2, 2, 'V'),
-    ('A', 4, 1, 1, 'P'),
-    ('I2', 0, 'S'),
-    ('W', 1, 0, 'V'),
-    ('A', 4, 2, 0, 'P'),
-    ('W', 2, 1, 'V'),
-    ('A', 4, 2, 1, 'P'),
-    ('q', 5, 1, 'V'),
-    ('A', 5, 0, 0, 'P'),
+    ('A', 0, 1, 0, 2, 'P'),
+    ('Q', 1, 0, 1, 'V'),
+    ('A', 0, 0, 1, 2, 'P'),
     ('q', 1, 1, 'V'),
-    ('A', 5, 0, 1, 'P'),
+    ('A', 0, 1, 1, 2, 'P'),
+    ('A', 0, 0, 2, 2, 'P'),
+    ('Q', 1, 1, 1, 'V'),
+    ('A', 0, 1, 2, 2, 'P'),
+    ('I', 4, 1, 'V'),
+    ('E', 1, 1, 'S'),
+    ('q', 3, 0, 'V'),
+    ('E', 1, 2, 'S'),
+    ('Q', 1, 3, 0, 'V'),
+    ('A', 0, 0, 0, 3, 'P'),
+    ('Q', 1, 2, 0, 'V'),
+    ('A', 0, 1, 0, 3, 'P'),
+    ('Q', 1, 2, 1, 'V'),
+    ('I', 4, 0, 'S'),
+    ('A', 0, 0, 1, 3, 'P'),
+    ('Q', 1, 1, 0, 'V'),
+    ('A', 0, 1, 1, 3, 'P'),
+    ('Q', 1, 4, 0, 'V'),
+    ('A', 0, 0, 2, 3, 'P'),
+    ('Q', 1, 5, 0, 'V'),
+    ('A', 0, 1, 2, 3, 'P'),
+    ('I', 5, 0, 'V'),
+    ('A', 1, 0, 0, 0, 'P'),
+    ('A', 1, 0, 1, 0, 'P'),
+    ('A', 1, 0, 0, 1, 'P'),
+    ('A', 1, 0, 1, 1, 'P'),
+    ('A', 1, 0, 0, 2, 'P'),
+    ('W', 1, 1, 0, 'V'),
+    ('I', 5, 1, 'S'),
+    ('A', 1, 0, 1, 2, 'P'),
+    ('q', 4, 0, 'V'),
+    ('A', 1, 0, 0, 3, 'P'),
+    ('A', 1, 0, 1, 3, 'P'),
+    ('q', 4, 1, 'V'),
+    ('A', 0, 0, 0, 4, 'P'),
+    ('A', 0, 1, 0, 4, 'P'),
+    ('W', 3, 3, 0, 'V'),
+    ('A', 0, 0, 1, 4, 'P'),
+    ('W', 0, 3, 0, 'V'),
+    ('A', 0, 1, 1, 4, 'P'),
+    ('q', 5, 0, 'V'),
+    ('A', 0, 0, 2, 4, 'P'),
+    ('A', 0, 1, 2, 4, 'P'),
+    ('W', 3, 2, 0, 'S'),
+    ('W', 0, 1, 0, 'V'),
+    ('A', 1, 0, 0, 4, 'P'),
+    ('W', 4, 2, 0, 'V'),
+    ('A', 1, 0, 1, 4, 'P'),
+    ('W', 0, 0, 0, 'S'),
+    ('W', 4, 1, 0, 'V'),
+    ('A', 0, 0, 0, 5, 'P'),
+    ('I', 3, 1, 'V'),
+    ('A', 0, 1, 0, 5, 'P'),
+    ('Y', 0, 0, 0, 'S'),
+    ('A', 0, 0, 1, 5, 'P'),
+    ('A', 0, 1, 1, 5, 'P'),
+    ('A', 0, 0, 2, 5, 'P'),
+    ('Y', 0, 1, 0, 'S'),
+    ('A', 0, 1, 2, 5, 'P'),
+    ('q', 5, 1, 'V'),
+    ('A', 1, 0, 0, 5, 'P'),
+    ('W', 1, 2, 0, 'S'),
+    ('A', 1, 0, 1, 5, 'P'),
     ('q', 3, 1, 'V'),
-    ('A', 5, 1, 0, 'P'),
-    ('A', 5, 1, 1, 'P'),
-    ('W', 3, 1, 'V'),
-    ('A', 5, 2, 0, 'P'),
-    ('W', 3, 0, 'V'),
-    ('A', 5, 2, 1, 'P'),
-    ('W', 5, 1, 'V'),
-    ('B2', 0, 0, 0, 0, 'P'),
-    ('Y', 'A', 0, 1, 'V'),
-    ('B2', 0, 0, 0, 1, 'P'),
-    ('B2', 0, 0, 0, 2, 'P'),
-    ('Y', 'A', 2, 1, 'S'),
-    ('B2', 0, 0, 0, 3, 'P'),
-    ('B2', 0, 0, 0, 4, 'P'),
-    ('B2', 0, 0, 0, 5, 'P'),
-    ('B2', 0, 0, 1, 0, 'P'),
-    ('B2', 0, 0, 1, 1, 'P'),
-    ('I2', 1, 'V'),
-    ('B2', 0, 0, 1, 2, 'P'),
-    ('B2', 0, 0, 1, 3, 'P'),
-    ('B2', 0, 0, 1, 4, 'P'),
-    ('Y', 'A', 0, 0, 'S'),
-    ('B2', 0, 0, 1, 5, 'P'),
-    ('B2', 0, 0, 2, 0, 'P'),
-    ('B2', 0, 0, 2, 1, 'P'),
-    ('B2', 0, 0, 2, 2, 'P'),
-    ('B2', 0, 0, 2, 3, 'P'),
-    ('B2', 0, 0, 2, 4, 'P'),
-    ('B2', 0, 0, 2, 5, 'P'),
-    ('Y', 'A', 1, 0, 'S'),
-    ('B2', 0, 1, 0, 0, 'P'),
-    ('B2', 0, 1, 0, 1, 'P'),
-    ('B2', 0, 1, 0, 2, 'P'),
-    ('B2', 0, 1, 0, 3, 'P'),
-    ('B2', 0, 1, 0, 4, 'P'),
-    ('B2', 0, 1, 0, 5, 'P'),
-    ('B2', 0, 1, 1, 0, 'P'),
-    ('q2', 0, 'V'),
-    ('Y', 'A', 2, 0, 'S'),
-    ('B2', 0, 1, 1, 1, 'P'),
-    ('B2', 0, 1, 1, 2, 'P'),
-    ('B2', 0, 1, 1, 3, 'P'),
-    ('B2', 0, 1, 1, 4, 'P'),
-    ('B2', 0, 1, 1, 5, 'P'),
-    ('B2', 0, 1, 2, 0, 'P'),
-    ('B2', 0, 1, 2, 1, 'P'),
-    ('W', 2, 3, 'S'),
-    ('B2', 0, 1, 2, 2, 'P'),
-    ('q2', 1, 'V'),
-    ('B2', 0, 1, 2, 3, 'P'),
-    ('B2', 0, 1, 2, 4, 'P'),
-    ('B2', 0, 1, 2, 5, 'P'),
-    ('C', 0, 0, 0, 0, 'P'),
-    ('C', 0, 0, 0, 1, 'P'),
-    ('C', 0, 0, 0, 2, 'P'),
-    ('C', 0, 0, 0, 3, 'P'),
-    ('Y', 'A', 1, 1, 'S'),
-    ('M0', 0, 'V'),
-    ('C', 0, 0, 0, 4, 'P'),
-    ('C', 0, 0, 0, 5, 'P'),
-    ('C', 0, 0, 1, 0, 'P'),
-    ('C', 0, 0, 1, 1, 'P'),
-    ('C', 0, 0, 1, 2, 'P'),
-    ('C', 0, 0, 1, 3, 'P'),
-    ('C', 0, 0, 1, 4, 'P'),
-    ('Y', 'B2', 0, 1, 'S'),
-    ('C', 0, 0, 1, 5, 'P'),
-    ('C', 0, 0, 2, 0, 'P'),
-    ('C', 0, 0, 2, 1, 'P'),
-    ('C', 0, 0, 2, 2, 'P'),
-    ('M0', 1, 'V'),
-    ('C', 0, 0, 2, 3, 'P'),
-    ('Y', 'B2', 0, 0, 'S'),
-    ('C', 0, 0, 2, 4, 'P'),
-    ('C', 0, 0, 2, 5, 'P'),
-    ('C', 0, 1, 0, 0, 'P'),
-    ('C', 0, 1, 0, 1, 'P'),
-    ('C', 0, 1, 0, 2, 'P'),
-    ('C', 0, 1, 0, 3, 'P'),
-    ('Y', 'C', 0, 0, 'S'),
-    ('C', 0, 1, 0, 4, 'P'),
-    ('C', 0, 1, 0, 5, 'P'),
-    ('C', 0, 1, 1, 0, 'P'),
-    ('M0', 'B2', 0, 'V'),
-    ('C', 0, 1, 1, 1, 'P'),
-    ('C', 0, 1, 1, 2, 'P'),
-    ('I2', 2, 'S'),
-    ('C', 0, 1, 1, 3, 'P'),
-    ('C', 0, 1, 1, 4, 'P'),
-    ('C', 0, 1, 1, 5, 'P'),
-    ('C', 0, 1, 2, 0, 'P'),
-    ('M1', 'A', 'V'),
-    ('C', 0, 1, 2, 1, 'P'),
-    ('C', 0, 1, 2, 2, 'P'),
-    ('C', 0, 1, 2, 3, 'P'),
-    ('C', 0, 1, 2, 4, 'P'),
-    ('C', 0, 1, 2, 5, 'P'),
-    ('B2', 1, 0, 0, 0, 'P'),
-    ('B2', 1, 0, 0, 1, 'P'),
-    ('Y', 'C', 0, 1, 'V'),
-    ('B2', 1, 0, 0, 2, 'P'),
-    ('B2', 1, 0, 0, 3, 'P'),
-    ('B2', 1, 0, 0, 4, 'P'),
-    ('B2', 1, 0, 0, 5, 'P'),
-    ('B2', 1, 0, 1, 0, 'P'),
-    ('B2', 1, 0, 1, 1, 'P'),
-    ('W', 4, 0, 'V'),
-    ('B2', 1, 0, 1, 2, 'P'),
-    ('B2', 1, 0, 1, 3, 'P'),
-    ('B2', 1, 0, 1, 4, 'P'),
-    ('M0', 'C', 0, 'V'),
-    ('B2', 1, 0, 1, 5, 'P'),
-    ('B2', 1, 0, 2, 0, 'P'),
-    ('B2', 1, 0, 2, 1, 'P'),
-    ('B2', 1, 0, 2, 2, 'P'),
-    ('B2', 1, 0, 2, 3, 'P'),
-    ('B2', 1, 0, 2, 4, 'P'),
-    ('M2', 'A', 'V'),
-    ('B2', 1, 0, 2, 5, 'P'),
-    ('B2', 1, 1, 0, 0, 'P'),
-    ('B2', 1, 1, 0, 1, 'P'),
-    ('B2', 1, 1, 0, 2, 'P'),
-    ('B2', 1, 1, 0, 3, 'P'),
-    ('B2', 1, 1, 0, 4, 'P'),
-    ('B2', 1, 1, 0, 5, 'P'),
-    ('M1', 'C', 0, 'V'),
-    ('W', 4, 1, 'S'),
-    ('B2', 1, 1, 1, 0, 'P'),
-    ('B2', 1, 1, 1, 1, 'P'),
-    ('B2', 1, 1, 1, 2, 'P'),
-    ('B2', 1, 1, 1, 3, 'P'),
-    ('W', 3, 3, 'V'),
-    ('B2', 1, 1, 1, 4, 'P'),
-    ('B2', 1, 1, 1, 5, 'P'),
-    ('B2', 1, 1, 2, 0, 'P'),
-    ('M2', 'C', 0, 'V'),
-    ('g', 'A', 'S'),
-    ('B2', 1, 1, 2, 1, 'P'),
-    ('B2', 1, 1, 2, 2, 'P'),
-    ('B2', 1, 1, 2, 3, 'P'),
-    ('B2', 1, 1, 2, 4, 'P'),
-    ('q2', 2, 'V'),
-    ('B2', 1, 1, 2, 5, 'P'),
-    ('C', 1, 0, 0, 0, 'P'),
-    ('C', 1, 0, 0, 1, 'P'),
-    ('C', 1, 0, 0, 2, 'P'),
-    ('g', 'C', 0, 'S'),
-    ('C', 1, 0, 0, 3, 'P'),
-    ('C', 1, 0, 0, 4, 'P'),
-    ('C', 1, 0, 0, 5, 'P'),
-    ('Y', 'B2', 1, 1, 'S'),
-    ('n', 'A', 1, 'V'),
-    ('C', 1, 0, 1, 0, 'P'),
-    ('C', 1, 0, 1, 1, 'P'),
-    ('n', 'C', 0, 'V'),
-    ('C', 1, 0, 1, 2, 'P'),
-    ('C', 1, 0, 1, 3, 'P'),
-    ('n', 'A', 0, 'V'),
-    ('C', 1, 0, 1, 4, 'P'),
-    ('n', 'B2', 0, 'V'),
-    ('C', 1, 0, 1, 5, 'P'),
-    ('Y', 'B2', 1, 0, 'S'),
-    ('C', 1, 0, 2, 0, 'P'),
-    ('W', 3, 2, 'V'),
-    ('C', 1, 0, 2, 1, 'P'),
-    ('C', 1, 0, 2, 2, 'P'),
-    ('C', 1, 0, 2, 3, 'P'),
-    ('e', 0, 0, 'V'),
-    ('C', 1, 0, 2, 4, 'P'),
-    ('W', 4, 2, 'S'),
-    ('C', 1, 0, 2, 5, 'P'),
-    ('C', 1, 1, 0, 0, 'P'),
-    ('C', 1, 1, 0, 1, 'P'),
-    ('C', 1, 1, 0, 2, 'P'),
-    ('C', 1, 1, 0, 3, 'P'),
-    ('C', 1, 1, 0, 4, 'P'),
-    ('C', 1, 1, 0, 5, 'P'),
-    ('C', 1, 1, 1, 0, 'P'),
-    ('I2', 3, 'S'),
+    ('A', 0, 2, 0, 0, 'P'),
+    ('W', 0, 2, 0, 'S'),
+    ('A', 0, 2, 0, 1, 'P'),
+    ('W', 0, 0, 1, 'V'),
+    ('A', 0, 2, 0, 2, 'P'),
+    ('Y', 0, 1, 2, 'S'),
+    ('W', 4, 3, 0, 'V'),
+    ('A', 0, 2, 0, 3, 'P'),
+    ('A', 0, 2, 0, 4, 'P'),
+    ('W', 0, 3, 1, 'V'),
+    ('Y', 0, 1, 1, 'S'),
+    ('A', 0, 2, 0, 5, 'P'),
+    ('W', 1, 0, 0, 'V'),
+    ('A', 0, 2, 1, 0, 'P'),
+    ('I2', 0, 0, 'V'),
+    ('Y', 0, 0, 1, 'S'),
+    ('A', 0, 2, 1, 1, 'P'),
+    ('A', 0, 2, 1, 2, 'P'),
+    ('W', 4, 0, 0, 'S'),
+    ('A', 0, 2, 1, 3, 'P'),
+    ('A', 0, 2, 1, 4, 'P'),
+    ('Y', 0, 0, 2, 'S'),
+    ('W', 1, 3, 0, 'V'),
+    ('A', 0, 2, 1, 5, 'P'),
+    ('A', 0, 2, 2, 0, 'P'),
+    ('W', 3, 1, 0, 'V'),
+    ('W', 5, 0, 0, 'S'),
+    ('A', 0, 2, 2, 1, 'P'),
+    ('M0', 0, 0, 'V'),
+    ('A', 0, 2, 2, 2, 'P'),
+    ('Y', 0, 2, 1, 'S'),
+    ('A', 0, 2, 2, 3, 'P'),
+    ('A', 0, 2, 2, 4, 'P'),
+    ('A', 0, 2, 2, 5, 'P'),
+    ('W', 2, 1, 0, 'S'),
+    ('A', 0, 3, 0, 0, 'P'),
+    ('A', 0, 3, 0, 1, 'P'),
+    ('Y', 0, 2, 0, 'S'),
+    ('I2', 1, 0, 'V'),
+    ('A', 0, 3, 0, 2, 'P'),
+    ('A', 0, 3, 0, 3, 'P'),
+    ('Y', 0, 2, 2, 'S'),
+    ('A', 0, 3, 0, 4, 'P'),
+    ('A', 0, 3, 0, 5, 'P'),
+    ('Y', 1, 0, 1, 'S'),
+    ('A', 0, 3, 1, 0, 'P'),
+    ('I2', 4, 0, 'V'),
+    ('A', 0, 3, 1, 1, 'P'),
+    ('W', 5, 3, 0, 'S'),
+    ('A', 0, 3, 1, 2, 'P'),
+    ('A', 0, 3, 1, 3, 'P'),
+    ('Y', 1, 0, 0, 'S'),
+    ('A', 0, 3, 1, 4, 'P'),
+    ('A', 0, 3, 1, 5, 'P'),
+    ('M1', 0, 0, 'V'),
+    ('W', 5, 1, 0, 'S'),
+    ('A', 0, 3, 2, 0, 'P'),
+    ('A', 0, 3, 2, 1, 'P'),
+    ('W', 2, 0, 0, 'V'),
+    ('Y', 0, 3, 1, 'S'),
+    ('A', 0, 3, 2, 2, 'P'),
+    ('q2', 4, 0, 'V'),
+    ('A', 0, 3, 2, 3, 'P'),
+    ('Y', 0, 3, 0, 'S'),
+    ('A', 0, 3, 2, 4, 'P'),
+    ('M2', 0, 0, 'V'),
+    ('A', 0, 3, 2, 5, 'P'),
+    ('A', 1, 0, 2, 0, 'P'),
+    ('W', 5, 2, 0, 'V'),
+    ('Y', 0, 3, 2, 'S'),
+    ('A', 1, 0, 2, 1, 'P'),
+    ('q2', 0, 0, 'V'),
+    ('A', 1, 0, 2, 2, 'P'),
+    ('A', 1, 0, 2, 3, 'P'),
+    ('W', 2, 3, 0, 'S'),
+    ('M0', 0, 1, 'V'),
+    ('A', 1, 0, 2, 4, 'P'),
+    ('A', 1, 0, 2, 5, 'P'),
+    ('g', 0, 0, 'S'),
+    ('A', 1, 1, 0, 0, 'P'),
+    ('A', 1, 1, 0, 1, 'P'),
+    ('I2', 5, 0, 'S'),
+    ('A', 1, 1, 0, 2, 'P'),
+    ('A', 1, 1, 0, 3, 'P'),
+    ('q2', 1, 0, 'V'),
+    ('A', 1, 1, 0, 4, 'P'),
+    ('A', 1, 1, 0, 5, 'P'),
+    ('M1', 0, 1, 'V'),
+    ('A', 1, 1, 1, 0, 'P'),
+    ('A', 1, 1, 1, 1, 'P'),
+    ('W', 3, 0, 0, 'V'),
+    ('A', 1, 1, 1, 2, 'P'),
+    ('A', 1, 1, 1, 3, 'P'),
+    ('n', 0, 1, 'V'),
+    ('M2', 0, 1, 'V'),
+    ('A', 1, 1, 1, 4, 'P'),
+    ('Y', 1, 0, 2, 'S'),
+    ('A', 1, 1, 1, 5, 'P'),
+    ('n', 0, 0, 'V'),
+    ('A', 1, 1, 2, 0, 'P'),
+    ('q2', 5, 0, 'V'),
+    ('g', 0, 1, 'S'),
+    ('A', 1, 1, 2, 1, 'P'),
+    ('A', 1, 1, 2, 2, 'P'),
+    ('W', 2, 2, 0, 'V'),
+    ('W', 0, 2, 1, 'S'),
+    ('A', 1, 1, 2, 3, 'P'),
+    ('n', 0, 3, 'V'),
+    ('A', 1, 1, 2, 4, 'P'),
+    ('n', 0, 2, 'V'),
+    ('I2', 3, 0, 'S'),
+    ('W', 2, 2, 1, 'V'),
+    ('A', 1, 1, 2, 5, 'P'),
+    ('A', 1, 2, 0, 0, 'P'),
     ('e', 0, 1, 'V'),
-    ('C', 1, 1, 1, 1, 'P'),
-    ('C', 1, 1, 1, 2, 'P'),
-    ('C', 1, 1, 1, 3, 'P'),
-    ('C', 1, 1, 1, 4, 'P'),
-    ('C', 1, 1, 1, 5, 'P'),
-    ('C', 1, 1, 2, 0, 'P'),
-    ('C', 1, 1, 2, 1, 'P'),
-    ('C', 1, 1, 2, 2, 'P'),
-    ('eq', 0, 0, 'V'),
-    ('C', 1, 1, 2, 3, 'P'),
-    ('C', 1, 1, 2, 4, 'P'),
+    ('A', 1, 2, 0, 1, 'P'),
+    ('A', 1, 2, 0, 2, 'P'),
+    ('A', 1, 2, 0, 3, 'P'),
+    ('A', 1, 2, 0, 4, 'P'),
+    ('A', 1, 2, 0, 5, 'P'),
     ('e', 0, 2, 'V'),
-    ('C', 1, 1, 2, 5, 'P'),
-    ('D', 0, 0, 0, 'P'),
-    ('D', 0, 0, 1, 'P'),
-    ('eq', 0, 1, 'V'),
-    ('D', 0, 0, 2, 'P'),
-    ('e', 0, 3, 'V'),
-    ('D', 0, 1, 0, 'P'),
-    ('D', 0, 1, 1, 'P'),
-    ('eq', 0, 2, 'V'),
-    ('D', 0, 1, 2, 'P'),
-    ('eq', 0, 3, 'V'),
-    ('Y', 'C', 1, 0, 'S'),
-    ('D', 0, 2, 0, 'P'),
+    ('A', 1, 2, 1, 0, 'P'),
+    ('A', 1, 2, 1, 1, 'P'),
+    ('A', 1, 2, 1, 2, 'P'),
+    ('Y', 1, 1, 2, 'S'),
+    ('A', 1, 2, 1, 3, 'P'),
+    ('A', 1, 2, 1, 4, 'P'),
+    ('Y', 1, 1, 0, 'S'),
+    ('q2', 3, 0, 'V'),
+    ('A', 1, 2, 1, 5, 'P'),
+    ('A', 1, 2, 2, 0, 'P'),
+    ('e', 0, 0, 'V'),
+    ('Y', 1, 2, 1, 'S'),
+    ('A', 1, 2, 2, 1, 'P'),
+    ('A', 1, 2, 2, 2, 'P'),
+    ('A', 1, 2, 2, 3, 'P'),
+    ('Y', 1, 2, 0, 'S'),
+    ('A', 1, 2, 2, 4, 'P'),
+    ('A', 1, 2, 2, 5, 'P'),
     ('e', 0, 4, 'V'),
-    ('D', 0, 2, 1, 'P'),
-    ('Y', 'C', 1, 1, 'S'),
-    ('D', 0, 2, 2, 'P'),
-    ('e', 0, 5, 'V'),
-    ('I2', 4, 'S'),
-    ('D', 0, 3, 0, 'P'),
-    ('D', 0, 3, 1, 'P'),
+    ('I2', 2, 0, 'S'),
+    ('A', 1, 3, 0, 0, 'P'),
+    ('A', 1, 3, 0, 1, 'P'),
+    ('A', 1, 3, 0, 2, 'P'),
+    ('A', 1, 3, 0, 3, 'P'),
+    ('e', 0, 3, 'V'),
+    ('A', 1, 3, 0, 4, 'P'),
+    ('A', 1, 3, 0, 5, 'P'),
+    ('A', 1, 3, 1, 0, 'P'),
+    ('A', 1, 3, 1, 1, 'P'),
+    ('A', 1, 3, 1, 2, 'P'),
+    ('Y', 1, 2, 2, 'S'),
+    ('eq', 0, 0, 'V'),
+    ('A', 1, 3, 1, 3, 'P'),
+    ('q2', 2, 0, 'V'),
+    ('A', 1, 3, 1, 4, 'P'),
+    ('Y', 1, 1, 1, 'S'),
+    ('A', 1, 3, 1, 5, 'P'),
+    ('eq', 0, 3, 'V'),
+    ('A', 1, 3, 2, 0, 'P'),
+    ('Y', 1, 3, 1, 'S'),
+    ('eq', 0, 1, 'V'),
+    ('A', 1, 3, 2, 1, 'P'),
+    ('A', 1, 3, 2, 2, 'P'),
+    ('eq', 0, 2, 'V'),
+    ('A', 1, 3, 2, 3, 'P'),
+    ('W', 1, 3, 1, 'S'),
+    ('M0', 1, 0, 'V'),
+    ('A', 1, 3, 2, 4, 'P'),
+    ('A', 1, 3, 2, 5, 'P'),
+    ('Y', 1, 3, 0, 'S'),
+    ('D', 0, 0, 0, 0, 'P'),
+    ('D', 0, 0, 0, 1, 'P'),
+    ('Y', 1, 3, 2, 'S'),
+    ('D', 0, 0, 0, 2, 'P'),
+    ('D', 0, 0, 0, 3, 'P'),
     ('eq', 0, 4, 'V'),
-    ('D', 0, 3, 2, 'P'),
+    ('W', 3, 3, 1, 'S'),
+    ('D', 0, 0, 0, 4, 'P'),
+    ('M0', 1, 1, 'V'),
+    ('D', 0, 0, 0, 5, 'P'),
+    ('W', 5, 3, 1, 'S'),
+    ('D', 0, 0, 1, 0, 'P'),
+    ('D', 0, 0, 1, 1, 'P'),
+    ('W', 2, 1, 1, 'S'),
+    ('D', 0, 0, 1, 2, 'P'),
+    ('D', 0, 0, 1, 3, 'P'),
+    ('W', 1, 1, 1, 'S'),
+    ('D', 0, 0, 1, 4, 'P'),
+    ('M1', 1, 0, 'V'),
+    ('D', 0, 0, 1, 5, 'P'),
+    ('W', 2, 0, 1, 'S'),
+    ('D', 0, 0, 2, 0, 'P'),
+    ('M1', 1, 1, 'V'),
+    ('D', 0, 0, 2, 1, 'P'),
+    ('W', 0, 1, 1, 'S'),
+    ('D', 0, 0, 2, 2, 'P'),
+    ('M2', 1, 0, 'V'),
+    ('D', 0, 0, 2, 3, 'P'),
+    ('W', 3, 1, 1, 'S'),
+    ('D', 0, 0, 2, 4, 'P'),
+    ('M2', 1, 1, 'V'),
+    ('D', 0, 0, 2, 5, 'P'),
+    ('D', 0, 0, 3, 0, 'P'),
+    ('g', 1, 0, 'S'),
+    ('e', 0, 5, 'V'),
+    ('D', 0, 0, 3, 1, 'P'),
+    ('D', 0, 0, 3, 2, 'P'),
+    ('g', 1, 1, 'S'),
+    ('D', 0, 0, 3, 3, 'P'),
+    ('D', 0, 0, 3, 4, 'P'),
+    ('W', 4, 2, 1, 'S'),
+    ('D', 0, 0, 3, 5, 'P'),
+    ('n', 1, 0, 'V'),
+    ('n', 1, 3, 'V'),
+    ('D', 0, 0, 4, 0, 'P'),
+    ('n', 1, 1, 'V'),
+    ('W', 4, 1, 1, 'S'),
+    ('n', 1, 2, 'V'),
+    ('D', 0, 0, 4, 1, 'P'),
     ('eq', 0, 5, 'V'),
-    ('M0', 'B2', 1, 'V'),
-    ('D', 0, 4, 0, 'P'),
-    ('D', 0, 4, 1, 'P'),
-    ('M0', 'C', 1, 'V'),
-    ('D', 0, 4, 2, 'P'),
-    ('q2', 3, 'V'),
-    ('D', 0, 5, 0, 'P'),
-    ('D', 0, 5, 1, 'P'),
-    ('D', 0, 5, 2, 'P'),
-    ('W', 5, 0, 'V'),
-    ('W', 5, 3, 'S'),
-    ('D', 0, 0, 3, 'P'),
-    ('M1', 'C', 1, 'V'),
-    ('D', 0, 1, 3, 'P'),
-    ('q2', 4, 'V'),
-    ('W', 5, 2, 'S'),
-    ('D', 0, 2, 3, 'P'),
-    ('D', 0, 3, 3, 'P'),
-    ('M2', 'C', 1, 'V'),
-    ('D', 0, 4, 3, 'P'),
-    ('I2', 5, 'V'),
-    ('g', 'C', 1, 'S'),
-    ('D', 0, 5, 3, 'P'),
-    ('D', 0, 0, 4, 'P'),
-    ('D', 0, 1, 4, 'P'),
-    ('D', 0, 2, 4, 'P'),
-    ('D', 0, 3, 4, 'P'),
-    ('n', 'B2', 1, 'V'),
-    ('q2', 5, 'V'),
-    ('D', 0, 4, 4, 'P'),
-    ('D', 0, 5, 4, 'P'),
-    ('n', 'C', 1, 'V'),
-    ('D', 0, 0, 5, 'P'),
+    ('D', 0, 0, 4, 2, 'P'),
+    ('W', 5, 1, 1, 'S'),
+    ('D', 0, 0, 4, 3, 'P'),
     ('e', 1, 0, 'V'),
-    ('D', 0, 1, 5, 'P'),
-    ('O', 0, 5, 'S'),
-    ('D', 0, 2, 5, 'P'),
+    ('D', 0, 0, 4, 4, 'P'),
+    ('W', 1, 0, 1, 'S'),
+    ('D', 0, 0, 4, 5, 'P'),
+    ('D', 0, 0, 5, 0, 'P'),
+    ('D', 0, 0, 5, 1, 'P'),
+    ('O', 0, 0, 4, 'S'),
+    ('D', 0, 0, 5, 2, 'P'),
     ('e', 1, 1, 'V'),
-    ('D', 0, 3, 5, 'P'),
-    ('O', 0, 1, 'S'),
-    ('D', 0, 4, 5, 'P'),
-    ('D', 0, 5, 5, 'P'),
+    ('D', 0, 0, 5, 3, 'P'),
+    ('D', 0, 0, 5, 4, 'P'),
+    ('O', 0, 0, 5, 'S'),
+    ('D', 0, 0, 5, 5, 'P'),
+    ('O', 0, 0, 1, 'S'),
     ('eq', 1, 0, 'V'),
-    ('O', 0, 0, 'S'),
-    ('eq', 1, 1, 'V'),
-    ('D', 1, 0, 0, 'P'),
     ('e', 1, 2, 'V'),
-    ('D', 1, 0, 1, 'P'),
-    ('O', 0, 2, 'S'),
-    ('D', 1, 0, 2, 'P'),
-    ('eq', 1, 2, 'V'),
-    ('D', 1, 1, 3, 'P'),
-    ('O', 0, 3, 'S'),
+    ('O', 0, 0, 3, 'S'),
+    ('D', 1, 0, 0, 0, 'P'),
+    ('D', 1, 0, 0, 1, 'P'),
+    ('W', 3, 2, 1, 'S'),
+    ('D', 1, 0, 0, 2, 'P'),
+    ('D', 1, 0, 0, 3, 'P'),
+    ('O', 0, 0, 0, 'S'),
+    ('eq', 1, 1, 'V'),
+    ('D', 1, 0, 0, 4, 'P'),
     ('e', 1, 3, 'V'),
-    ('D', 1, 1, 5, 'P'),
-    ('D', 1, 1, 4, 'P'),
-    ('O', 0, 4, 'S'),
-    ('D', 1, 2, 2, 'P'),
-    ('eq', 1, 3, 'V'),
+    ('D', 1, 0, 0, 5, 'P'),
+    ('O', 0, 0, 2, 'S'),
+    ('D', 1, 0, 1, 0, 'P'),
+    ('D', 1, 0, 1, 1, 'P'),
+    ('W', 2, 3, 1, 'S'),
+    ('D', 1, 0, 1, 2, 'P'),
+    ('D', 1, 0, 1, 3, 'P'),
+    ('eq', 1, 2, 'V'),
+    ('W', 4, 3, 1, 'S'),
+    ('D', 1, 0, 1, 4, 'P'),
     ('e', 1, 4, 'V'),
-    ('D', 1, 2, 0, 'P'),
-    ('D', 1, 2, 1, 'P'),
-    ('D', 1, 3, 5, 'P'),
-    ('eq', 1, 4, 'V'),
-    ('D', 1, 3, 4, 'P'),
+    ('D', 1, 0, 1, 5, 'P'),
+    ('D', 1, 0, 2, 0, 'P'),
+    ('W', 5, 2, 1, 'S'),
+    ('D', 1, 0, 2, 1, 'P'),
+    ('D', 1, 0, 2, 2, 'P'),
+    ('I2', 0, 1, 'S'),
+    ('D', 1, 0, 2, 3, 'P'),
+    ('eq', 1, 3, 'V'),
+    ('D', 1, 0, 2, 4, 'P'),
     ('e', 1, 5, 'V'),
-    ('D', 1, 3, 3, 'P'),
-    ('D', 1, 4, 1, 'P'),
-    ('D', 1, 4, 2, 'P'),
+    ('D', 1, 0, 2, 5, 'P'),
+    ('D', 1, 0, 3, 0, 'P'),
+    ('D', 1, 0, 3, 1, 'P'),
+    ('D', 1, 0, 3, 2, 'P'),
+    ('D', 1, 0, 3, 3, 'P'),
+    ('eq', 1, 4, 'V'),
+    ('D', 1, 0, 3, 4, 'P'),
+    ('W', 1, 2, 1, 'V'),
+    ('D', 1, 0, 3, 5, 'P'),
+    ('W', 3, 0, 1, 'V'),
+    ('D', 1, 0, 4, 0, 'P'),
+    ('I2', 1, 1, 'S'),
+    ('q2', 0, 1, 'V'),
+    ('D', 1, 0, 4, 1, 'P'),
+    ('D', 1, 0, 4, 2, 'P'),
     ('eq', 1, 5, 'V'),
-    ('D', 1, 4, 0, 'P'),
-    ('D', 1, 5, 4, 'P'),
-    ('D', 1, 5, 3, 'P'),
-    ('O', 1, 0, 'S'),
-    ('D', 1, 5, 5, 'P'),
-    ('O', 1, 1, 'V'),
-    ('D', 1, 0, 3, 'P'),
-    ('O', 1, 2, 'S'),
-    ('D', 1, 1, 0, 'P'),
-    ('D', 1, 2, 5, 'P'),
-    ('D', 1, 3, 2, 'P'),
-    ('D', 1, 4, 4, 'P'),
-    ('D', 1, 5, 1, 'P'),
-    ('D', 1, 0, 4, 'P'),
-    ('O', 1, 3, 'V'),
-    ('D', 1, 1, 2, 'P'),
-    ('D', 1, 2, 3, 'P'),
-    ('D', 1, 3, 1, 'P'),
-    ('D', 1, 4, 5, 'P'),
-    ('D', 1, 5, 0, 'P'),
-    ('D', 1, 0, 5, 'P'),
-    ('O', 1, 4, 'S'),
-    ('D', 1, 1, 1, 'P'),
-    ('D', 1, 2, 4, 'P'),
-    ('D', 1, 3, 0, 'P'),
-    ('D', 1, 4, 3, 'P'),
-    ('D', 1, 5, 2, 'P'),
-    ('O', 1, 5, 'V'),
+    ('D', 1, 0, 4, 3, 'P'),
+    ('I2', 2, 1, 'V'),
+    ('D', 1, 0, 4, 4, 'P'),
+    ('D', 1, 0, 4, 5, 'P'),
+    ('D', 1, 0, 5, 0, 'P'),
+    ('D', 1, 0, 5, 1, 'P'),
+    ('D', 1, 0, 5, 2, 'P'),
+    ('O', 1, 0, 4, 'V'),
+    ('D', 1, 0, 5, 3, 'P'),
+    ('O', 1, 0, 3, 'S'),
+    ('D', 1, 0, 5, 4, 'P'),
+    ('W', 5, 0, 1, 'V'),
+    ('D', 1, 0, 5, 5, 'P'),
+    ('O', 1, 0, 5, 'S'),
+    ('O', 1, 0, 1, 'V'),
+    ('D', 0, 1, 0, 0, 'P'),
+    ('D', 0, 1, 1, 0, 'P'),
+    ('O', 1, 0, 2, 'S'),
+    ('q2', 1, 1, 'V'),
+    ('D', 0, 1, 2, 0, 'P'),
+    ('D', 0, 1, 3, 0, 'P'),
+    ('O', 1, 0, 0, 'S'),
+    ('D', 0, 1, 4, 0, 'P'),
+    ('I2', 3, 1, 'V'),
+    ('D', 0, 1, 5, 0, 'P'),
+    ('D', 0, 1, 0, 1, 'P'),
+    ('W', 4, 0, 1, 'S'),
+    ('D', 0, 1, 1, 1, 'P'),
+    ('D', 0, 1, 2, 1, 'P'),
+    ('q2', 2, 1, 'V'),
+    ('D', 0, 1, 3, 1, 'P'),
+    ('I2', 4, 1, 'S'),
+    ('D', 0, 1, 4, 1, 'P'),
+    ('q2', 3, 1, 'V'),
+    ('D', 0, 1, 5, 1, 'P'),
+    ('D', 0, 1, 0, 2, 'P'),
+    ('D', 0, 1, 1, 2, 'P'),
+    ('I2', 5, 1, 'V'),
+    ('D', 0, 1, 2, 2, 'P'),
+    ('D', 0, 1, 3, 2, 'P'),
+    ('D', 0, 1, 4, 2, 'P'),
+    ('D', 0, 1, 5, 2, 'P'),
+    ('D', 0, 1, 0, 3, 'P'),
+    ('D', 0, 1, 1, 3, 'P'),
+    ('q2', 4, 1, 'V'),
+    ('D', 0, 1, 2, 3, 'P'),
+    ('D', 0, 1, 3, 3, 'P'),
+    ('q2', 5, 1, 'V'),
+    ('D', 0, 1, 4, 3, 'P'),
+    ('D', 0, 1, 5, 3, 'P'),
+    ('D', 0, 1, 0, 4, 'P'),
+    ('D', 0, 1, 1, 4, 'P'),
+    ('D', 0, 1, 2, 4, 'P'),
+    ('D', 0, 1, 3, 4, 'P'),
+    ('D', 0, 1, 4, 4, 'P'),
+    ('D', 0, 1, 5, 4, 'P'),
+    ('D', 0, 1, 0, 5, 'P'),
+    ('D', 0, 1, 1, 5, 'P'),
+    ('D', 0, 1, 2, 5, 'P'),
+    ('D', 0, 1, 3, 5, 'P'),
+    ('O', 0, 1, 3, 'V'),
+    ('D', 0, 1, 4, 5, 'P'),
+    ('O', 0, 1, 0, 'S'),
+    ('D', 0, 1, 5, 5, 'P'),
+    ('O', 0, 1, 4, 'V'),
+    ('D', 1, 1, 0, 0, 'P'),
+    ('D', 1, 1, 1, 3, 'P'),
+    ('O', 0, 1, 2, 'V'),
+    ('D', 1, 1, 2, 2, 'P'),
+    ('D', 1, 1, 3, 5, 'P'),
+    ('D', 1, 1, 4, 1, 'P'),
+    ('O', 0, 1, 5, 'V'),
+    ('D', 1, 1, 5, 4, 'P'),
+    ('D', 1, 1, 0, 1, 'P'),
+    ('O', 0, 1, 1, 'V'),
+    ('O', 1, 1, 0, 'S'),
+    ('D', 1, 1, 1, 5, 'P'),
+    ('D', 1, 1, 2, 0, 'P'),
+    ('D', 1, 1, 3, 4, 'P'),
+    ('D', 1, 1, 4, 2, 'P'),
+    ('D', 1, 1, 5, 3, 'P'),
+    ('D', 1, 1, 0, 2, 'P'),
+    ('O', 1, 1, 1, 'V'),
+    ('D', 1, 1, 1, 4, 'P'),
+    ('D', 1, 1, 2, 1, 'P'),
+    ('D', 1, 1, 3, 3, 'P'),
+    ('D', 1, 1, 4, 0, 'P'),
+    ('D', 1, 1, 5, 5, 'P'),
+    ('D', 1, 1, 0, 3, 'P'),
+    ('O', 1, 1, 2, 'V'),
+    ('D', 1, 1, 1, 0, 'P'),
+    ('D', 1, 1, 2, 5, 'P'),
+    ('D', 1, 1, 3, 2, 'P'),
+    ('D', 1, 1, 4, 4, 'P'),
+    ('D', 1, 1, 5, 1, 'P'),
+    ('D', 1, 1, 0, 4, 'P'),
+    ('O', 1, 1, 3, 'V'),
+    ('D', 1, 1, 1, 2, 'P'),
+    ('D', 1, 1, 2, 3, 'P'),
+    ('D', 1, 1, 3, 1, 'P'),
+    ('D', 1, 1, 4, 5, 'P'),
+    ('D', 1, 1, 5, 0, 'P'),
+    ('D', 1, 1, 0, 5, 'P'),
+    ('O', 1, 1, 4, 'V'),
+    ('D', 1, 1, 1, 1, 'P'),
+    ('D', 1, 1, 2, 4, 'P'),
+    ('D', 1, 1, 3, 0, 'P'),
+    ('D', 1, 1, 4, 3, 'P'),
+    ('D', 1, 1, 5, 2, 'P'),
+    ('O', 1, 1, 5, 'V'),
 )
 
 P = 128
-XH = 2
 F32 = mybir.dt.float32
 BF16 = mybir.dt.bfloat16
 U32 = mybir.dt.uint32
@@ -441,11 +605,11 @@ def tile_dihedralthreegroupblock_kernel(tc, x, w1, b1, ls, w2_bytes, w2_scale, o
     with ExitStack() as ctx:
         keep = ctx.enter_context(tc.tile_pool(name="keep", bufs=1))
         work = ctx.enter_context(tc.tile_pool(name="work", bufs=3))
-        psum = ctx.enter_context(tc.psum_pool(name="psum", bufs=8))
+        psum = ctx.enter_context(tc.psum_pool(name="psum", bufs=1))
         ctx.enter_context(tc.manual_schedule())
 
-        def bank(shape):
-            return psum.tile(shape, F32, name="bank")
+        def bank(shape, slot):
+            return psum.tile(shape, F32, name="bank%d" % slot)
 
         b1_sb = keep.tile([P, 4], BF16, name="b1_sb")
         ls_sb = keep.tile([P, 4], BF16, name="ls_sb")
@@ -454,24 +618,25 @@ def tile_dihedralthreegroupblock_kernel(tc, x, w1, b1, ls, w2_bytes, w2_scale, o
         nc.scalar.dma_start(out=b1_sb[:], in_=b1.rearrange("(p t) -> p t", t=4))
         nc.scalar.dma_start(out=ls_sb[:], in_=ls.rearrange("(p t) -> p t", t=4))
 
-        xs = []
-        for i in range(G // XH):
-            t = keep.tile([P, 2, XH, C], BF16, name="xs%d" % i, align_bytes=64)
-            nc.sync.dma_start(
-                out=t[:].rearrange("p a h c -> p a (h c)"),
-                in_=x[:, XH * i : XH * i + XH, :].rearrange("(a p) h c -> p a (h c)", p=P),
-            )
-            xs.append(t)
-        w1_raw = []
-        for j in range(G):
-            t = keep.tile([P, 4, C], BF16, name="w1_raw%d" % j, align_bytes=64)
-            nc.sync.dma_start(out=t[:], in_=w1[j].rearrange("(p t) d -> p t d", t=4))
-            w1_raw.append(t)
-        w2_raw = []
-        for j in range(G):
-            t = keep.tile([P, 4, C], U8, name="w2_raw%d" % j, align_bytes=64)
-            nc.sync.dma_start(out=t[:], in_=w2_bytes[j].rearrange("(p t) d -> p t d", t=4))
-            w2_raw.append(t)
+        xs = {}
+        w1_raw = {}
+        w2_raw = {}
+        for load in LOADS:
+            if load[0] == "x":
+                a, b = load[1:]
+                t = keep.tile([P, 2, C], BF16, name="xs%d_%d" % (a, b), align_bytes=64)
+                nc.sync.dma_start(out=t[:], in_=x[a * P : (a + 1) * P, 2 * b : 2 * b + 2, :])
+                xs[a, b] = t
+            elif load[0] == "w1":
+                j = load[1]
+                t = keep.tile([P, 4, C], BF16, name="w1_raw%d" % j, align_bytes=64)
+                nc.sync.dma_start(out=t[:], in_=w1[j].rearrange("(p t) d -> p t d", t=4))
+                w1_raw[j] = t
+            else:
+                j = load[1]
+                t = keep.tile([P, 4, C], U8, name="w2_raw%d" % j, align_bytes=64)
+                nc.sync.dma_start(out=t[:], in_=w2_bytes[j].rearrange("(p t) d -> p t d", t=4))
+                w2_raw[j] = t
 
         ident = keep.tile([P, P], F32, name="ident")
         make_identity(nc, ident[:])
@@ -479,20 +644,20 @@ def tile_dihedralthreegroupblock_kernel(tc, x, w1, b1, ls, w2_bytes, w2_scale, o
         nc.gpsimd.memset(warm[:], 0.0)
         nc.scalar.activation(out=warm[:], in_=warm[:], func=ACT.Sigmoid)
 
-        xc = [keep.tile([P, 3, N], U32, name="xc%d" % i, align_bytes=64) for i in range(3)]
-        xsc = [keep.tile([P, 3, N], U8, name="xsc%d" % i, align_bytes=64) for i in range(3)]
+        xc = [keep.tile([P, 2, 3, P], U32, name="xc%d" % i, align_bytes=64) for i in range(3)]
+        xsc = [keep.tile([P, 2, 3, P], U8, name="xsc%d" % i, align_bytes=64) for i in range(3)]
         w1c = [keep.tile([P, C], U32, name="w1c%d" % j, align_bytes=64) for j in range(G)]
         w1s = [keep.tile([P, C], U8, name="w1s%d" % j, align_bytes=64) for j in range(G)]
         w2c = [keep.tile([P, C], U32, name="w2c%d" % j, align_bytes=64) for j in range(G)]
         w2s = [keep.tile([P, C], U8, name="w2s%d" % j, align_bytes=64) for j in range(G)]
-        y_sb = keep.tile([P, 4, G, N], F32, name="y_sb", align_bytes=64)
-        m3 = keep.tile([P, 4, 3, N], F32, name="m3", align_bytes=64)
-        m_sb = keep.tile([P, 4, N], F32, name="m_sb", align_bytes=64)
-        s_sb = keep.tile([P, 4, N], F32, name="s_sb", align_bytes=64)
+        y_sb = keep.tile([P, 2, 4, G, P], F32, name="y_sb", align_bytes=64)
+        m3 = keep.tile([P, 2, 4, 3, P], F32, name="m3", align_bytes=64)
+        m_sb = keep.tile([P, 2, 4, P], F32, name="m_sb", align_bytes=64)
+        s_sb = keep.tile([P, 2, 4, P], F32, name="s_sb", align_bytes=64)
         eg = {}
         ec = [[keep.tile([P, 2, P], U32, name="ec%d_%d" % (a, q), align_bytes=64) for q in range(3)] for a in range(2)]
         es = [[keep.tile([P, 2, P], U8, name="es%d_%d" % (a, q), align_bytes=64) for q in range(3)] for a in range(2)]
-        xg = [keep.tile([P, N, 4], BF16, name="xg", align_bytes=64, bufs=6) for h in range(G)]
+        xg = {}
         tb = {}
 
         def copy(eng, out, in_):
@@ -501,28 +666,29 @@ def tile_dihedralthreegroupblock_kernel(tc, x, w1, b1, ls, w2_bytes, w2_scale, o
             else:
                 nc.vector.tensor_copy(out=out, in_=in_)
 
-        def x_transpose(h):
-            b = bank([P, 2, 2, P])
-            for a in range(2):
-                words = xs[h // XH][:, a, h % XH, :].bitcast(F32)
+        def x_transpose(a, b, slot):
+            t = bank([P, 2, 2, P], slot)
+            for i in range(2):
+                words = xs[a, b][:, i, :].bitcast(F32)
                 for u in range(2):
-                    nc.tensor.transpose(b[:, a, u, :], words[:, u : C // 2 : 2], ident[:])
-            tb[h] = b
+                    nc.tensor.transpose(t[:, i, u, :], words[:, u : C // 2 : 2], ident[:])
+            tb[a, b] = t
 
-        def x_evac(h, eng):
+        def x_evac(a, b, eng):
+            xg[a, b] = keep.tile([P, 2, P, 4], BF16, name="xg", tag="xg", align_bytes=64, bufs=6)
             copy(
                 eng,
-                xg[h][:].rearrange("p n t -> p (n t)").bitcast(F32).rearrange("p (a r u) -> p a r u", a=2, u=2),
-                tb[h][:].rearrange("p a u r -> p a r u"),
+                xg[a, b][:].rearrange("p i n t -> p (i n t)").bitcast(F32).rearrange("p (i r u) -> p i r u", i=2, u=2),
+                tb[a, b][:].rearrange("p i u r -> p i r u"),
             )
 
-        def x_quant(h, dup=False):
+        def x_quant(a, h, dup):
             q = [i for i in range(3) if h in PAIRS[i]][0]
             slot = 2 if dup else PAIRS[q].index(h)
             nc.vector.quantize_mx(
-                out=xc[q][:, slot, :].bitcast(FP8X4),
-                scales=xsc[q][:, slot, :],
-                in_=xg[h][:].rearrange("p n t -> p (n t)"),
+                out=xc[q][:, a, slot, :].bitcast(FP8X4),
+                scales=xsc[q][:, a, slot, :],
+                in_=xg[a, h // 2][:, h % 2].rearrange("p n t -> p (n t)"),
             )
 
         wg = {}
@@ -547,28 +713,30 @@ def tile_dihedralthreegroupblock_kernel(tc, x, w1, b1, ls, w2_bytes, w2_scale, o
         wide = {}
         grp = {}
 
-        def w2_widen(j, t, eng):
-            if j not in wide:
-                wide[j] = work.tile([P, 4, C], BF16, name="wide", align_bytes=64, bufs=6)
-            src = w2_raw[j][:, t, :].bitcast(FP8)
+        def w2_widen(j, t, dh, eng):
+            if (j, dh) not in wide:
+                wide[j, dh] = work.tile([P, 4, C // 2], BF16, name="wide", align_bytes=64, bufs=12)
+            src = w2_raw[j][:, t, dh * C // 2 : (dh + 1) * C // 2].bitcast(FP8)
+            dst = wide[j, dh][:, t, :]
             if eng == "S":
-                nc.scalar.activation(out=wide[j][:, t, :], in_=src, func=ACT.Copy, scale=sc_sb[:, t : t + 1])
+                nc.scalar.activation(out=dst, in_=src, func=ACT.Copy, scale=sc_sb[:, t : t + 1])
             else:
-                nc.vector.tensor_scalar(
-                    out=wide[j][:, t, :], in0=src, scalar1=sc_sb[:, t : t + 1], scalar2=None, op0=ALU.mult
-                )
+                nc.vector.tensor_scalar(out=dst, in0=src, scalar1=sc_sb[:, t : t + 1], scalar2=None, op0=ALU.mult)
 
-        def w2_inter(j, eng):
-            grp[j] = work.tile([P, C, 4], BF16, name="grp", align_bytes=64, bufs=6)
+        def w2_inter(j, dh, eng):
+            grp[j, dh] = work.tile([P, C // 2, 4], BF16, name="grp", align_bytes=64, bufs=12)
             copy(
                 eng,
-                grp[j][:].rearrange("p (c i) t -> p c t i", i=4),
-                wide[j][:].rearrange("p t (c i) -> p c t i", i=4),
+                grp[j, dh][:].rearrange("p (c i) t -> p c t i", i=4),
+                wide[j, dh][:].rearrange("p t (c i) -> p c t i", i=4),
             )
 
-        def w2_quant(j):
+        def w2_quant(j, dh):
+            cols = slice(dh * C // 2, (dh + 1) * C // 2)
             nc.vector.quantize_mx(
-                out=w2c[j][:].bitcast(FP8X4), scales=w2s[j][:], in_=grp[j][:].rearrange("p n t -> p (n t)")
+                out=w2c[j][:, cols].bitcast(FP8X4),
+                scales=w2s[j][:, cols],
+                in_=grp[j, dh][:].rearrange("p n t -> p (n t)"),
             )
 
         def window(gp, j):
@@ -580,32 +748,17 @@ def tile_dihedralthreegroupblock_kernel(tc, x, w1, b1, ls, w2_bytes, w2_scale, o
                     return q, 1
             raise ValueError("no window")
 
-        def conv1_pair(acc, t, gp, j, first, last):
+        def conv1(acc, a, t, gp, j, first, last):
             q, s0 = window(gp, j)
             cols = slice(t * P, (t + 1) * P)
             nc.tensor.matmul_mx(
                 out=acc[:],
                 lhsT=w1c[j][:, cols].bitcast(FP8X4),
                 lhsT_scale=w1s[j][:, cols],
-                rhs=xc[q][:, s0 : s0 + 2, :].rearrange("p s n -> p (s n)").bitcast(FP8X4),
-                rhs_scale=xsc[q][:, s0 : s0 + 2, :].rearrange("p s n -> p (s n)"),
+                rhs=xc[q][:, a, s0 : s0 + 2, :].rearrange("p s n -> p (s n)").bitcast(FP8X4),
+                rhs_scale=xsc[q][:, a, s0 : s0 + 2, :].rearrange("p s n -> p (s n)"),
                 start=first,
                 stop=last,
-            )
-
-        def conv1_half(acc, t, pos, a, i):
-            h = POS[i]
-            j = K[h][POS[pos]]
-            cols = slice(t * P, (t + 1) * P)
-            n = slice(a * P, (a + 1) * P)
-            nc.tensor.matmul_mx(
-                out=acc,
-                lhsT=w1c[j][:, cols].bitcast(FP8X4),
-                lhsT_scale=w1s[j][:, cols],
-                rhs=xc[i // 2][:, i % 2, n].bitcast(FP8X4),
-                rhs_scale=xsc[i // 2][:, i % 2, n],
-                start=(i == 0),
-                stop=(i == G - 1),
             )
 
         def y_evac(out, in_, t, eng):
@@ -614,31 +767,30 @@ def tile_dihedralthreegroupblock_kernel(tc, x, w1, b1, ls, w2_bytes, w2_scale, o
             else:
                 nc.vector.tensor_scalar(out=out, in0=in_, scalar1=b1_sb[:, t : t + 1], scalar2=None, op0=ALU.add)
 
-        def pool_max0(t, n):
-            nc.vector.tensor_tensor(out=m3[:, t, :, n], in0=y_sb[:, t, 0:3, n], in1=y_sb[:, t, 3:6, n], op=ALU.max)
+        def pool_max0(a, tt):
+            nc.vector.tensor_tensor(out=m3[:, a, tt], in0=y_sb[:, a, tt, 0:3, :], in1=y_sb[:, a, tt, 3:6, :], op=ALU.max)
 
-        def pool_max1(t, n):
-            nc.vector.tensor_tensor(out=m_sb[:, t, n], in0=m3[:, t, 0, n], in1=m3[:, t, 1, n], op=ALU.max)
+        def pool_max1(a, tt):
+            nc.vector.tensor_tensor(out=m_sb[:, a, tt], in0=m3[:, a, tt, 0, :], in1=m3[:, a, tt, 1, :], op=ALU.max)
 
-        def pool_max2(t, n):
-            nc.vector.tensor_tensor(out=m_sb[:, t, n], in0=m_sb[:, t, n], in1=m3[:, t, 2, n], op=ALU.max)
+        def pool_max2(a, tt):
+            nc.vector.tensor_tensor(out=m_sb[:, a, tt], in0=m_sb[:, a, tt], in1=m3[:, a, tt, 2, :], op=ALU.max)
 
-        def gate(t, n):
-            nc.scalar.activation(out=s_sb[:, t, n], in_=m_sb[:, t, n], func=ACT.Sigmoid)
+        def gate(a, tt):
+            nc.scalar.activation(out=s_sb[:, a, tt], in_=m_sb[:, a, tt], func=ACT.Sigmoid)
 
-        def gain(t, n):
+        def gain(a, t):
             nc.vector.tensor_scalar(
-                out=s_sb[:, t, n], in0=s_sb[:, t, n], scalar1=ls_sb[:, t : t + 1], scalar2=None, op0=ALU.mult
+                out=s_sb[:, a, t], in0=s_sb[:, a, t], scalar1=ls_sb[:, t : t + 1], scalar2=None, op0=ALU.mult
             )
 
         def e_mult(a, pos):
-            n = slice(a * P, (a + 1) * P)
             if (a, pos // 2) not in eg:
                 eg[a, pos // 2] = keep.tile([P, 2, P, 4], BF16, name="eg", tag="xg", align_bytes=64, bufs=6)
             nc.vector.tensor_tensor(
                 out=eg[a, pos // 2][:, pos % 2].rearrange("p (c i) t -> p c t i", i=4),
-                in0=y_sb[:, :, pos, n].rearrange("p t (c i) -> p c t i", i=4),
-                in1=s_sb[:, :, n].rearrange("p t (c i) -> p c t i", i=4),
+                in0=y_sb[:, a, :, pos, :].rearrange("p t (c i) -> p c t i", i=4),
+                in1=s_sb[:, a].rearrange("p t (c i) -> p c t i", i=4),
                 op=ALU.mult,
             )
 
@@ -649,99 +801,75 @@ def tile_dihedralthreegroupblock_kernel(tc, x, w1, b1, ls, w2_bytes, w2_scale, o
                 in_=eg[a, pos // 2][:, pos % 2].rearrange("p n t -> p (n t)"),
             )
 
-        def conv2(acc, a, h, j, first, last):
+        def conv2(acc, a, dh, h, j, first, last):
             i = POS.index(h)
+            cols = slice(dh * C // 2, (dh + 1) * C // 2)
             nc.tensor.matmul_mx(
                 out=acc[:],
                 lhsT=ec[a][i // 2][:, i % 2, :].bitcast(FP8X4),
                 lhsT_scale=es[a][i // 2][:, i % 2, :],
-                rhs=w2c[j][:].bitcast(FP8X4),
-                rhs_scale=w2s[j][:],
+                rhs=w2c[j][:, cols].bitcast(FP8X4),
+                rhs_scale=w2s[j][:, cols],
                 start=first,
                 stop=last,
             )
 
-        def store(acc, a, g, eng):
-            o = work.tile([P, C], F32, name="o_sb", bufs=4)
+        def store(acc, a, dh, g, eng):
+            o = work.tile([P, C // 2], F32, name="o_sb", bufs=8)
             copy(eng, o[:], acc[:])
-            nc.sync.dma_start(out=out[a * P : (a + 1) * P, g, :], in_=o[:])
+            nc.sync.dma_start(out=out[a * P : (a + 1) * P, g, dh * C // 2 : (dh + 1) * C // 2], in_=o[:])
 
-        ALL = slice(0, N)
-        HALF = (slice(0, P), slice(P, N))
         accs = {}
         count = {}
 
-        def group(key, shape):
+        def group(key):
             if key not in accs:
-                accs[key] = bank(shape)
-            return accs[key]
-
-        def nth(key):
+                accs[key] = bank([P, 2 * P], SLOTS[key])
             count[key] = count.get(key, 0) + 1
-            return count[key]
-
-        def flat(ap):
-            return ap.rearrange("p g n -> p (g n)")
+            return accs[key], count[key] == 1, count[key] == G
 
         for step in PROGRAM:
             kind, arg, eng = step[0], step[1:-1], step[-1]
             if kind == "T":
-                x_transpose(arg[0])
+                x_transpose(arg[0], arg[1], SLOTS[("T",) + arg])
             elif kind == "E":
-                x_evac(arg[0], eng)
+                x_evac(arg[0], arg[1], eng)
             elif kind == "Q":
-                x_quant(arg[0], dup=(arg[1] == 1))
+                x_quant(arg[0], arg[1], arg[2] == 1)
             elif kind == "I":
                 w1_inter(arg[0], arg[1], eng)
             elif kind == "q":
                 w1_quant(arg[0], arg[1])
             elif kind == "W":
-                w2_widen(arg[0], arg[1], eng)
+                w2_widen(arg[0], arg[1], arg[2], eng)
             elif kind == "I2":
-                w2_inter(arg[0], eng)
+                w2_inter(arg[0], arg[1], eng)
             elif kind == "q2":
-                w2_quant(arg[0])
+                w2_quant(arg[0], arg[1])
             elif kind == "A":
-                j, gp, t = arg
-                n = nth(("A", gp, t))
-                conv1_pair(group(("A", gp, t), [P, C]), t, gp, j, n == 1, n == G)
-            elif kind in ("B2", "C"):
-                a, k, i, z = arg
-                t = 2 if kind == "B2" else 3
-                conv1_half(group((kind, a, k), [P, 3, P])[:, i, :], t, 3 * k + i, a, z)
+                a, t, gp, j = arg
+                acc, first, last = group(("A", a, t, gp))
+                conv1(acc, a, t, gp, j, first, last)
             elif kind == "Y":
-                if arg[0] == "A":
-                    gp, t = arg[1:]
-                    y_evac(flat(y_sb[:, t, 2 * gp : 2 * gp + 2, :]), accs["A", gp, t][:], t, eng)
-                else:
-                    t = 2 if arg[0] == "B2" else 3
-                    a, k = arg[1:]
-                    y_evac(y_sb[:, t, 3 * k : 3 * k + 3, HALF[a]], accs[arg[0], a, k][:], t, eng)
-            elif kind == "M0":
-                if arg[0] in (0, 1):
-                    pool_max0(arg[0], ALL)
-                else:
-                    pool_max0(2 if arg[0] == "B2" else 3, HALF[arg[1]])
-            elif kind in ("M1", "M2", "g"):
-                f = {"M1": pool_max1, "M2": pool_max2, "g": gate}[kind]
-                if arg[0] == "A":
-                    f(slice(0, 2), ALL)
-                else:
-                    f(slice(2, 4), HALF[arg[1]])
+                a, t, gp = arg
+                y_evac(
+                    y_sb[:, a, t, 2 * gp : 2 * gp + 2, :].rearrange("p g n -> p (g n)"), accs["A", a, t, gp][:], t, eng
+                )
+            elif kind in ("M0", "M1", "M2", "g"):
+                f = {"M0": pool_max0, "M1": pool_max1, "M2": pool_max2, "g": gate}[kind]
+                f(arg[0], slice(2 * arg[1], 2 * arg[1] + 2))
             elif kind == "n":
-                if arg[0] == "A":
-                    gain(arg[1], ALL)
-                else:
-                    gain(2 if arg[0] == "B2" else 3, HALF[arg[1]])
+                gain(arg[0], arg[1])
             elif kind == "e":
                 e_mult(arg[0], arg[1])
             elif kind == "eq":
                 e_quant(arg[0], arg[1])
             elif kind == "D":
-                a, pos, j = arg
+                a, dh, pos, j = arg
                 h = POS[pos]
                 g = [gg for gg in range(G) if K[h][gg] == j][0]
-                n = nth(("D", a, g))
-                conv2(group(("D", a, g), [P, C]), a, h, j, n == 1, n == G)
+                acc, first, last = group(("D", a, dh, g))
+                conv2(acc, a, dh, h, j, first, last)
             elif kind == "O":
-                store(accs["D", arg[0], arg[1]], arg[0], arg[1], eng)
+                a, dh, g = arg
+                store(accs["D", a, dh, g], a, dh, g, eng)

@@ -17,6 +17,8 @@ K = (
 PAIRS = ((0, 3), (1, 5), (2, 4))
 POS = (0, 3, 1, 5, 2, 4)
 
+YMERGE = ((0, 2), (0, 3), (1, 1), (1, 2), (1, 3))
+
 LOADS = (('x', 0, 0), ('x', 0, 1), ('x', 0, 2), ('w1', 0), ('w1', 1), ('x', 1, 0), ('x', 1, 1), ('x', 1, 2), ('w1', 2), ('w1', 3), ('w1', 4), ('w1', 5), ('w2', 0), ('w2', 1), ('w2', 2), ('w2', 3), ('w2', 4), ('w2', 5))
 
 SLOTS = {
@@ -35,45 +37,28 @@ SLOTS = {
     ('A', 1, 0, 0): 2,
     ('A', 1, 0, 1): 1,
     ('A', 0, 2, 0): 3,
-    ('A', 0, 2, 1): 4,
-    ('A', 0, 2, 2): 5,
-    ('A', 0, 3, 0): 6,
-    ('A', 0, 3, 1): 7,
-    ('A', 0, 3, 2): 0,
-    ('A', 1, 0, 2): 2,
-    ('A', 1, 1, 0): 1,
-    ('A', 1, 1, 1): 3,
-    ('A', 1, 1, 2): 4,
-    ('A', 1, 2, 0): 5,
-    ('A', 1, 2, 1): 6,
-    ('A', 1, 2, 2): 7,
-    ('A', 1, 3, 0): 0,
-    ('A', 1, 3, 1): 2,
-    ('A', 1, 3, 2): 1,
-    ('D', 0, 0, 0): 3,
-    ('D', 0, 0, 1): 4,
-    ('D', 0, 0, 2): 5,
-    ('D', 0, 0, 3): 6,
-    ('D', 0, 0, 4): 7,
-    ('D', 0, 0, 5): 0,
-    ('D', 1, 0, 0): 2,
-    ('D', 1, 0, 1): 1,
-    ('D', 1, 0, 2): 7,
-    ('D', 1, 0, 3): 6,
+    ('A', 0, 2, 2): 4,
+    ('A', 0, 3, 0): 5,
+    ('A', 0, 3, 2): 6,
+    ('A', 1, 0, 2): 7,
+    ('A', 1, 1, 0): 0,
+    ('A', 1, 1, 2): 2,
+    ('A', 1, 2, 0): 1,
+    ('A', 1, 2, 2): 3,
+    ('A', 1, 3, 0): 4,
+    ('A', 1, 3, 2): 5,
+    ('D', 0, 0, 0): 6,
+    ('D', 0, 0, 1): 7,
+    ('D', 0, 0, 3): 0,
+    ('D', 0, 0, 5): 2,
+    ('D', 0, 0, 2): 1,
+    ('D', 0, 0, 4): 3,
+    ('D', 1, 0, 0): 4,
+    ('D', 1, 0, 1): 5,
+    ('D', 1, 0, 2): 2,
+    ('D', 1, 0, 3): 7,
     ('D', 1, 0, 4): 0,
-    ('D', 1, 0, 5): 4,
-    ('D', 0, 1, 0): 3,
-    ('D', 0, 1, 3): 5,
-    ('D', 0, 1, 1): 0,
-    ('D', 0, 1, 5): 6,
-    ('D', 0, 1, 2): 4,
-    ('D', 0, 1, 4): 1,
-    ('D', 1, 1, 0): 2,
-    ('D', 1, 1, 1): 7,
-    ('D', 1, 1, 2): 6,
-    ('D', 1, 1, 3): 0,
-    ('D', 1, 1, 4): 5,
-    ('D', 1, 1, 5): 3,
+    ('D', 1, 0, 5): 6,
 }
 
 PROGRAM = (
@@ -82,511 +67,357 @@ PROGRAM = (
     ('E', 0, 0, 'S'),
     ('T', 0, 2, 'P'),
     ('E', 0, 1, 'S'),
-    ('Q', 0, 0, 1, 'V'),
-    ('Q', 0, 1, 1, 'V'),
     ('Q', 0, 0, 0, 'V'),
+    ('Q', 0, 0, 1, 'V'),
     ('E', 0, 2, 'S'),
     ('Q', 0, 1, 0, 'V'),
-    ('Q', 0, 3, 0, 'V'),
     ('I', 0, 0, 'V'),
     ('I', 0, 1, 'S'),
-    ('Q', 0, 4, 0, 'V'),
     ('q', 0, 0, 'V'),
-    ('Q', 0, 5, 0, 'V'),
+    ('Q', 0, 1, 1, 'V'),
     ('A', 0, 0, 0, 0, 'P'),
+    ('I', 1, 0, 'S'),
     ('Q', 0, 2, 0, 'V'),
-    ('I', 1, 1, 'S'),
-    ('I', 1, 0, 'V'),
     ('A', 0, 1, 0, 0, 'P'),
     ('A', 0, 0, 1, 0, 'P'),
+    ('Q', 0, 2, 1, 'V'),
     ('A', 0, 1, 1, 0, 'P'),
+    ('I', 1, 1, 'V'),
     ('A', 0, 0, 2, 0, 'P'),
     ('A', 0, 1, 2, 0, 'P'),
-    ('Q', 0, 2, 1, 'V'),
     ('T', 1, 0, 'P'),
-    ('q', 1, 0, 'V'),
-    ('A', 0, 0, 0, 1, 'P'),
+    ('q', 0, 1, 'V'),
     ('E', 1, 0, 'S'),
+    ('q', 1, 0, 'V'),
+    ('q', 1, 1, 'V'),
+    ('A', 0, 0, 0, 1, 'P'),
+    ('Q', 1, 0, 0, 'V'),
     ('A', 0, 1, 0, 1, 'P'),
     ('A', 0, 0, 1, 1, 'P'),
+    ('I', 2, 1, 'S'),
     ('A', 0, 1, 1, 1, 'P'),
+    ('I', 2, 0, 'V'),
     ('A', 0, 0, 2, 1, 'P'),
     ('A', 0, 1, 2, 1, 'P'),
     ('T', 1, 1, 'P'),
-    ('I', 2, 1, 'S'),
-    ('I', 2, 0, 'V'),
-    ('T', 1, 2, 'P'),
-    ('q', 0, 1, 'V'),
     ('q', 2, 0, 'V'),
-    ('Q', 1, 0, 0, 'V'),
-    ('I', 3, 0, 'S'),
+    ('T', 1, 2, 'P'),
+    ('E', 1, 1, 'S'),
+    ('I', 3, 0, 'V'),
     ('A', 0, 0, 0, 2, 'P'),
-    ('q', 2, 1, 'V'),
     ('A', 0, 1, 0, 2, 'P'),
-    ('Q', 1, 0, 1, 'V'),
+    ('E', 1, 2, 'S'),
     ('A', 0, 0, 1, 2, 'P'),
-    ('q', 1, 1, 'V'),
+    ('Q', 1, 1, 0, 'V'),
     ('A', 0, 1, 1, 2, 'P'),
     ('A', 0, 0, 2, 2, 'P'),
-    ('Q', 1, 1, 1, 'V'),
-    ('A', 0, 1, 2, 2, 'P'),
-    ('I', 4, 1, 'V'),
-    ('E', 1, 1, 'S'),
     ('q', 3, 0, 'V'),
-    ('E', 1, 2, 'S'),
-    ('Q', 1, 3, 0, 'V'),
-    ('A', 0, 0, 0, 3, 'P'),
+    ('A', 0, 1, 2, 2, 'P'),
+    ('I', 3, 1, 'S'),
     ('Q', 1, 2, 0, 'V'),
+    ('A', 0, 0, 0, 3, 'P'),
     ('A', 0, 1, 0, 3, 'P'),
-    ('Q', 1, 2, 1, 'V'),
-    ('I', 4, 0, 'S'),
+    ('I', 4, 0, 'V'),
     ('A', 0, 0, 1, 3, 'P'),
-    ('Q', 1, 1, 0, 'V'),
     ('A', 0, 1, 1, 3, 'P'),
-    ('Q', 1, 4, 0, 'V'),
     ('A', 0, 0, 2, 3, 'P'),
-    ('Q', 1, 5, 0, 'V'),
     ('A', 0, 1, 2, 3, 'P'),
-    ('I', 5, 0, 'V'),
     ('A', 1, 0, 0, 0, 'P'),
+    ('Q', 1, 9, 1, 'V'),
+    ('I', 5, 0, 'S'),
     ('A', 1, 0, 1, 0, 'P'),
     ('A', 1, 0, 0, 1, 'P'),
     ('A', 1, 0, 1, 1, 'P'),
-    ('A', 1, 0, 0, 2, 'P'),
-    ('W', 1, 1, 0, 'V'),
-    ('I', 5, 1, 'S'),
-    ('A', 1, 0, 1, 2, 'P'),
     ('q', 4, 0, 'V'),
+    ('A', 1, 0, 0, 2, 'P'),
+    ('A', 1, 0, 1, 2, 'P'),
     ('A', 1, 0, 0, 3, 'P'),
+    ('I', 5, 1, 'V'),
     ('A', 1, 0, 1, 3, 'P'),
-    ('q', 4, 1, 'V'),
     ('A', 0, 0, 0, 4, 'P'),
     ('A', 0, 1, 0, 4, 'P'),
-    ('W', 3, 3, 0, 'V'),
     ('A', 0, 0, 1, 4, 'P'),
-    ('W', 0, 3, 0, 'V'),
+    ('W', 0, 1, 'S'),
     ('A', 0, 1, 1, 4, 'P'),
     ('q', 5, 0, 'V'),
     ('A', 0, 0, 2, 4, 'P'),
     ('A', 0, 1, 2, 4, 'P'),
-    ('W', 3, 2, 0, 'S'),
-    ('W', 0, 1, 0, 'V'),
+    ('q', 3, 1, 'V'),
     ('A', 1, 0, 0, 4, 'P'),
-    ('W', 4, 2, 0, 'V'),
     ('A', 1, 0, 1, 4, 'P'),
-    ('W', 0, 0, 0, 'S'),
-    ('W', 4, 1, 0, 'V'),
     ('A', 0, 0, 0, 5, 'P'),
-    ('I', 3, 1, 'V'),
+    ('q', 2, 1, 'V'),
     ('A', 0, 1, 0, 5, 'P'),
-    ('Y', 0, 0, 0, 'S'),
     ('A', 0, 0, 1, 5, 'P'),
+    ('Y', 0, 0, 0, 'S'),
+    ('I', 4, 1, 'V'),
     ('A', 0, 1, 1, 5, 'P'),
     ('A', 0, 0, 2, 5, 'P'),
-    ('Y', 0, 1, 0, 'S'),
-    ('A', 0, 1, 2, 5, 'P'),
-    ('q', 5, 1, 'V'),
-    ('A', 1, 0, 0, 5, 'P'),
-    ('W', 1, 2, 0, 'S'),
-    ('A', 1, 0, 1, 5, 'P'),
-    ('q', 3, 1, 'V'),
-    ('A', 0, 2, 0, 0, 'P'),
-    ('W', 0, 2, 0, 'S'),
-    ('A', 0, 2, 0, 1, 'P'),
-    ('W', 0, 0, 1, 'V'),
-    ('A', 0, 2, 0, 2, 'P'),
-    ('Y', 0, 1, 2, 'S'),
-    ('W', 4, 3, 0, 'V'),
-    ('A', 0, 2, 0, 3, 'P'),
-    ('A', 0, 2, 0, 4, 'P'),
-    ('W', 0, 3, 1, 'V'),
-    ('Y', 0, 1, 1, 'S'),
-    ('A', 0, 2, 0, 5, 'P'),
-    ('W', 1, 0, 0, 'V'),
-    ('A', 0, 2, 1, 0, 'P'),
-    ('I2', 0, 0, 'V'),
     ('Y', 0, 0, 1, 'S'),
+    ('A', 0, 1, 2, 5, 'P'),
+    ('A', 1, 0, 0, 5, 'P'),
+    ('A', 1, 0, 1, 5, 'P'),
+    ('W', 0, 0, 'S'),
+    ('A', 0, 2, 0, 0, 'P'),
+    ('q', 5, 1, 'V'),
+    ('A', 0, 2, 0, 1, 'P'),
+    ('A', 0, 2, 0, 2, 'P'),
+    ('q', 4, 1, 'V'),
+    ('A', 0, 2, 0, 3, 'P'),
+    ('W', 1, 3, 'V'),
+    ('A', 0, 2, 0, 4, 'P'),
+    ('A', 0, 2, 0, 5, 'P'),
+    ('Y', 0, 1, 1, 'S'),
+    ('A', 0, 2, 1, 0, 'P'),
     ('A', 0, 2, 1, 1, 'P'),
+    ('Y', 0, 1, 0, 'V'),
+    ('W', 1, 1, 'S'),
     ('A', 0, 2, 1, 2, 'P'),
-    ('W', 4, 0, 0, 'S'),
     ('A', 0, 2, 1, 3, 'P'),
+    ('W', 1, 0, 'V'),
     ('A', 0, 2, 1, 4, 'P'),
-    ('Y', 0, 0, 2, 'S'),
-    ('W', 1, 3, 0, 'V'),
     ('A', 0, 2, 1, 5, 'P'),
     ('A', 0, 2, 2, 0, 'P'),
-    ('W', 3, 1, 0, 'V'),
-    ('W', 5, 0, 0, 'S'),
     ('A', 0, 2, 2, 1, 'P'),
-    ('M0', 0, 0, 'V'),
     ('A', 0, 2, 2, 2, 'P'),
-    ('Y', 0, 2, 1, 'S'),
+    ('Y', 0, 1, 2, 'V'),
     ('A', 0, 2, 2, 3, 'P'),
     ('A', 0, 2, 2, 4, 'P'),
+    ('Y', 0, 0, 2, 'S'),
+    ('W', 0, 2, 'V'),
     ('A', 0, 2, 2, 5, 'P'),
-    ('W', 2, 1, 0, 'S'),
     ('A', 0, 3, 0, 0, 'P'),
-    ('A', 0, 3, 0, 1, 'P'),
     ('Y', 0, 2, 0, 'S'),
-    ('I2', 1, 0, 'V'),
+    ('A', 0, 3, 0, 1, 'P'),
     ('A', 0, 3, 0, 2, 'P'),
     ('A', 0, 3, 0, 3, 'P'),
-    ('Y', 0, 2, 2, 'S'),
+    ('W', 0, 3, 'V'),
     ('A', 0, 3, 0, 4, 'P'),
+    ('Y', 0, 2, 2, 'S'),
     ('A', 0, 3, 0, 5, 'P'),
-    ('Y', 1, 0, 1, 'S'),
     ('A', 0, 3, 1, 0, 'P'),
-    ('I2', 4, 0, 'V'),
     ('A', 0, 3, 1, 1, 'P'),
-    ('W', 5, 3, 0, 'S'),
+    ('W', 1, 2, 'S'),
+    ('M0', 0, 0, 'V'),
     ('A', 0, 3, 1, 2, 'P'),
     ('A', 0, 3, 1, 3, 'P'),
-    ('Y', 1, 0, 0, 'S'),
     ('A', 0, 3, 1, 4, 'P'),
     ('A', 0, 3, 1, 5, 'P'),
-    ('M1', 0, 0, 'V'),
-    ('W', 5, 1, 0, 'S'),
     ('A', 0, 3, 2, 0, 'P'),
     ('A', 0, 3, 2, 1, 'P'),
-    ('W', 2, 0, 0, 'V'),
-    ('Y', 0, 3, 1, 'S'),
+    ('Y', 1, 0, 0, 'V'),
     ('A', 0, 3, 2, 2, 'P'),
-    ('q2', 4, 0, 'V'),
     ('A', 0, 3, 2, 3, 'P'),
     ('Y', 0, 3, 0, 'S'),
     ('A', 0, 3, 2, 4, 'P'),
-    ('M2', 0, 0, 'V'),
+    ('I2', 0, 0, 'V'),
     ('A', 0, 3, 2, 5, 'P'),
     ('A', 1, 0, 2, 0, 'P'),
-    ('W', 5, 2, 0, 'V'),
-    ('Y', 0, 3, 2, 'S'),
     ('A', 1, 0, 2, 1, 'P'),
-    ('q2', 0, 0, 'V'),
+    ('Y', 1, 0, 1, 'S'),
     ('A', 1, 0, 2, 2, 'P'),
     ('A', 1, 0, 2, 3, 'P'),
-    ('W', 2, 3, 0, 'S'),
-    ('M0', 0, 1, 'V'),
     ('A', 1, 0, 2, 4, 'P'),
+    ('Y', 0, 3, 2, 'S'),
     ('A', 1, 0, 2, 5, 'P'),
-    ('g', 0, 0, 'S'),
     ('A', 1, 1, 0, 0, 'P'),
+    ('I2', 2, 0, 'S'),
     ('A', 1, 1, 0, 1, 'P'),
-    ('I2', 5, 0, 'S'),
+    ('M0', 0, 1, 'V'),
     ('A', 1, 1, 0, 2, 'P'),
     ('A', 1, 1, 0, 3, 'P'),
-    ('q2', 1, 0, 'V'),
     ('A', 1, 1, 0, 4, 'P'),
     ('A', 1, 1, 0, 5, 'P'),
-    ('M1', 0, 1, 'V'),
     ('A', 1, 1, 1, 0, 'P'),
     ('A', 1, 1, 1, 1, 'P'),
-    ('W', 3, 0, 0, 'V'),
     ('A', 1, 1, 1, 2, 'P'),
+    ('q2', 0, 0, 'V'),
     ('A', 1, 1, 1, 3, 'P'),
-    ('n', 0, 1, 'V'),
-    ('M2', 0, 1, 'V'),
     ('A', 1, 1, 1, 4, 'P'),
-    ('Y', 1, 0, 2, 'S'),
     ('A', 1, 1, 1, 5, 'P'),
-    ('n', 0, 0, 'V'),
     ('A', 1, 1, 2, 0, 'P'),
-    ('q2', 5, 0, 'V'),
-    ('g', 0, 1, 'S'),
+    ('M1', 0, 2, 'V'),
     ('A', 1, 1, 2, 1, 'P'),
     ('A', 1, 1, 2, 2, 'P'),
-    ('W', 2, 2, 0, 'V'),
-    ('W', 0, 2, 1, 'S'),
     ('A', 1, 1, 2, 3, 'P'),
-    ('n', 0, 3, 'V'),
     ('A', 1, 1, 2, 4, 'P'),
-    ('n', 0, 2, 'V'),
-    ('I2', 3, 0, 'S'),
-    ('W', 2, 2, 1, 'V'),
     ('A', 1, 1, 2, 5, 'P'),
     ('A', 1, 2, 0, 0, 'P'),
-    ('e', 0, 1, 'V'),
+    ('M2', 0, 2, 'V'),
     ('A', 1, 2, 0, 1, 'P'),
+    ('Y', 1, 1, 0, 'S'),
     ('A', 1, 2, 0, 2, 'P'),
     ('A', 1, 2, 0, 3, 'P'),
     ('A', 1, 2, 0, 4, 'P'),
+    ('W', 2, 1, 'V'),
     ('A', 1, 2, 0, 5, 'P'),
-    ('e', 0, 2, 'V'),
+    ('g', 0, 2, 'S'),
     ('A', 1, 2, 1, 0, 'P'),
     ('A', 1, 2, 1, 1, 'P'),
     ('A', 1, 2, 1, 2, 'P'),
-    ('Y', 1, 1, 2, 'S'),
     ('A', 1, 2, 1, 3, 'P'),
+    ('W', 2, 2, 'V'),
     ('A', 1, 2, 1, 4, 'P'),
-    ('Y', 1, 1, 0, 'S'),
-    ('q2', 3, 0, 'V'),
+    ('Y', 1, 1, 2, 'S'),
     ('A', 1, 2, 1, 5, 'P'),
     ('A', 1, 2, 2, 0, 'P'),
-    ('e', 0, 0, 'V'),
-    ('Y', 1, 2, 1, 'S'),
+    ('n', 0, 1, 'S'),
     ('A', 1, 2, 2, 1, 'P'),
+    ('n', 0, 2, 'V'),
     ('A', 1, 2, 2, 2, 'P'),
+    ('I2', 1, 0, 'S'),
+    ('n', 0, 3, 'V'),
     ('A', 1, 2, 2, 3, 'P'),
-    ('Y', 1, 2, 0, 'S'),
+    ('n', 0, 0, 'V'),
     ('A', 1, 2, 2, 4, 'P'),
+    ('Y', 1, 0, 2, 'V'),
     ('A', 1, 2, 2, 5, 'P'),
-    ('e', 0, 4, 'V'),
-    ('I2', 2, 0, 'S'),
     ('A', 1, 3, 0, 0, 'P'),
     ('A', 1, 3, 0, 1, 'P'),
+    ('e', 0, 2, 'V'),
     ('A', 1, 3, 0, 2, 'P'),
     ('A', 1, 3, 0, 3, 'P'),
-    ('e', 0, 3, 'V'),
     ('A', 1, 3, 0, 4, 'P'),
     ('A', 1, 3, 0, 5, 'P'),
     ('A', 1, 3, 1, 0, 'P'),
+    ('e', 0, 3, 'V'),
     ('A', 1, 3, 1, 1, 'P'),
     ('A', 1, 3, 1, 2, 'P'),
-    ('Y', 1, 2, 2, 'S'),
-    ('eq', 0, 0, 'V'),
     ('A', 1, 3, 1, 3, 'P'),
-    ('q2', 2, 0, 'V'),
     ('A', 1, 3, 1, 4, 'P'),
-    ('Y', 1, 1, 1, 'S'),
     ('A', 1, 3, 1, 5, 'P'),
-    ('eq', 0, 3, 'V'),
+    ('e', 0, 1, 'V'),
     ('A', 1, 3, 2, 0, 'P'),
-    ('Y', 1, 3, 1, 'S'),
-    ('eq', 0, 1, 'V'),
     ('A', 1, 3, 2, 1, 'P'),
     ('A', 1, 3, 2, 2, 'P'),
-    ('eq', 0, 2, 'V'),
+    ('W', 2, 3, 'S'),
     ('A', 1, 3, 2, 3, 'P'),
-    ('W', 1, 3, 1, 'S'),
-    ('M0', 1, 0, 'V'),
     ('A', 1, 3, 2, 4, 'P'),
+    ('e', 0, 4, 'V'),
     ('A', 1, 3, 2, 5, 'P'),
-    ('Y', 1, 3, 0, 'S'),
-    ('D', 0, 0, 0, 0, 'P'),
-    ('D', 0, 0, 0, 1, 'P'),
+    ('e', 0, 0, 'V'),
+    ('Y', 1, 2, 0, 'S'),
+    ('eq', 0, 1, 'V'),
     ('Y', 1, 3, 2, 'S'),
-    ('D', 0, 0, 0, 2, 'P'),
-    ('D', 0, 0, 0, 3, 'P'),
-    ('eq', 0, 4, 'V'),
-    ('W', 3, 3, 1, 'S'),
-    ('D', 0, 0, 0, 4, 'P'),
-    ('M0', 1, 1, 'V'),
-    ('D', 0, 0, 0, 5, 'P'),
-    ('W', 5, 3, 1, 'S'),
+    ('eq', 0, 0, 'V'),
+    ('Y', 1, 3, 0, 'S'),
+    ('q2', 1, 0, 'V'),
+    ('D', 0, 0, 0, 0, 'P'),
+    ('I2', 3, 0, 'S'),
+    ('e', 0, 5, 'V'),
+    ('D', 0, 0, 0, 1, 'P'),
     ('D', 0, 0, 1, 0, 'P'),
     ('D', 0, 0, 1, 1, 'P'),
-    ('W', 2, 1, 1, 'S'),
-    ('D', 0, 0, 1, 2, 'P'),
-    ('D', 0, 0, 1, 3, 'P'),
-    ('W', 1, 1, 1, 'S'),
-    ('D', 0, 0, 1, 4, 'P'),
-    ('M1', 1, 0, 'V'),
-    ('D', 0, 0, 1, 5, 'P'),
-    ('W', 2, 0, 1, 'S'),
+    ('Y', 1, 2, 2, 'V'),
     ('D', 0, 0, 2, 0, 'P'),
-    ('M1', 1, 1, 'V'),
+    ('W', 2, 0, 'V'),
     ('D', 0, 0, 2, 1, 'P'),
-    ('W', 0, 1, 1, 'S'),
-    ('D', 0, 0, 2, 2, 'P'),
-    ('M2', 1, 0, 'V'),
-    ('D', 0, 0, 2, 3, 'P'),
-    ('W', 3, 1, 1, 'S'),
-    ('D', 0, 0, 2, 4, 'P'),
-    ('M2', 1, 1, 'V'),
-    ('D', 0, 0, 2, 5, 'P'),
     ('D', 0, 0, 3, 0, 'P'),
-    ('g', 1, 0, 'S'),
-    ('e', 0, 5, 'V'),
+    ('eq', 0, 2, 'V'),
     ('D', 0, 0, 3, 1, 'P'),
-    ('D', 0, 0, 3, 2, 'P'),
-    ('g', 1, 1, 'S'),
-    ('D', 0, 0, 3, 3, 'P'),
-    ('D', 0, 0, 3, 4, 'P'),
-    ('W', 4, 2, 1, 'S'),
-    ('D', 0, 0, 3, 5, 'P'),
-    ('n', 1, 0, 'V'),
-    ('n', 1, 3, 'V'),
+    ('q2', 2, 0, 'V'),
     ('D', 0, 0, 4, 0, 'P'),
-    ('n', 1, 1, 'V'),
-    ('W', 4, 1, 1, 'S'),
-    ('n', 1, 2, 'V'),
+    ('I2', 4, 0, 'S'),
     ('D', 0, 0, 4, 1, 'P'),
-    ('eq', 0, 5, 'V'),
-    ('D', 0, 0, 4, 2, 'P'),
-    ('W', 5, 1, 1, 'S'),
-    ('D', 0, 0, 4, 3, 'P'),
-    ('e', 1, 0, 'V'),
-    ('D', 0, 0, 4, 4, 'P'),
-    ('W', 1, 0, 1, 'S'),
-    ('D', 0, 0, 4, 5, 'P'),
+    ('q2', 3, 0, 'V'),
     ('D', 0, 0, 5, 0, 'P'),
     ('D', 0, 0, 5, 1, 'P'),
-    ('O', 0, 0, 4, 'S'),
+    ('D', 0, 0, 0, 2, 'P'),
+    ('M0', 1, 0, 'V'),
+    ('D', 0, 0, 1, 2, 'P'),
+    ('D', 0, 0, 2, 2, 'P'),
+    ('D', 0, 0, 3, 2, 'P'),
+    ('M0', 1, 1, 'V'),
+    ('D', 0, 0, 4, 2, 'P'),
     ('D', 0, 0, 5, 2, 'P'),
-    ('e', 1, 1, 'V'),
+    ('I2', 5, 0, 'S'),
+    ('D', 0, 0, 0, 3, 'P'),
+    ('q2', 4, 0, 'V'),
+    ('D', 0, 0, 1, 3, 'P'),
+    ('D', 0, 0, 2, 3, 'P'),
+    ('M1', 1, 2, 'V'),
+    ('D', 0, 0, 3, 3, 'P'),
+    ('D', 0, 0, 4, 3, 'P'),
     ('D', 0, 0, 5, 3, 'P'),
+    ('M2', 1, 2, 'V'),
+    ('D', 0, 0, 0, 4, 'P'),
+    ('D', 0, 0, 1, 4, 'P'),
+    ('D', 0, 0, 2, 4, 'P'),
+    ('g', 1, 2, 'S'),
+    ('D', 0, 0, 3, 4, 'P'),
+    ('q2', 5, 0, 'V'),
+    ('D', 0, 0, 4, 4, 'P'),
     ('D', 0, 0, 5, 4, 'P'),
+    ('n', 1, 0, 'S'),
+    ('n', 1, 2, 'V'),
+    ('D', 0, 0, 0, 5, 'P'),
+    ('n', 1, 3, 'V'),
+    ('n', 1, 1, 'S'),
+    ('D', 0, 0, 1, 5, 'P'),
+    ('e', 1, 0, 'V'),
     ('O', 0, 0, 5, 'S'),
-    ('D', 0, 0, 5, 5, 'P'),
+    ('D', 0, 0, 2, 5, 'P'),
+    ('D', 0, 0, 3, 5, 'P'),
     ('O', 0, 0, 1, 'S'),
-    ('eq', 1, 0, 'V'),
-    ('e', 1, 2, 'V'),
-    ('O', 0, 0, 3, 'S'),
+    ('D', 0, 0, 4, 5, 'P'),
+    ('eq', 1, 0, 0, 'V'),
+    ('D', 0, 0, 5, 5, 'P'),
+    ('e', 1, 1, 'V'),
+    ('O', 0, 0, 4, 'S'),
     ('D', 1, 0, 0, 0, 'P'),
     ('D', 1, 0, 0, 1, 'P'),
-    ('W', 3, 2, 1, 'S'),
     ('D', 1, 0, 0, 2, 'P'),
-    ('D', 1, 0, 0, 3, 'P'),
-    ('O', 0, 0, 0, 'S'),
-    ('eq', 1, 1, 'V'),
-    ('D', 1, 0, 0, 4, 'P'),
-    ('e', 1, 3, 'V'),
-    ('D', 1, 0, 0, 5, 'P'),
     ('O', 0, 0, 2, 'S'),
-    ('D', 1, 0, 1, 0, 'P'),
-    ('D', 1, 0, 1, 1, 'P'),
-    ('W', 2, 3, 1, 'S'),
-    ('D', 1, 0, 1, 2, 'P'),
+    ('eq', 1, 0, 1, 'V'),
+    ('D', 1, 0, 0, 3, 'P'),
+    ('e', 1, 2, 'V'),
     ('D', 1, 0, 1, 3, 'P'),
-    ('eq', 1, 2, 'V'),
-    ('W', 4, 3, 1, 'S'),
-    ('D', 1, 0, 1, 4, 'P'),
-    ('e', 1, 4, 'V'),
     ('D', 1, 0, 1, 5, 'P'),
-    ('D', 1, 0, 2, 0, 'P'),
-    ('W', 5, 2, 1, 'S'),
-    ('D', 1, 0, 2, 1, 'P'),
+    ('D', 1, 0, 1, 4, 'P'),
+    ('eq', 1, 1, 2, 'V'),
+    ('D', 1, 0, 1, 0, 'P'),
+    ('e', 1, 3, 'V'),
     ('D', 1, 0, 2, 2, 'P'),
-    ('I2', 0, 1, 'S'),
-    ('D', 1, 0, 2, 3, 'P'),
-    ('eq', 1, 3, 'V'),
-    ('D', 1, 0, 2, 4, 'P'),
-    ('e', 1, 5, 'V'),
+    ('D', 1, 0, 2, 0, 'P'),
+    ('D', 1, 0, 2, 1, 'P'),
+    ('eq', 1, 1, 3, 'V'),
     ('D', 1, 0, 2, 5, 'P'),
-    ('D', 1, 0, 3, 0, 'P'),
-    ('D', 1, 0, 3, 1, 'P'),
-    ('D', 1, 0, 3, 2, 'P'),
-    ('D', 1, 0, 3, 3, 'P'),
-    ('eq', 1, 4, 'V'),
-    ('D', 1, 0, 3, 4, 'P'),
-    ('W', 1, 2, 1, 'V'),
+    ('e', 1, 4, 'V'),
     ('D', 1, 0, 3, 5, 'P'),
-    ('W', 3, 0, 1, 'V'),
-    ('D', 1, 0, 4, 0, 'P'),
-    ('I2', 1, 1, 'S'),
-    ('q2', 0, 1, 'V'),
+    ('D', 1, 0, 3, 4, 'P'),
+    ('D', 1, 0, 3, 3, 'P'),
+    ('eq', 1, 2, 4, 'V'),
+    ('D', 1, 0, 3, 2, 'P'),
+    ('e', 1, 5, 'V'),
     ('D', 1, 0, 4, 1, 'P'),
     ('D', 1, 0, 4, 2, 'P'),
-    ('eq', 1, 5, 'V'),
-    ('D', 1, 0, 4, 3, 'P'),
-    ('I2', 2, 1, 'V'),
+    ('D', 1, 0, 4, 0, 'P'),
+    ('eq', 1, 2, 5, 'V'),
     ('D', 1, 0, 4, 4, 'P'),
+    ('O', 0, 0, 3, 'V'),
+    ('D', 1, 0, 5, 4, 'P'),
+    ('D', 1, 0, 5, 3, 'P'),
+    ('O', 1, 0, 0, 'V'),
+    ('D', 1, 0, 5, 5, 'P'),
+    ('D', 1, 0, 5, 1, 'P'),
+    ('O', 1, 0, 2, 'S'),
+    ('D', 1, 0, 0, 4, 'P'),
+    ('O', 1, 0, 3, 'V'),
+    ('D', 1, 0, 1, 2, 'P'),
+    ('O', 0, 0, 0, 'S'),
+    ('D', 1, 0, 2, 3, 'P'),
+    ('D', 1, 0, 3, 1, 'P'),
     ('D', 1, 0, 4, 5, 'P'),
     ('D', 1, 0, 5, 0, 'P'),
-    ('D', 1, 0, 5, 1, 'P'),
-    ('D', 1, 0, 5, 2, 'P'),
+    ('D', 1, 0, 0, 5, 'P'),
     ('O', 1, 0, 4, 'V'),
-    ('D', 1, 0, 5, 3, 'P'),
-    ('O', 1, 0, 3, 'S'),
-    ('D', 1, 0, 5, 4, 'P'),
-    ('W', 5, 0, 1, 'V'),
-    ('D', 1, 0, 5, 5, 'P'),
-    ('O', 1, 0, 5, 'S'),
+    ('D', 1, 0, 1, 1, 'P'),
+    ('D', 1, 0, 2, 4, 'P'),
     ('O', 1, 0, 1, 'V'),
-    ('D', 0, 1, 0, 0, 'P'),
-    ('D', 0, 1, 1, 0, 'P'),
-    ('O', 1, 0, 2, 'S'),
-    ('q2', 1, 1, 'V'),
-    ('D', 0, 1, 2, 0, 'P'),
-    ('D', 0, 1, 3, 0, 'P'),
-    ('O', 1, 0, 0, 'S'),
-    ('D', 0, 1, 4, 0, 'P'),
-    ('I2', 3, 1, 'V'),
-    ('D', 0, 1, 5, 0, 'P'),
-    ('D', 0, 1, 0, 1, 'P'),
-    ('W', 4, 0, 1, 'S'),
-    ('D', 0, 1, 1, 1, 'P'),
-    ('D', 0, 1, 2, 1, 'P'),
-    ('q2', 2, 1, 'V'),
-    ('D', 0, 1, 3, 1, 'P'),
-    ('I2', 4, 1, 'S'),
-    ('D', 0, 1, 4, 1, 'P'),
-    ('q2', 3, 1, 'V'),
-    ('D', 0, 1, 5, 1, 'P'),
-    ('D', 0, 1, 0, 2, 'P'),
-    ('D', 0, 1, 1, 2, 'P'),
-    ('I2', 5, 1, 'V'),
-    ('D', 0, 1, 2, 2, 'P'),
-    ('D', 0, 1, 3, 2, 'P'),
-    ('D', 0, 1, 4, 2, 'P'),
-    ('D', 0, 1, 5, 2, 'P'),
-    ('D', 0, 1, 0, 3, 'P'),
-    ('D', 0, 1, 1, 3, 'P'),
-    ('q2', 4, 1, 'V'),
-    ('D', 0, 1, 2, 3, 'P'),
-    ('D', 0, 1, 3, 3, 'P'),
-    ('q2', 5, 1, 'V'),
-    ('D', 0, 1, 4, 3, 'P'),
-    ('D', 0, 1, 5, 3, 'P'),
-    ('D', 0, 1, 0, 4, 'P'),
-    ('D', 0, 1, 1, 4, 'P'),
-    ('D', 0, 1, 2, 4, 'P'),
-    ('D', 0, 1, 3, 4, 'P'),
-    ('D', 0, 1, 4, 4, 'P'),
-    ('D', 0, 1, 5, 4, 'P'),
-    ('D', 0, 1, 0, 5, 'P'),
-    ('D', 0, 1, 1, 5, 'P'),
-    ('D', 0, 1, 2, 5, 'P'),
-    ('D', 0, 1, 3, 5, 'P'),
-    ('O', 0, 1, 3, 'V'),
-    ('D', 0, 1, 4, 5, 'P'),
-    ('O', 0, 1, 0, 'S'),
-    ('D', 0, 1, 5, 5, 'P'),
-    ('O', 0, 1, 4, 'V'),
-    ('D', 1, 1, 0, 0, 'P'),
-    ('D', 1, 1, 1, 3, 'P'),
-    ('O', 0, 1, 2, 'V'),
-    ('D', 1, 1, 2, 2, 'P'),
-    ('D', 1, 1, 3, 5, 'P'),
-    ('D', 1, 1, 4, 1, 'P'),
-    ('O', 0, 1, 5, 'V'),
-    ('D', 1, 1, 5, 4, 'P'),
-    ('D', 1, 1, 0, 1, 'P'),
-    ('O', 0, 1, 1, 'V'),
-    ('O', 1, 1, 0, 'S'),
-    ('D', 1, 1, 1, 5, 'P'),
-    ('D', 1, 1, 2, 0, 'P'),
-    ('D', 1, 1, 3, 4, 'P'),
-    ('D', 1, 1, 4, 2, 'P'),
-    ('D', 1, 1, 5, 3, 'P'),
-    ('D', 1, 1, 0, 2, 'P'),
-    ('O', 1, 1, 1, 'V'),
-    ('D', 1, 1, 1, 4, 'P'),
-    ('D', 1, 1, 2, 1, 'P'),
-    ('D', 1, 1, 3, 3, 'P'),
-    ('D', 1, 1, 4, 0, 'P'),
-    ('D', 1, 1, 5, 5, 'P'),
-    ('D', 1, 1, 0, 3, 'P'),
-    ('O', 1, 1, 2, 'V'),
-    ('D', 1, 1, 1, 0, 'P'),
-    ('D', 1, 1, 2, 5, 'P'),
-    ('D', 1, 1, 3, 2, 'P'),
-    ('D', 1, 1, 4, 4, 'P'),
-    ('D', 1, 1, 5, 1, 'P'),
-    ('D', 1, 1, 0, 4, 'P'),
-    ('O', 1, 1, 3, 'V'),
-    ('D', 1, 1, 1, 2, 'P'),
-    ('D', 1, 1, 2, 3, 'P'),
-    ('D', 1, 1, 3, 1, 'P'),
-    ('D', 1, 1, 4, 5, 'P'),
-    ('D', 1, 1, 5, 0, 'P'),
-    ('D', 1, 1, 0, 5, 'P'),
-    ('O', 1, 1, 4, 'V'),
-    ('D', 1, 1, 1, 1, 'P'),
-    ('D', 1, 1, 2, 4, 'P'),
-    ('D', 1, 1, 3, 0, 'P'),
-    ('D', 1, 1, 4, 3, 'P'),
-    ('D', 1, 1, 5, 2, 'P'),
-    ('O', 1, 1, 5, 'V'),
+    ('D', 1, 0, 3, 0, 'P'),
+    ('D', 1, 0, 4, 3, 'P'),
+    ('D', 1, 0, 5, 2, 'P'),
+    ('O', 1, 0, 5, 'S'),
 )
 
 P = 128
@@ -594,6 +425,7 @@ F32 = mybir.dt.float32
 BF16 = mybir.dt.bfloat16
 U32 = mybir.dt.uint32
 U8 = mybir.dt.uint8
+I32 = mybir.dt.int32
 FP8X4 = mybir.dt.float8_e4m3fn_x4
 FP8 = mybir.dt.float8_e4m3fn
 ACT = mybir.ActivationFunctionType
@@ -617,6 +449,8 @@ def tile_dihedralthreegroupblock_kernel(tc, x, w1, b1, ls, w2_bytes, w2_scale, o
         nc.scalar.dma_start(out=sc_sb[:], in_=w2_scale.rearrange("o (p t) z -> p (o t z)", t=4))
         nc.scalar.dma_start(out=b1_sb[:], in_=b1.rearrange("(p t) -> p t", t=4))
         nc.scalar.dma_start(out=ls_sb[:], in_=ls.rearrange("(p t) -> p t", t=4))
+        ls32 = keep.tile([P, 4], F32, name="ls32")
+        nc.gpsimd.tensor_copy(out=ls32[:], in_=ls_sb[:])
 
         xs = {}
         w1_raw = {}
@@ -625,7 +459,8 @@ def tile_dihedralthreegroupblock_kernel(tc, x, w1, b1, ls, w2_bytes, w2_scale, o
             if load[0] == "x":
                 a, b = load[1:]
                 t = keep.tile([P, 2, C], BF16, name="xs%d_%d" % (a, b), align_bytes=64)
-                nc.sync.dma_start(out=t[:], in_=x[a * P : (a + 1) * P, 2 * b : 2 * b + 2, :])
+                h0, h1 = PAIRS[b]
+                nc.sync.dma_start(out=t[:], in_=x[a * P : (a + 1) * P, h0 : h1 + 1 : h1 - h0, :])
                 xs[a, b] = t
             elif load[0] == "w1":
                 j = load[1]
@@ -634,9 +469,9 @@ def tile_dihedralthreegroupblock_kernel(tc, x, w1, b1, ls, w2_bytes, w2_scale, o
                 w1_raw[j] = t
             else:
                 j = load[1]
-                t = keep.tile([P, 4, C], U8, name="w2_raw%d" % j, align_bytes=64)
-                nc.sync.dma_start(out=t[:], in_=w2_bytes[j].rearrange("(p t) d -> p t d", t=4))
-                w2_raw[j] = t
+                if j % 2 == 0:
+                    w2_raw[j // 2] = keep.tile([P, 4, 2, C], U8, name="w2_raw%d" % (j // 2), align_bytes=64)
+                nc.sync.dma_start(out=w2_raw[j // 2][:, :, j % 2, :], in_=w2_bytes[j].rearrange("(p t) d -> p t d", t=4))
 
         ident = keep.tile([P, P], F32, name="ident")
         make_identity(nc, ident[:])
@@ -644,8 +479,9 @@ def tile_dihedralthreegroupblock_kernel(tc, x, w1, b1, ls, w2_bytes, w2_scale, o
         nc.gpsimd.memset(warm[:], 0.0)
         nc.scalar.activation(out=warm[:], in_=warm[:], func=ACT.Sigmoid)
 
-        xc = [keep.tile([P, 2, 3, P], U32, name="xc%d" % i, align_bytes=64) for i in range(3)]
-        xsc = [keep.tile([P, 2, 3, P], U8, name="xsc%d" % i, align_bytes=64) for i in range(3)]
+        xc = [keep.tile([P, 3, 3, P], U32, name="xc%d" % a, align_bytes=64) for a in range(2)]
+        xsc = [keep.tile([P, 3, 3, P], U8, name="xsc%d" % a, align_bytes=64) for a in range(2)]
+        nc.gpsimd.memset(xsc[1][:].rearrange("p q s n -> p (q s n)").bitcast(I32), 0)
         w1c = [keep.tile([P, C], U32, name="w1c%d" % j, align_bytes=64) for j in range(G)]
         w1s = [keep.tile([P, C], U8, name="w1s%d" % j, align_bytes=64) for j in range(G)]
         w2c = [keep.tile([P, C], U32, name="w2c%d" % j, align_bytes=64) for j in range(G)]
@@ -682,28 +518,33 @@ def tile_dihedralthreegroupblock_kernel(tc, x, w1, b1, ls, w2_bytes, w2_scale, o
                 tb[a, b][:].rearrange("p i u r -> p i r u"),
             )
 
-        def x_quant(a, h, dup):
-            q = [i for i in range(3) if h in PAIRS[i]][0]
-            slot = 2 if dup else PAIRS[q].index(h)
-            nc.vector.quantize_mx(
-                out=xc[q][:, a, slot, :].bitcast(FP8X4),
-                scales=xsc[q][:, a, slot, :],
-                in_=xg[a, h // 2][:, h % 2].rearrange("p n t -> p (n t)"),
-            )
+        def x_quant(a, b, dup):
+            if not dup:
+                nc.vector.quantize_mx(
+                    out=xc[a][:, b, 0:2, :].rearrange("p s n -> p (s n)").bitcast(FP8X4),
+                    scales=xsc[a][:, b, 0:2, :].rearrange("p s n -> p (s n)"),
+                    in_=xg[a, b][:].rearrange("p i n t -> p (i n t)"),
+                )
+            elif b < 3:
+                nc.vector.quantize_mx(
+                    out=xc[a][:, b, 2, :].bitcast(FP8X4),
+                    scales=xsc[a][:, b, 2, :],
+                    in_=xg[a, b][:, 0].rearrange("p n t -> p (n t)"),
+                )
+            else:
+                nc.vector.tensor_copy(out=xc[a][:, :, 2, :].bitcast(I32), in_=xc[a][:, :, 0, :].bitcast(I32))
+                nc.vector.tensor_copy(out=xsc[a][:, :, 2, :].bitcast(I32), in_=xsc[a][:, :, 0, :].bitcast(I32))
 
         wg = {}
 
         def w1_inter(j, th, eng):
-            g = work.tile([P, 2, P, 4], BF16, name="wg", align_bytes=64, bufs=8)
-            copy(
-                eng,
-                g[:],
-                w1_raw[j][:].rearrange("p j (m t) -> p t m j", t=4)[:, 2 * th : 2 * th + 2],
-            )
+            t0, t1 = (0, 4) if th == 2 else (2 * th, 2 * th + 2)
+            g = work.tile([P, t1 - t0, P, 4], BF16, name="wg", align_bytes=64, bufs=8)
+            copy(eng, g[:], w1_raw[j][:].rearrange("p j (m t) -> p t m j", t=4)[:, t0:t1])
             wg[j, th] = g
 
         def w1_quant(j, th):
-            cols = slice(2 * th * P, 2 * (th + 1) * P)
+            cols = slice(0, C) if th == 2 else slice(2 * th * P, 2 * (th + 1) * P)
             nc.vector.quantize_mx(
                 out=w1c[j][:, cols].bitcast(FP8X4),
                 scales=w1s[j][:, cols],
@@ -713,30 +554,27 @@ def tile_dihedralthreegroupblock_kernel(tc, x, w1, b1, ls, w2_bytes, w2_scale, o
         wide = {}
         grp = {}
 
-        def w2_widen(j, t, dh, eng):
-            if (j, dh) not in wide:
-                wide[j, dh] = work.tile([P, 4, C // 2], BF16, name="wide", align_bytes=64, bufs=12)
-            src = w2_raw[j][:, t, dh * C // 2 : (dh + 1) * C // 2].bitcast(FP8)
-            dst = wide[j, dh][:, t, :]
+        def w2_widen(b, t, eng):
+            if b not in wide:
+                wide[b] = work.tile([P, 4, 2, C], BF16, name="wide", align_bytes=64, bufs=3)
+            src = w2_raw[b][:, t].rearrange("p j d -> p (j d)").bitcast(FP8)
+            dst = wide[b][:, t].rearrange("p j d -> p (j d)")
             if eng == "S":
                 nc.scalar.activation(out=dst, in_=src, func=ACT.Copy, scale=sc_sb[:, t : t + 1])
             else:
                 nc.vector.tensor_scalar(out=dst, in0=src, scalar1=sc_sb[:, t : t + 1], scalar2=None, op0=ALU.mult)
 
-        def w2_inter(j, dh, eng):
-            grp[j, dh] = work.tile([P, C // 2, 4], BF16, name="grp", align_bytes=64, bufs=12)
+        def w2_inter(j, eng):
+            grp[j] = work.tile([P, C, 4], BF16, name="grp", align_bytes=64, bufs=6)
             copy(
                 eng,
-                grp[j, dh][:].rearrange("p (c i) t -> p c t i", i=4),
-                wide[j, dh][:].rearrange("p t (c i) -> p c t i", i=4),
+                grp[j][:].rearrange("p (c i) t -> p c t i", i=4),
+                wide[j // 2][:, :, j % 2, :].rearrange("p t (c i) -> p c t i", i=4),
             )
 
-        def w2_quant(j, dh):
-            cols = slice(dh * C // 2, (dh + 1) * C // 2)
+        def w2_quant(j):
             nc.vector.quantize_mx(
-                out=w2c[j][:, cols].bitcast(FP8X4),
-                scales=w2s[j][:, cols],
-                in_=grp[j, dh][:].rearrange("p n t -> p (n t)"),
+                out=w2c[j][:].bitcast(FP8X4), scales=w2s[j][:], in_=grp[j][:].rearrange("p n t -> p (n t)")
             )
 
         def window(gp, j):
@@ -752,11 +590,11 @@ def tile_dihedralthreegroupblock_kernel(tc, x, w1, b1, ls, w2_bytes, w2_scale, o
             q, s0 = window(gp, j)
             cols = slice(t * P, (t + 1) * P)
             nc.tensor.matmul_mx(
-                out=acc[:],
+                out=acc,
                 lhsT=w1c[j][:, cols].bitcast(FP8X4),
                 lhsT_scale=w1s[j][:, cols],
-                rhs=xc[q][:, a, s0 : s0 + 2, :].rearrange("p s n -> p (s n)").bitcast(FP8X4),
-                rhs_scale=xsc[q][:, a, s0 : s0 + 2, :].rearrange("p s n -> p (s n)"),
+                rhs=xc[a][:, q, s0 : s0 + 2, :].rearrange("p s n -> p (s n)").bitcast(FP8X4),
+                rhs_scale=xsc[a][:, q, s0 : s0 + 2, :].rearrange("p s n -> p (s n)"),
                 start=first,
                 stop=last,
             )
@@ -779,54 +617,56 @@ def tile_dihedralthreegroupblock_kernel(tc, x, w1, b1, ls, w2_bytes, w2_scale, o
         def gate(a, tt):
             nc.scalar.activation(out=s_sb[:, a, tt], in_=m_sb[:, a, tt], func=ACT.Sigmoid)
 
-        def gain(a, t):
-            nc.vector.tensor_scalar(
-                out=s_sb[:, a, t], in0=s_sb[:, a, t], scalar1=ls_sb[:, t : t + 1], scalar2=None, op0=ALU.mult
-            )
+        def gain(a, t, eng):
+            if eng == "S":
+                nc.scalar.activation(out=s_sb[:, a, t], in_=s_sb[:, a, t], func=ACT.Copy, scale=ls32[:, t : t + 1])
+            else:
+                nc.vector.tensor_scalar(
+                    out=s_sb[:, a, t], in0=s_sb[:, a, t], scalar1=ls32[:, t : t + 1], scalar2=None, op0=ALU.mult
+                )
 
         def e_mult(a, pos):
             if (a, pos // 2) not in eg:
                 eg[a, pos // 2] = keep.tile([P, 2, P, 4], BF16, name="eg", tag="xg", align_bytes=64, bufs=6)
             nc.vector.tensor_tensor(
-                out=eg[a, pos // 2][:, pos % 2].rearrange("p (c i) t -> p c t i", i=4),
-                in0=y_sb[:, a, :, pos, :].rearrange("p t (c i) -> p c t i", i=4),
-                in1=s_sb[:, a].rearrange("p t (c i) -> p c t i", i=4),
+                out=eg[a, pos // 2][:, pos % 2].rearrange("p (c i) t -> p c t i", i=2),
+                in0=y_sb[:, a, :, pos, :].rearrange("p t (c i) -> p c t i", i=2),
+                in1=s_sb[:, a].rearrange("p t (c i) -> p c t i", i=2),
                 op=ALU.mult,
             )
 
-        def e_quant(a, pos):
+        def e_quant(a, q, i0, i1):
             nc.vector.quantize_mx(
-                out=ec[a][pos // 2][:, pos % 2, :].bitcast(FP8X4),
-                scales=es[a][pos // 2][:, pos % 2, :],
-                in_=eg[a, pos // 2][:, pos % 2].rearrange("p n t -> p (n t)"),
+                out=ec[a][q][:, i0:i1, :].rearrange("p s n -> p (s n)").bitcast(FP8X4),
+                scales=es[a][q][:, i0:i1, :].rearrange("p s n -> p (s n)"),
+                in_=eg[a, q][:, i0:i1].rearrange("p s n t -> p (s n t)"),
             )
 
-        def conv2(acc, a, dh, h, j, first, last):
+        def conv2(acc, a, h, j, first, last):
             i = POS.index(h)
-            cols = slice(dh * C // 2, (dh + 1) * C // 2)
             nc.tensor.matmul_mx(
-                out=acc[:],
+                out=acc,
                 lhsT=ec[a][i // 2][:, i % 2, :].bitcast(FP8X4),
                 lhsT_scale=es[a][i // 2][:, i % 2, :],
-                rhs=w2c[j][:, cols].bitcast(FP8X4),
-                rhs_scale=w2s[j][:, cols],
+                rhs=w2c[j][:].bitcast(FP8X4),
+                rhs_scale=w2s[j][:],
                 start=first,
                 stop=last,
             )
 
-        def store(acc, a, dh, g, eng):
-            o = work.tile([P, C // 2], F32, name="o_sb", bufs=8)
+        def store(acc, a, g, eng):
+            o = work.tile([P, C], F32, name="o_sb", bufs=6)
             copy(eng, o[:], acc[:])
-            nc.sync.dma_start(out=out[a * P : (a + 1) * P, g, dh * C // 2 : (dh + 1) * C // 2], in_=o[:])
+            nc.sync.dma_start(out=out[a * P : (a + 1) * P, g, :], in_=o[:])
 
-        accs = {}
+        banks = {}
         count = {}
 
-        def group(key):
-            if key not in accs:
-                accs[key] = bank([P, 2 * P], SLOTS[key])
+        def group(key, bank_key, c0, c1):
+            if bank_key not in banks:
+                banks[bank_key] = bank([P, C], SLOTS[bank_key])
             count[key] = count.get(key, 0) + 1
-            return accs[key], count[key] == 1, count[key] == G
+            return banks[bank_key][:, c0:c1], count[key] == 1, count[key] == G
 
         for step in PROGRAM:
             kind, arg, eng = step[0], step[1:-1], step[-1]
@@ -841,35 +681,45 @@ def tile_dihedralthreegroupblock_kernel(tc, x, w1, b1, ls, w2_bytes, w2_scale, o
             elif kind == "q":
                 w1_quant(arg[0], arg[1])
             elif kind == "W":
-                w2_widen(arg[0], arg[1], arg[2], eng)
+                w2_widen(arg[0], arg[1], eng)
             elif kind == "I2":
-                w2_inter(arg[0], arg[1], eng)
+                w2_inter(arg[0], eng)
             elif kind == "q2":
-                w2_quant(arg[0], arg[1])
+                w2_quant(arg[0])
             elif kind == "A":
                 a, t, gp, j = arg
-                acc, first, last = group(("A", a, t, gp))
+                if (a, t) in YMERGE and gp < 2:
+                    acc, first, last = group(step[:4], ("A", a, t, 0), 256 * gp, 256 * gp + 256)
+                else:
+                    acc, first, last = group(step[:4], step[:4], 0, 256)
                 conv1(acc, a, t, gp, j, first, last)
             elif kind == "Y":
                 a, t, gp = arg
+                w = 2 if (a, t) in YMERGE and gp == 0 else 1
                 y_evac(
-                    y_sb[:, a, t, 2 * gp : 2 * gp + 2, :].rearrange("p g n -> p (g n)"), accs["A", a, t, gp][:], t, eng
+                    y_sb[:, a, t, 2 * gp : 2 * gp + 2 * w, :].rearrange("p g n -> p (g n)"),
+                    banks["A", a, t, gp][:, 0 : 256 * w],
+                    t,
+                    eng,
                 )
             elif kind in ("M0", "M1", "M2", "g"):
                 f = {"M0": pool_max0, "M1": pool_max1, "M2": pool_max2, "g": gate}[kind]
-                f(arg[0], slice(2 * arg[1], 2 * arg[1] + 2))
+                f(arg[0], slice(0, 4) if arg[1] == 2 else slice(2 * arg[1], 2 * arg[1] + 2))
             elif kind == "n":
-                gain(arg[0], arg[1])
+                gain(arg[0], arg[1], eng)
             elif kind == "e":
                 e_mult(arg[0], arg[1])
             elif kind == "eq":
-                e_quant(arg[0], arg[1])
+                if len(arg) == 2:
+                    e_quant(arg[0], arg[1], 0, 2)
+                else:
+                    e_quant(arg[0], arg[1], arg[2] % 2, arg[2] % 2 + 1)
             elif kind == "D":
                 a, dh, pos, j = arg
                 h = POS[pos]
                 g = [gg for gg in range(G) if K[h][gg] == j][0]
-                acc, first, last = group(("D", a, dh, g))
-                conv2(acc, a, dh, h, j, first, last)
+                acc, first, last = group(("D", a, dh, g), ("D", a, dh, g), 0, C)
+                conv2(acc, a, h, j, first, last)
             elif kind == "O":
                 a, dh, g = arg
-                store(accs["D", a, dh, g], a, dh, g, eng)
+                store(banks["D", a, dh, g], a, g, eng)

@@ -19,413 +19,448 @@ POS = (0, 3, 1, 5, 2, 4)
 
 YMERGE = ((0, 2), (0, 3), (1, 1), (1, 2), (1, 3))
 
-LOADS = (('x', 0, 0), ('x', 0, 1), ('x', 0, 2), ('w1', 0), ('w1', 1), ('x', 1, 0), ('x', 1, 1), ('x', 1, 2), ('w1', 2), ('w1', 3), ('w1', 4), ('w1', 5), ('w2', 0), ('w2', 1), ('w2', 2), ('w2', 3), ('w2', 4), ('w2', 5))
+LOADS = (('w1', 0), ('x', 0, 0), ('x', 0, 1), ('x', 0, 2), ('w1', 1), ('x', 1, 0), ('x', 1, 1), ('x', 1, 2), ('w1', 2), ('w1', 3), ('w1', 4), ('w1', 5), ('w2', 0), ('w2', 1), ('w2', 2), ('w2', 3), ('w2', 4), ('w2', 5))
 
 SLOTS = {
-    ('T', 0, 0): 0,
-    ('T', 0, 1): 1,
-    ('T', 0, 2): 2,
-    ('A', 0, 0, 0): 3,
-    ('A', 0, 1, 0): 4,
-    ('A', 0, 0, 1): 5,
-    ('A', 0, 1, 1): 6,
-    ('A', 0, 0, 2): 7,
-    ('A', 0, 1, 2): 0,
-    ('T', 1, 0): 1,
-    ('T', 1, 1): 2,
-    ('T', 1, 2): 1,
-    ('A', 1, 0, 0): 2,
-    ('A', 1, 0, 1): 1,
-    ('A', 0, 2, 0): 3,
-    ('A', 0, 2, 2): 4,
-    ('A', 0, 3, 0): 5,
-    ('A', 0, 3, 2): 6,
-    ('A', 1, 0, 2): 7,
-    ('A', 1, 1, 0): 0,
-    ('A', 1, 1, 2): 2,
-    ('A', 1, 2, 0): 1,
-    ('A', 1, 2, 2): 3,
-    ('A', 1, 3, 0): 4,
-    ('A', 1, 3, 2): 5,
-    ('D', 0, 0, 0): 6,
-    ('D', 0, 0, 1): 7,
-    ('D', 0, 0, 3): 0,
-    ('D', 0, 0, 5): 2,
-    ('D', 0, 0, 2): 1,
-    ('D', 0, 0, 4): 3,
-    ('D', 1, 0, 0): 4,
-    ('D', 1, 0, 1): 5,
-    ('D', 1, 0, 2): 2,
-    ('D', 1, 0, 3): 7,
-    ('D', 1, 0, 4): 0,
-    ('D', 1, 0, 5): 6,
+    ('Z',): 0,
+    ('T', 0, 0): 1,
+    ('T', 0, 1): 2,
+    ('T', 0, 2): 3,
+    ('A', 0, 0, 0): 4,
+    ('A', 0, 1, 0): 5,
+    ('A', 0, 0, 1): 6,
+    ('A', 0, 1, 1): 7,
+    ('A', 0, 0, 2): 1,
+    ('A', 0, 1, 2): 2,
+    ('T', 1, 0): 3,
+    ('T', 1, 1): 0,
+    ('T', 1, 2): 3,
+    ('A', 1, 0, 0): 0,
+    ('A', 1, 0, 1): 3,
+    ('A', 0, 2, 0): 4,
+    ('A', 0, 2, 2): 5,
+    ('A', 0, 3, 0): 6,
+    ('A', 0, 3, 2): 7,
+    ('A', 1, 0, 2): 1,
+    ('A', 1, 1, 0): 2,
+    ('A', 1, 1, 2): 0,
+    ('A', 1, 2, 0): 3,
+    ('A', 1, 2, 2): 4,
+    ('A', 1, 3, 0): 5,
+    ('A', 1, 3, 2): 6,
+    ('D', 0, 0, 0): 7,
+    ('D', 0, 0, 1): 1,
+    ('D', 0, 0, 3): 2,
+    ('D', 0, 0, 5): 0,
+    ('D', 0, 0, 2): 3,
+    ('D', 0, 0, 4): 4,
+    ('D', 1, 0, 0): 5,
+    ('D', 1, 0, 1): 6,
+    ('D', 1, 0, 2): 0,
+    ('D', 1, 0, 3): 1,
+    ('D', 1, 0, 4): 2,
+    ('D', 1, 1, 5): 7,
+    ('D', 1, 2, 5): 4,
 }
 
 PROGRAM = (
+    ('Z', 0, 'P'),
+    ('Z', 1, 'P'),
+    ('Z', 2, 'P'),
+    ('Z', 3, 'P'),
+    ('Z', 4, 'P'),
+    ('Z', 5, 'P'),
+    ('Z', 6, 'P'),
+    ('Z', 7, 'P'),
+    ('I', 0, 0, 'V'),
+    ('I', 0, 1, 'S'),
     ('T', 0, 0, 'P'),
     ('T', 0, 1, 'P'),
     ('E', 0, 0, 'S'),
     ('T', 0, 2, 'P'),
     ('E', 0, 1, 'S'),
-    ('Q', 0, 0, 0, 'V'),
-    ('Q', 0, 0, 1, 'V'),
-    ('E', 0, 2, 'S'),
     ('Q', 0, 1, 0, 'V'),
-    ('I', 0, 0, 'V'),
-    ('I', 0, 1, 'S'),
+    ('Q', 0, 0, 0, 'V'),
+    ('Z', 8, 'P'),
     ('q', 0, 0, 'V'),
+    ('E', 0, 2, 'S'),
+    ('Q', 0, 3, 0, 'V'),
     ('Q', 0, 1, 1, 'V'),
     ('A', 0, 0, 0, 0, 'P'),
-    ('I', 1, 0, 'S'),
     ('Q', 0, 2, 0, 'V'),
+    ('I', 1, 1, 'S'),
     ('A', 0, 1, 0, 0, 'P'),
+    ('Q', 0, 5, 0, 'V'),
+    ('Q', 0, 4, 0, 'V'),
     ('A', 0, 0, 1, 0, 'P'),
-    ('Q', 0, 2, 1, 'V'),
+    ('I', 1, 0, 'V'),
     ('A', 0, 1, 1, 0, 'P'),
-    ('I', 1, 1, 'V'),
     ('A', 0, 0, 2, 0, 'P'),
     ('A', 0, 1, 2, 0, 'P'),
     ('T', 1, 0, 'P'),
+    ('Q', 0, 2, 1, 'V'),
+    ('q', 1, 0, 'V'),
     ('q', 0, 1, 'V'),
     ('E', 1, 0, 'S'),
-    ('q', 1, 0, 'V'),
-    ('q', 1, 1, 'V'),
     ('A', 0, 0, 0, 1, 'P'),
-    ('Q', 1, 0, 0, 'V'),
+    ('q', 1, 1, 'V'),
     ('A', 0, 1, 0, 1, 'P'),
     ('A', 0, 0, 1, 1, 'P'),
-    ('I', 2, 1, 'S'),
+    ('Q', 0, 0, 1, 'V'),
     ('A', 0, 1, 1, 1, 'P'),
-    ('I', 2, 0, 'V'),
+    ('Q', 1, 0, 1, 'V'),
     ('A', 0, 0, 2, 1, 'P'),
     ('A', 0, 1, 2, 1, 'P'),
-    ('T', 1, 1, 'P'),
-    ('q', 2, 0, 'V'),
-    ('T', 1, 2, 'P'),
-    ('E', 1, 1, 'S'),
-    ('I', 3, 0, 'V'),
-    ('A', 0, 0, 0, 2, 'P'),
-    ('A', 0, 1, 0, 2, 'P'),
-    ('E', 1, 2, 'S'),
-    ('A', 0, 0, 1, 2, 'P'),
     ('Q', 1, 1, 0, 'V'),
-    ('A', 0, 1, 1, 2, 'P'),
-    ('A', 0, 0, 2, 2, 'P'),
+    ('T', 1, 1, 'P'),
+    ('I', 2, 0, 'S'),
+    ('I', 2, 1, 'V'),
+    ('T', 1, 2, 'P'),
+    ('Q', 1, 0, 0, 'V'),
+    ('q', 2, 1, 'V'),
+    ('I', 3, 0, 'V'),
+    ('E', 1, 1, 'S'),
+    ('E', 1, 2, 'S'),
+    ('q', 2, 0, 'V'),
     ('q', 3, 0, 'V'),
-    ('A', 0, 1, 2, 2, 'P'),
-    ('I', 3, 1, 'S'),
+    ('A', 0, 0, 0, 2, 'P'),
+    ('I', 4, 0, 'S'),
+    ('Q', 1, 3, 0, 'V'),
+    ('A', 0, 1, 0, 2, 'P'),
+    ('Q', 1, 1, 1, 'V'),
+    ('A', 0, 0, 1, 2, 'P'),
+    ('Q', 1, 5, 0, 'V'),
+    ('A', 0, 1, 1, 2, 'P'),
     ('Q', 1, 2, 0, 'V'),
-    ('A', 0, 0, 0, 3, 'P'),
-    ('A', 0, 1, 0, 3, 'P'),
-    ('I', 4, 0, 'V'),
-    ('A', 0, 0, 1, 3, 'P'),
-    ('A', 0, 1, 1, 3, 'P'),
-    ('A', 0, 0, 2, 3, 'P'),
-    ('A', 0, 1, 2, 3, 'P'),
+    ('A', 0, 0, 2, 2, 'P'),
+    ('A', 0, 1, 2, 2, 'P'),
+    ('Q', 1, 4, 0, 'V'),
     ('A', 1, 0, 0, 0, 'P'),
-    ('Q', 1, 9, 1, 'V'),
-    ('I', 5, 0, 'S'),
+    ('I', 4, 1, 'V'),
     ('A', 1, 0, 1, 0, 'P'),
     ('A', 1, 0, 0, 1, 'P'),
     ('A', 1, 0, 1, 1, 'P'),
-    ('q', 4, 0, 'V'),
+    ('I', 5, 1, 'S'),
     ('A', 1, 0, 0, 2, 'P'),
+    ('Q', 1, 2, 1, 'V'),
     ('A', 1, 0, 1, 2, 'P'),
+    ('A', 0, 0, 0, 3, 'P'),
+    ('I', 5, 0, 'V'),
+    ('A', 0, 1, 0, 3, 'P'),
+    ('A', 0, 0, 1, 3, 'P'),
+    ('A', 0, 1, 1, 3, 'P'),
+    ('A', 0, 0, 2, 3, 'P'),
+    ('q', 4, 0, 'V'),
+    ('A', 0, 1, 2, 3, 'P'),
     ('A', 1, 0, 0, 3, 'P'),
-    ('I', 5, 1, 'V'),
+    ('W', 0, 2, 'S'),
     ('A', 1, 0, 1, 3, 'P'),
+    ('q', 5, 0, 'V'),
     ('A', 0, 0, 0, 4, 'P'),
     ('A', 0, 1, 0, 4, 'P'),
+    ('q', 4, 1, 'V'),
     ('A', 0, 0, 1, 4, 'P'),
-    ('W', 0, 1, 'S'),
     ('A', 0, 1, 1, 4, 'P'),
-    ('q', 5, 0, 'V'),
+    ('I', 3, 1, 'V'),
     ('A', 0, 0, 2, 4, 'P'),
     ('A', 0, 1, 2, 4, 'P'),
-    ('q', 3, 1, 'V'),
     ('A', 1, 0, 0, 4, 'P'),
+    ('W', 0, 3, 'S'),
     ('A', 1, 0, 1, 4, 'P'),
     ('A', 0, 0, 0, 5, 'P'),
-    ('q', 2, 1, 'V'),
+    ('q', 5, 1, 'V'),
     ('A', 0, 1, 0, 5, 'P'),
     ('A', 0, 0, 1, 5, 'P'),
-    ('Y', 0, 0, 0, 'S'),
-    ('I', 4, 1, 'V'),
+    ('Y', 0, 0, 0, 'V'),
     ('A', 0, 1, 1, 5, 'P'),
     ('A', 0, 0, 2, 5, 'P'),
-    ('Y', 0, 0, 1, 'S'),
+    ('q', 3, 1, 'V'),
     ('A', 0, 1, 2, 5, 'P'),
     ('A', 1, 0, 0, 5, 'P'),
+    ('W', 1, 3, 'S'),
+    ('Y', 0, 1, 1, 'V'),
     ('A', 1, 0, 1, 5, 'P'),
-    ('W', 0, 0, 'S'),
     ('A', 0, 2, 0, 0, 'P'),
-    ('q', 5, 1, 'V'),
+    ('W', 0, 1, 'V'),
     ('A', 0, 2, 0, 1, 'P'),
     ('A', 0, 2, 0, 2, 'P'),
-    ('q', 4, 1, 'V'),
     ('A', 0, 2, 0, 3, 'P'),
-    ('W', 1, 3, 'V'),
     ('A', 0, 2, 0, 4, 'P'),
+    ('W', 2, 2, 'V'),
     ('A', 0, 2, 0, 5, 'P'),
-    ('Y', 0, 1, 1, 'S'),
     ('A', 0, 2, 1, 0, 'P'),
+    ('Y', 0, 0, 2, 'S'),
     ('A', 0, 2, 1, 1, 'P'),
-    ('Y', 0, 1, 0, 'V'),
-    ('W', 1, 1, 'S'),
     ('A', 0, 2, 1, 2, 'P'),
+    ('Y', 0, 1, 0, 'S'),
+    ('Y', 0, 0, 1, 'V'),
     ('A', 0, 2, 1, 3, 'P'),
-    ('W', 1, 0, 'V'),
     ('A', 0, 2, 1, 4, 'P'),
+    ('Y', 1, 0, 0, 'S'),
+    ('W', 1, 1, 'V'),
     ('A', 0, 2, 1, 5, 'P'),
     ('A', 0, 2, 2, 0, 'P'),
+    ('Y', 0, 1, 2, 'S'),
     ('A', 0, 2, 2, 1, 'P'),
     ('A', 0, 2, 2, 2, 'P'),
-    ('Y', 0, 1, 2, 'V'),
+    ('Y', 0, 2, 0, 'S'),
+    ('W', 0, 0, 'V'),
     ('A', 0, 2, 2, 3, 'P'),
     ('A', 0, 2, 2, 4, 'P'),
-    ('Y', 0, 0, 2, 'S'),
-    ('W', 0, 2, 'V'),
     ('A', 0, 2, 2, 5, 'P'),
     ('A', 0, 3, 0, 0, 'P'),
-    ('Y', 0, 2, 0, 'S'),
+    ('Y', 1, 0, 1, 'S'),
+    ('Y', 0, 2, 2, 'V'),
     ('A', 0, 3, 0, 1, 'P'),
     ('A', 0, 3, 0, 2, 'P'),
+    ('I2', 1, 0, 'S'),
+    ('M0', 0, 0, 'V'),
     ('A', 0, 3, 0, 3, 'P'),
-    ('W', 0, 3, 'V'),
     ('A', 0, 3, 0, 4, 'P'),
-    ('Y', 0, 2, 2, 'S'),
     ('A', 0, 3, 0, 5, 'P'),
     ('A', 0, 3, 1, 0, 'P'),
     ('A', 0, 3, 1, 1, 'P'),
-    ('W', 1, 2, 'S'),
-    ('M0', 0, 0, 'V'),
     ('A', 0, 3, 1, 2, 'P'),
+    ('I2', 0, 0, 'V'),
     ('A', 0, 3, 1, 3, 'P'),
     ('A', 0, 3, 1, 4, 'P'),
     ('A', 0, 3, 1, 5, 'P'),
     ('A', 0, 3, 2, 0, 'P'),
     ('A', 0, 3, 2, 1, 'P'),
-    ('Y', 1, 0, 0, 'V'),
     ('A', 0, 3, 2, 2, 'P'),
     ('A', 0, 3, 2, 3, 'P'),
-    ('Y', 0, 3, 0, 'S'),
     ('A', 0, 3, 2, 4, 'P'),
-    ('I2', 0, 0, 'V'),
     ('A', 0, 3, 2, 5, 'P'),
     ('A', 1, 0, 2, 0, 'P'),
+    ('M1', 0, 0, 'V'),
     ('A', 1, 0, 2, 1, 'P'),
-    ('Y', 1, 0, 1, 'S'),
     ('A', 1, 0, 2, 2, 'P'),
+    ('Y', 0, 3, 2, 'V'),
+    ('Y', 0, 3, 0, 'S'),
     ('A', 1, 0, 2, 3, 'P'),
     ('A', 1, 0, 2, 4, 'P'),
-    ('Y', 0, 3, 2, 'S'),
+    ('M2', 0, 0, 'V'),
     ('A', 1, 0, 2, 5, 'P'),
     ('A', 1, 1, 0, 0, 'P'),
-    ('I2', 2, 0, 'S'),
+    ('W', 1, 0, 'V'),
+    ('W', 1, 2, 'S'),
     ('A', 1, 1, 0, 1, 'P'),
-    ('M0', 0, 1, 'V'),
     ('A', 1, 1, 0, 2, 'P'),
     ('A', 1, 1, 0, 3, 'P'),
     ('A', 1, 1, 0, 4, 'P'),
+    ('W', 2, 3, 'V'),
     ('A', 1, 1, 0, 5, 'P'),
     ('A', 1, 1, 1, 0, 'P'),
     ('A', 1, 1, 1, 1, 'P'),
     ('A', 1, 1, 1, 2, 'P'),
-    ('q2', 0, 0, 'V'),
+    ('M0', 0, 1, 'V'),
+    ('g', 0, 0, 'S'),
     ('A', 1, 1, 1, 3, 'P'),
     ('A', 1, 1, 1, 4, 'P'),
     ('A', 1, 1, 1, 5, 'P'),
+    ('I2', 2, 0, 'S'),
     ('A', 1, 1, 2, 0, 'P'),
-    ('M1', 0, 2, 'V'),
     ('A', 1, 1, 2, 1, 'P'),
     ('A', 1, 1, 2, 2, 'P'),
+    ('W', 2, 0, 'V'),
     ('A', 1, 1, 2, 3, 'P'),
     ('A', 1, 1, 2, 4, 'P'),
     ('A', 1, 1, 2, 5, 'P'),
     ('A', 1, 2, 0, 0, 'P'),
-    ('M2', 0, 2, 'V'),
+    ('n', 0, 0, 'V'),
+    ('M1', 0, 1, 'V'),
     ('A', 1, 2, 0, 1, 'P'),
-    ('Y', 1, 1, 0, 'S'),
     ('A', 1, 2, 0, 2, 'P'),
     ('A', 1, 2, 0, 3, 'P'),
-    ('A', 1, 2, 0, 4, 'P'),
     ('W', 2, 1, 'V'),
+    ('A', 1, 2, 0, 4, 'P'),
     ('A', 1, 2, 0, 5, 'P'),
-    ('g', 0, 2, 'S'),
     ('A', 1, 2, 1, 0, 'P'),
     ('A', 1, 2, 1, 1, 'P'),
+    ('M2', 0, 1, 'V'),
     ('A', 1, 2, 1, 2, 'P'),
     ('A', 1, 2, 1, 3, 'P'),
-    ('W', 2, 2, 'V'),
+    ('q2', 0, 0, 'V'),
     ('A', 1, 2, 1, 4, 'P'),
-    ('Y', 1, 1, 2, 'S'),
     ('A', 1, 2, 1, 5, 'P'),
+    ('g', 0, 1, 'S'),
     ('A', 1, 2, 2, 0, 'P'),
-    ('n', 0, 1, 'S'),
     ('A', 1, 2, 2, 1, 'P'),
-    ('n', 0, 2, 'V'),
+    ('n', 0, 1, 'S'),
+    ('q2', 1, 0, 'V'),
     ('A', 1, 2, 2, 2, 'P'),
-    ('I2', 1, 0, 'S'),
-    ('n', 0, 3, 'V'),
+    ('n', 0, 2, 'S'),
     ('A', 1, 2, 2, 3, 'P'),
-    ('n', 0, 0, 'V'),
+    ('n', 0, 3, 'S'),
     ('A', 1, 2, 2, 4, 'P'),
-    ('Y', 1, 0, 2, 'V'),
+    ('Y', 1, 1, 0, 'S'),
     ('A', 1, 2, 2, 5, 'P'),
+    ('e', 0, 1, 'V'),
     ('A', 1, 3, 0, 0, 'P'),
     ('A', 1, 3, 0, 1, 'P'),
-    ('e', 0, 2, 'V'),
     ('A', 1, 3, 0, 2, 'P'),
+    ('Y', 1, 2, 2, 'S'),
     ('A', 1, 3, 0, 3, 'P'),
     ('A', 1, 3, 0, 4, 'P'),
+    ('e', 0, 0, 'V'),
+    ('Y', 1, 0, 2, 'S'),
     ('A', 1, 3, 0, 5, 'P'),
     ('A', 1, 3, 1, 0, 'P'),
-    ('e', 0, 3, 'V'),
     ('A', 1, 3, 1, 1, 'P'),
+    ('Y', 1, 2, 0, 'S'),
     ('A', 1, 3, 1, 2, 'P'),
     ('A', 1, 3, 1, 3, 'P'),
+    ('e', 0, 2, 'V'),
     ('A', 1, 3, 1, 4, 'P'),
     ('A', 1, 3, 1, 5, 'P'),
-    ('e', 0, 1, 'V'),
+    ('Y', 1, 1, 2, 'S'),
     ('A', 1, 3, 2, 0, 'P'),
     ('A', 1, 3, 2, 1, 'P'),
-    ('A', 1, 3, 2, 2, 'P'),
-    ('W', 2, 3, 'S'),
-    ('A', 1, 3, 2, 3, 'P'),
-    ('A', 1, 3, 2, 4, 'P'),
-    ('e', 0, 4, 'V'),
-    ('A', 1, 3, 2, 5, 'P'),
-    ('e', 0, 0, 'V'),
-    ('Y', 1, 2, 0, 'S'),
-    ('eq', 0, 1, 'V'),
-    ('Y', 1, 3, 2, 'S'),
-    ('eq', 0, 0, 'V'),
-    ('Y', 1, 3, 0, 'S'),
-    ('q2', 1, 0, 'V'),
-    ('D', 0, 0, 0, 0, 'P'),
     ('I2', 3, 0, 'S'),
-    ('e', 0, 5, 'V'),
+    ('eq', 0, 0, 0, 'V'),
+    ('A', 1, 3, 2, 2, 'P'),
+    ('A', 1, 3, 2, 3, 'P'),
+    ('e', 0, 3, 'V'),
+    ('A', 1, 3, 2, 4, 'P'),
+    ('A', 1, 3, 2, 5, 'P'),
+    ('D', 0, 0, 0, 0, 'P'),
+    ('eq', 0, 0, 1, 'V'),
     ('D', 0, 0, 0, 1, 'P'),
+    ('eq', 0, 1, 2, 'V'),
     ('D', 0, 0, 1, 0, 'P'),
+    ('e', 0, 4, 'V'),
     ('D', 0, 0, 1, 1, 'P'),
-    ('Y', 1, 2, 2, 'V'),
     ('D', 0, 0, 2, 0, 'P'),
-    ('W', 2, 0, 'V'),
+    ('eq', 0, 1, 3, 'V'),
     ('D', 0, 0, 2, 1, 'P'),
+    ('eq', 0, 2, 4, 'V'),
+    ('e', 0, 5, 'V'),
     ('D', 0, 0, 3, 0, 'P'),
-    ('eq', 0, 2, 'V'),
+    ('Y', 1, 3, 0, 'S'),
     ('D', 0, 0, 3, 1, 'P'),
-    ('q2', 2, 0, 'V'),
     ('D', 0, 0, 4, 0, 'P'),
     ('I2', 4, 0, 'S'),
     ('D', 0, 0, 4, 1, 'P'),
-    ('q2', 3, 0, 'V'),
+    ('eq', 0, 2, 5, 'V'),
+    ('q2', 2, 0, 'V'),
     ('D', 0, 0, 5, 0, 'P'),
     ('D', 0, 0, 5, 1, 'P'),
+    ('q2', 3, 0, 'V'),
     ('D', 0, 0, 0, 2, 'P'),
-    ('M0', 1, 0, 'V'),
     ('D', 0, 0, 1, 2, 'P'),
+    ('Y', 1, 3, 2, 'V'),
     ('D', 0, 0, 2, 2, 'P'),
+    ('M0', 1, 0, 'V'),
     ('D', 0, 0, 3, 2, 'P'),
-    ('M0', 1, 1, 'V'),
     ('D', 0, 0, 4, 2, 'P'),
     ('D', 0, 0, 5, 2, 'P'),
     ('I2', 5, 0, 'S'),
+    ('M0', 1, 1, 'V'),
     ('D', 0, 0, 0, 3, 'P'),
-    ('q2', 4, 0, 'V'),
     ('D', 0, 0, 1, 3, 'P'),
     ('D', 0, 0, 2, 3, 'P'),
-    ('M1', 1, 2, 'V'),
+    ('q2', 4, 0, 'V'),
     ('D', 0, 0, 3, 3, 'P'),
     ('D', 0, 0, 4, 3, 'P'),
+    ('M1', 1, 1, 'V'),
     ('D', 0, 0, 5, 3, 'P'),
-    ('M2', 1, 2, 'V'),
+    ('M1', 1, 0, 'V'),
     ('D', 0, 0, 0, 4, 'P'),
+    ('M2', 1, 1, 'V'),
     ('D', 0, 0, 1, 4, 'P'),
+    ('M2', 1, 0, 'V'),
     ('D', 0, 0, 2, 4, 'P'),
-    ('g', 1, 2, 'S'),
+    ('g', 1, 1, 'S'),
     ('D', 0, 0, 3, 4, 'P'),
     ('q2', 5, 0, 'V'),
+    ('g', 1, 0, 'S'),
     ('D', 0, 0, 4, 4, 'P'),
     ('D', 0, 0, 5, 4, 'P'),
     ('n', 1, 0, 'S'),
-    ('n', 1, 2, 'V'),
-    ('D', 0, 0, 0, 5, 'P'),
+    ('n', 1, 1, 'V'),
     ('n', 1, 3, 'V'),
-    ('n', 1, 1, 'S'),
+    ('D', 0, 0, 0, 5, 'P'),
+    ('n', 1, 2, 'V'),
     ('D', 0, 0, 1, 5, 'P'),
     ('e', 1, 0, 'V'),
     ('O', 0, 0, 5, 'S'),
     ('D', 0, 0, 2, 5, 'P'),
     ('D', 0, 0, 3, 5, 'P'),
-    ('O', 0, 0, 1, 'S'),
+    ('O', 0, 0, 3, 'S'),
     ('D', 0, 0, 4, 5, 'P'),
     ('eq', 1, 0, 0, 'V'),
     ('D', 0, 0, 5, 5, 'P'),
     ('e', 1, 1, 'V'),
-    ('O', 0, 0, 4, 'S'),
+    ('O', 0, 0, 1, 'S'),
     ('D', 1, 0, 0, 0, 'P'),
     ('D', 1, 0, 0, 1, 'P'),
-    ('D', 1, 0, 0, 2, 'P'),
     ('O', 0, 0, 2, 'S'),
+    ('D', 1, 0, 0, 2, 'P'),
     ('eq', 1, 0, 1, 'V'),
-    ('D', 1, 0, 0, 3, 'P'),
     ('e', 1, 2, 'V'),
+    ('D', 1, 0, 0, 3, 'P'),
+    ('O', 0, 0, 4, 'S'),
     ('D', 1, 0, 1, 3, 'P'),
     ('D', 1, 0, 1, 5, 'P'),
+    ('O', 0, 0, 0, 'S'),
     ('D', 1, 0, 1, 4, 'P'),
     ('eq', 1, 1, 2, 'V'),
-    ('D', 1, 0, 1, 0, 'P'),
     ('e', 1, 3, 'V'),
+    ('D', 1, 0, 1, 0, 'P'),
     ('D', 1, 0, 2, 2, 'P'),
     ('D', 1, 0, 2, 0, 'P'),
-    ('D', 1, 0, 2, 1, 'P'),
     ('eq', 1, 1, 3, 'V'),
-    ('D', 1, 0, 2, 5, 'P'),
+    ('D', 1, 0, 2, 1, 'P'),
     ('e', 1, 4, 'V'),
+    ('D', 1, 0, 2, 5, 'P'),
     ('D', 1, 0, 3, 5, 'P'),
     ('D', 1, 0, 3, 4, 'P'),
-    ('D', 1, 0, 3, 3, 'P'),
     ('eq', 1, 2, 4, 'V'),
-    ('D', 1, 0, 3, 2, 'P'),
+    ('D', 1, 0, 3, 3, 'P'),
     ('e', 1, 5, 'V'),
+    ('D', 1, 0, 3, 2, 'P'),
     ('D', 1, 0, 4, 1, 'P'),
     ('D', 1, 0, 4, 2, 'P'),
-    ('D', 1, 0, 4, 0, 'P'),
     ('eq', 1, 2, 5, 'V'),
+    ('D', 1, 0, 4, 0, 'P'),
     ('D', 1, 0, 4, 4, 'P'),
-    ('O', 0, 0, 3, 'V'),
     ('D', 1, 0, 5, 4, 'P'),
     ('D', 1, 0, 5, 3, 'P'),
-    ('O', 1, 0, 0, 'V'),
+    ('O', 1, 0, 0, 'S'),
     ('D', 1, 0, 5, 5, 'P'),
+    ('O', 1, 0, 1, 'V'),
     ('D', 1, 0, 5, 1, 'P'),
     ('O', 1, 0, 2, 'S'),
     ('D', 1, 0, 0, 4, 'P'),
     ('O', 1, 0, 3, 'V'),
     ('D', 1, 0, 1, 2, 'P'),
-    ('O', 0, 0, 0, 'S'),
     ('D', 1, 0, 2, 3, 'P'),
     ('D', 1, 0, 3, 1, 'P'),
     ('D', 1, 0, 4, 5, 'P'),
     ('D', 1, 0, 5, 0, 'P'),
-    ('D', 1, 0, 0, 5, 'P'),
-    ('O', 1, 0, 4, 'V'),
-    ('D', 1, 0, 1, 1, 'P'),
-    ('D', 1, 0, 2, 4, 'P'),
-    ('O', 1, 0, 1, 'V'),
-    ('D', 1, 0, 3, 0, 'P'),
-    ('D', 1, 0, 4, 3, 'P'),
-    ('D', 1, 0, 5, 2, 'P'),
-    ('O', 1, 0, 5, 'S'),
+    ('D', 1, 1, 0, 5, 'P'),
+    ('O', 1, 0, 4, 'S'),
+    ('D', 1, 1, 1, 1, 'P'),
+    ('D', 1, 1, 2, 4, 'P'),
+    ('D', 1, 1, 3, 0, 'P'),
+    ('D', 1, 1, 4, 3, 'P'),
+    ('D', 1, 1, 5, 2, 'P'),
+    ('D', 1, 2, 0, 5, 'P'),
+    ('O', 1, 1, 5, 'S'),
+    ('D', 1, 2, 1, 1, 'P'),
+    ('D', 1, 2, 2, 4, 'P'),
+    ('D', 1, 2, 3, 0, 'P'),
+    ('D', 1, 2, 4, 3, 'P'),
+    ('D', 1, 2, 5, 2, 'P'),
+    ('O', 1, 2, 5, 'V'),
 )
 
 P = 128
+COLS = ((0, 512), (0, 256), (256, 512))
 F32 = mybir.dt.float32
 BF16 = mybir.dt.bfloat16
 U32 = mybir.dt.uint32
 U8 = mybir.dt.uint8
-I32 = mybir.dt.int32
 FP8X4 = mybir.dt.float8_e4m3fn_x4
 FP8 = mybir.dt.float8_e4m3fn
 ACT = mybir.ActivationFunctionType
@@ -446,11 +481,9 @@ def tile_dihedralthreegroupblock_kernel(tc, x, w1, b1, ls, w2_bytes, w2_scale, o
         b1_sb = keep.tile([P, 4], BF16, name="b1_sb")
         ls_sb = keep.tile([P, 4], BF16, name="ls_sb")
         sc_sb = keep.tile([P, 4], F32, name="sc_sb")
-        nc.scalar.dma_start(out=sc_sb[:], in_=w2_scale.rearrange("o (p t) z -> p (o t z)", t=4))
-        nc.scalar.dma_start(out=b1_sb[:], in_=b1.rearrange("(p t) -> p t", t=4))
-        nc.scalar.dma_start(out=ls_sb[:], in_=ls.rearrange("(p t) -> p t", t=4))
         ls32 = keep.tile([P, 4], F32, name="ls32")
-        nc.gpsimd.tensor_copy(out=ls32[:], in_=ls_sb[:])
+        zero = keep.tile([P, C], BF16, name="zero", align_bytes=64)
+        nc.vector.memset(zero[:], 0.0)
 
         xs = {}
         w1_raw = {}
@@ -459,8 +492,7 @@ def tile_dihedralthreegroupblock_kernel(tc, x, w1, b1, ls, w2_bytes, w2_scale, o
             if load[0] == "x":
                 a, b = load[1:]
                 t = keep.tile([P, 2, C], BF16, name="xs%d_%d" % (a, b), align_bytes=64)
-                h0, h1 = PAIRS[b]
-                nc.sync.dma_start(out=t[:], in_=x[a * P : (a + 1) * P, h0 : h1 + 1 : h1 - h0, :])
+                nc.sync.dma_start(out=t[:], in_=x[a * P : (a + 1) * P, 2 * b : 2 * b + 2, :])
                 xs[a, b] = t
             elif load[0] == "w1":
                 j = load[1]
@@ -469,6 +501,10 @@ def tile_dihedralthreegroupblock_kernel(tc, x, w1, b1, ls, w2_bytes, w2_scale, o
                 w1_raw[j] = t
             else:
                 j = load[1]
+                if j == 0:
+                    nc.sync.dma_start(out=sc_sb[:], in_=w2_scale.rearrange("o (p t) z -> p (o t z)", t=4))
+                    nc.sync.dma_start(out=b1_sb[:], in_=b1.rearrange("(p t) -> p t", t=4))
+                    nc.sync.dma_start(out=ls_sb[:], in_=ls.rearrange("(p t) -> p t", t=4))
                 if j % 2 == 0:
                     w2_raw[j // 2] = keep.tile([P, 4, 2, C], U8, name="w2_raw%d" % (j // 2), align_bytes=64)
                 nc.sync.dma_start(out=w2_raw[j // 2][:, :, j % 2, :], in_=w2_bytes[j].rearrange("(p t) d -> p t d", t=4))
@@ -478,10 +514,10 @@ def tile_dihedralthreegroupblock_kernel(tc, x, w1, b1, ls, w2_bytes, w2_scale, o
         warm = keep.tile([P, 1], F32, name="warm")
         nc.gpsimd.memset(warm[:], 0.0)
         nc.scalar.activation(out=warm[:], in_=warm[:], func=ACT.Sigmoid)
+        nc.gpsimd.tensor_copy(out=ls32[:], in_=ls_sb[:])
 
-        xc = [keep.tile([P, 3, 3, P], U32, name="xc%d" % a, align_bytes=64) for a in range(2)]
-        xsc = [keep.tile([P, 3, 3, P], U8, name="xsc%d" % a, align_bytes=64) for a in range(2)]
-        nc.gpsimd.memset(xsc[1][:].rearrange("p q s n -> p (q s n)").bitcast(I32), 0)
+        xc = [[keep.tile([P, 3, P], U32, name="xc%d_%d" % (a, q), align_bytes=64) for q in range(3)] for a in range(2)]
+        xsc = [[keep.tile([P, 3, P], U8, name="xsc%d_%d" % (a, q), align_bytes=64) for q in range(3)] for a in range(2)]
         w1c = [keep.tile([P, C], U32, name="w1c%d" % j, align_bytes=64) for j in range(G)]
         w1s = [keep.tile([P, C], U8, name="w1s%d" % j, align_bytes=64) for j in range(G)]
         w2c = [keep.tile([P, C], U32, name="w2c%d" % j, align_bytes=64) for j in range(G)]
@@ -518,22 +554,14 @@ def tile_dihedralthreegroupblock_kernel(tc, x, w1, b1, ls, w2_bytes, w2_scale, o
                 tb[a, b][:].rearrange("p i u r -> p i r u"),
             )
 
-        def x_quant(a, b, dup):
-            if not dup:
-                nc.vector.quantize_mx(
-                    out=xc[a][:, b, 0:2, :].rearrange("p s n -> p (s n)").bitcast(FP8X4),
-                    scales=xsc[a][:, b, 0:2, :].rearrange("p s n -> p (s n)"),
-                    in_=xg[a, b][:].rearrange("p i n t -> p (i n t)"),
-                )
-            elif b < 3:
-                nc.vector.quantize_mx(
-                    out=xc[a][:, b, 2, :].bitcast(FP8X4),
-                    scales=xsc[a][:, b, 2, :],
-                    in_=xg[a, b][:, 0].rearrange("p n t -> p (n t)"),
-                )
-            else:
-                nc.vector.tensor_copy(out=xc[a][:, :, 2, :].bitcast(I32), in_=xc[a][:, :, 0, :].bitcast(I32))
-                nc.vector.tensor_copy(out=xsc[a][:, :, 2, :].bitcast(I32), in_=xsc[a][:, :, 0, :].bitcast(I32))
+        def x_quant(a, h, dup):
+            q = [i for i in range(3) if h in PAIRS[i]][0]
+            slot = 2 if dup else PAIRS[q].index(h)
+            nc.vector.quantize_mx(
+                out=xc[a][q][:, slot, :].bitcast(FP8X4),
+                scales=xsc[a][q][:, slot, :],
+                in_=xg[a, h // 2][:, h % 2].rearrange("p n t -> p (n t)"),
+            )
 
         wg = {}
 
@@ -593,8 +621,8 @@ def tile_dihedralthreegroupblock_kernel(tc, x, w1, b1, ls, w2_bytes, w2_scale, o
                 out=acc,
                 lhsT=w1c[j][:, cols].bitcast(FP8X4),
                 lhsT_scale=w1s[j][:, cols],
-                rhs=xc[a][:, q, s0 : s0 + 2, :].rearrange("p s n -> p (s n)").bitcast(FP8X4),
-                rhs_scale=xsc[a][:, q, s0 : s0 + 2, :].rearrange("p s n -> p (s n)"),
+                rhs=xc[a][q][:, s0 : s0 + 2, :].rearrange("p s n -> p (s n)").bitcast(FP8X4),
+                rhs_scale=xsc[a][q][:, s0 : s0 + 2, :].rearrange("p s n -> p (s n)"),
                 start=first,
                 stop=last,
             )
@@ -629,9 +657,9 @@ def tile_dihedralthreegroupblock_kernel(tc, x, w1, b1, ls, w2_bytes, w2_scale, o
             if (a, pos // 2) not in eg:
                 eg[a, pos // 2] = keep.tile([P, 2, P, 4], BF16, name="eg", tag="xg", align_bytes=64, bufs=6)
             nc.vector.tensor_tensor(
-                out=eg[a, pos // 2][:, pos % 2].rearrange("p (c i) t -> p c t i", i=2),
-                in0=y_sb[:, a, :, pos, :].rearrange("p t (c i) -> p c t i", i=2),
-                in1=s_sb[:, a].rearrange("p t (c i) -> p c t i", i=2),
+                out=eg[a, pos // 2][:, pos % 2].rearrange("p (c i) t -> p c t i", i=4),
+                in0=y_sb[:, a, :, pos, :].rearrange("p t (c i) -> p c t i", i=4),
+                in1=s_sb[:, a].rearrange("p t (c i) -> p c t i", i=4),
                 op=ALU.mult,
             )
 
@@ -642,22 +670,22 @@ def tile_dihedralthreegroupblock_kernel(tc, x, w1, b1, ls, w2_bytes, w2_scale, o
                 in_=eg[a, q][:, i0:i1].rearrange("p s n t -> p (s n t)"),
             )
 
-        def conv2(acc, a, h, j, first, last):
+        def conv2(acc, a, h, j, c0, c1, first, last):
             i = POS.index(h)
             nc.tensor.matmul_mx(
                 out=acc,
                 lhsT=ec[a][i // 2][:, i % 2, :].bitcast(FP8X4),
                 lhsT_scale=es[a][i // 2][:, i % 2, :],
-                rhs=w2c[j][:].bitcast(FP8X4),
-                rhs_scale=w2s[j][:],
+                rhs=w2c[j][:, c0:c1].bitcast(FP8X4),
+                rhs_scale=w2s[j][:, c0:c1],
                 start=first,
                 stop=last,
             )
 
-        def store(acc, a, g, eng):
-            o = work.tile([P, C], F32, name="o_sb", bufs=6)
-            copy(eng, o[:], acc[:])
-            nc.sync.dma_start(out=out[a * P : (a + 1) * P, g, :], in_=o[:])
+        def store(acc, a, g, c0, c1, eng):
+            o = work.tile([P, c1 - c0], F32, name="o_sb", bufs=6)
+            copy(eng, o[:], acc[:, 0 : c1 - c0])
+            nc.sync.dma_start(out=out[a * P : (a + 1) * P, g, c0:c1], in_=o[:])
 
         banks = {}
         count = {}
@@ -670,7 +698,11 @@ def tile_dihedralthreegroupblock_kernel(tc, x, w1, b1, ls, w2_bytes, w2_scale, o
 
         for step in PROGRAM:
             kind, arg, eng = step[0], step[1:-1], step[-1]
-            if kind == "T":
+            if kind == "Z":
+                if "Z" not in banks:
+                    banks["Z"] = bank([P, C], SLOTS["Z",])
+                nc.tensor.matmul(out=banks["Z"][:], lhsT=zero[:, 0:P], rhs=zero[:], start=True, stop=True)
+            elif kind == "T":
                 x_transpose(arg[0], arg[1], SLOTS[("T",) + arg])
             elif kind == "E":
                 x_evac(arg[0], arg[1], eng)
@@ -718,8 +750,9 @@ def tile_dihedralthreegroupblock_kernel(tc, x, w1, b1, ls, w2_bytes, w2_scale, o
                 a, dh, pos, j = arg
                 h = POS[pos]
                 g = [gg for gg in range(G) if K[h][gg] == j][0]
-                acc, first, last = group(("D", a, dh, g), ("D", a, dh, g), 0, C)
-                conv2(acc, a, h, j, first, last)
+                c0, c1 = COLS[dh]
+                acc, first, last = group(("D", a, dh, g), ("D", a, dh, g), 0, c1 - c0)
+                conv2(acc, a, h, j, c0, c1, first, last)
             elif kind == "O":
                 a, dh, g = arg
-                store(banks["D", a, dh, g], a, g, eng)
+                store(banks["D", a, dh, g], a, g, *COLS[dh], eng)

@@ -15,744 +15,432 @@ K = (
     (5, 4, 3, 2, 1, 0),
 )
 PAIRS = ((0, 3), (1, 5), (2, 4))
-POS = (0, 3, 1, 5, 2, 4)
-
-YMERGE = ((0, 2), (0, 3), (1, 1), (1, 2), (1, 3))
-
-LOADS = (('w1', 0), ('x', 0, 0), ('x', 0, 1), ('x', 0, 2), ('w1', 1), ('x', 1, 0), ('x', 1, 1), ('x', 1, 2), ('w1', 2), ('w1', 3), ('w1', 4), ('w1', 5), ('w2', 0), ('w2', 1), ('w2', 2), ('w2', 3), ('w2', 4), ('w2', 5))
-
-SLOTS = {
-    ('Z',): 0,
-    ('T', 0, 0): 1,
-    ('T', 0, 1): 2,
-    ('T', 0, 2): 3,
-    ('A', 0, 0, 0): 4,
-    ('A', 0, 1, 0): 5,
-    ('A', 0, 0, 1): 6,
-    ('A', 0, 1, 1): 7,
-    ('A', 0, 0, 2): 1,
-    ('A', 0, 1, 2): 2,
-    ('T', 1, 0): 3,
-    ('T', 1, 1): 0,
-    ('T', 1, 2): 3,
-    ('A', 1, 0, 0): 0,
-    ('A', 1, 0, 1): 3,
-    ('A', 0, 2, 0): 4,
-    ('A', 0, 2, 2): 5,
-    ('A', 0, 3, 0): 6,
-    ('A', 0, 3, 2): 7,
-    ('A', 1, 0, 2): 1,
-    ('A', 1, 1, 0): 2,
-    ('A', 1, 1, 2): 0,
-    ('A', 1, 2, 0): 3,
-    ('A', 1, 2, 2): 4,
-    ('A', 1, 3, 0): 5,
-    ('A', 1, 3, 2): 6,
-    ('D', 0, 0, 0): 7,
-    ('D', 0, 0, 1): 1,
-    ('D', 0, 0, 3): 2,
-    ('D', 0, 0, 5): 0,
-    ('D', 0, 0, 2): 3,
-    ('D', 0, 0, 4): 4,
-    ('D', 1, 0, 0): 5,
-    ('D', 1, 0, 1): 6,
-    ('D', 1, 0, 2): 0,
-    ('D', 1, 0, 3): 1,
-    ('D', 1, 0, 4): 2,
-    ('D', 1, 1, 5): 7,
-    ('D', 1, 2, 5): 4,
-}
-
-PROGRAM = (
-    ('Z', 0, 'P'),
-    ('Z', 1, 'P'),
-    ('Z', 2, 'P'),
-    ('Z', 3, 'P'),
-    ('Z', 4, 'P'),
-    ('Z', 5, 'P'),
-    ('Z', 6, 'P'),
-    ('Z', 7, 'P'),
-    ('I', 0, 0, 'V'),
-    ('I', 0, 1, 'S'),
-    ('T', 0, 0, 'P'),
-    ('T', 0, 1, 'P'),
-    ('E', 0, 0, 'S'),
-    ('T', 0, 2, 'P'),
-    ('E', 0, 1, 'S'),
-    ('Q', 0, 1, 0, 'V'),
-    ('Q', 0, 0, 0, 'V'),
-    ('Z', 8, 'P'),
-    ('q', 0, 0, 'V'),
-    ('E', 0, 2, 'S'),
-    ('Q', 0, 3, 0, 'V'),
-    ('Q', 0, 1, 1, 'V'),
-    ('A', 0, 0, 0, 0, 'P'),
-    ('Q', 0, 2, 0, 'V'),
-    ('I', 1, 1, 'S'),
-    ('A', 0, 1, 0, 0, 'P'),
-    ('Q', 0, 5, 0, 'V'),
-    ('Q', 0, 4, 0, 'V'),
-    ('A', 0, 0, 1, 0, 'P'),
-    ('I', 1, 0, 'V'),
-    ('A', 0, 1, 1, 0, 'P'),
-    ('A', 0, 0, 2, 0, 'P'),
-    ('A', 0, 1, 2, 0, 'P'),
-    ('T', 1, 0, 'P'),
-    ('Q', 0, 2, 1, 'V'),
-    ('q', 1, 0, 'V'),
-    ('q', 0, 1, 'V'),
-    ('E', 1, 0, 'S'),
-    ('A', 0, 0, 0, 1, 'P'),
-    ('q', 1, 1, 'V'),
-    ('A', 0, 1, 0, 1, 'P'),
-    ('A', 0, 0, 1, 1, 'P'),
-    ('Q', 0, 0, 1, 'V'),
-    ('A', 0, 1, 1, 1, 'P'),
-    ('Q', 1, 0, 1, 'V'),
-    ('A', 0, 0, 2, 1, 'P'),
-    ('A', 0, 1, 2, 1, 'P'),
-    ('Q', 1, 1, 0, 'V'),
-    ('T', 1, 1, 'P'),
-    ('I', 2, 0, 'S'),
-    ('I', 2, 1, 'V'),
-    ('T', 1, 2, 'P'),
-    ('Q', 1, 0, 0, 'V'),
-    ('q', 2, 1, 'V'),
-    ('I', 3, 0, 'V'),
-    ('E', 1, 1, 'S'),
-    ('E', 1, 2, 'S'),
-    ('q', 2, 0, 'V'),
-    ('q', 3, 0, 'V'),
-    ('A', 0, 0, 0, 2, 'P'),
-    ('I', 4, 0, 'S'),
-    ('Q', 1, 3, 0, 'V'),
-    ('A', 0, 1, 0, 2, 'P'),
-    ('Q', 1, 1, 1, 'V'),
-    ('A', 0, 0, 1, 2, 'P'),
-    ('Q', 1, 5, 0, 'V'),
-    ('A', 0, 1, 1, 2, 'P'),
-    ('Q', 1, 2, 0, 'V'),
-    ('A', 0, 0, 2, 2, 'P'),
-    ('A', 0, 1, 2, 2, 'P'),
-    ('Q', 1, 4, 0, 'V'),
-    ('A', 1, 0, 0, 0, 'P'),
-    ('I', 4, 1, 'V'),
-    ('A', 1, 0, 1, 0, 'P'),
-    ('A', 1, 0, 0, 1, 'P'),
-    ('A', 1, 0, 1, 1, 'P'),
-    ('I', 5, 1, 'S'),
-    ('A', 1, 0, 0, 2, 'P'),
-    ('Q', 1, 2, 1, 'V'),
-    ('A', 1, 0, 1, 2, 'P'),
-    ('A', 0, 0, 0, 3, 'P'),
-    ('I', 5, 0, 'V'),
-    ('A', 0, 1, 0, 3, 'P'),
-    ('A', 0, 0, 1, 3, 'P'),
-    ('A', 0, 1, 1, 3, 'P'),
-    ('A', 0, 0, 2, 3, 'P'),
-    ('q', 4, 0, 'V'),
-    ('A', 0, 1, 2, 3, 'P'),
-    ('A', 1, 0, 0, 3, 'P'),
-    ('W', 0, 2, 'S'),
-    ('A', 1, 0, 1, 3, 'P'),
-    ('q', 5, 0, 'V'),
-    ('A', 0, 0, 0, 4, 'P'),
-    ('A', 0, 1, 0, 4, 'P'),
-    ('q', 4, 1, 'V'),
-    ('A', 0, 0, 1, 4, 'P'),
-    ('A', 0, 1, 1, 4, 'P'),
-    ('I', 3, 1, 'V'),
-    ('A', 0, 0, 2, 4, 'P'),
-    ('A', 0, 1, 2, 4, 'P'),
-    ('A', 1, 0, 0, 4, 'P'),
-    ('W', 0, 3, 'S'),
-    ('A', 1, 0, 1, 4, 'P'),
-    ('A', 0, 0, 0, 5, 'P'),
-    ('q', 5, 1, 'V'),
-    ('A', 0, 1, 0, 5, 'P'),
-    ('A', 0, 0, 1, 5, 'P'),
-    ('Y', 0, 0, 0, 'V'),
-    ('A', 0, 1, 1, 5, 'P'),
-    ('A', 0, 0, 2, 5, 'P'),
-    ('q', 3, 1, 'V'),
-    ('A', 0, 1, 2, 5, 'P'),
-    ('A', 1, 0, 0, 5, 'P'),
-    ('W', 1, 3, 'S'),
-    ('Y', 0, 1, 1, 'V'),
-    ('A', 1, 0, 1, 5, 'P'),
-    ('A', 0, 2, 0, 0, 'P'),
-    ('W', 0, 1, 'V'),
-    ('A', 0, 2, 0, 1, 'P'),
-    ('A', 0, 2, 0, 2, 'P'),
-    ('A', 0, 2, 0, 3, 'P'),
-    ('A', 0, 2, 0, 4, 'P'),
-    ('W', 2, 2, 'V'),
-    ('A', 0, 2, 0, 5, 'P'),
-    ('A', 0, 2, 1, 0, 'P'),
-    ('Y', 0, 0, 2, 'S'),
-    ('A', 0, 2, 1, 1, 'P'),
-    ('A', 0, 2, 1, 2, 'P'),
-    ('Y', 0, 1, 0, 'S'),
-    ('Y', 0, 0, 1, 'V'),
-    ('A', 0, 2, 1, 3, 'P'),
-    ('A', 0, 2, 1, 4, 'P'),
-    ('Y', 1, 0, 0, 'S'),
-    ('W', 1, 1, 'V'),
-    ('A', 0, 2, 1, 5, 'P'),
-    ('A', 0, 2, 2, 0, 'P'),
-    ('Y', 0, 1, 2, 'S'),
-    ('A', 0, 2, 2, 1, 'P'),
-    ('A', 0, 2, 2, 2, 'P'),
-    ('Y', 0, 2, 0, 'S'),
-    ('W', 0, 0, 'V'),
-    ('A', 0, 2, 2, 3, 'P'),
-    ('A', 0, 2, 2, 4, 'P'),
-    ('A', 0, 2, 2, 5, 'P'),
-    ('A', 0, 3, 0, 0, 'P'),
-    ('Y', 1, 0, 1, 'S'),
-    ('Y', 0, 2, 2, 'V'),
-    ('A', 0, 3, 0, 1, 'P'),
-    ('A', 0, 3, 0, 2, 'P'),
-    ('I2', 1, 0, 'S'),
-    ('M0', 0, 0, 'V'),
-    ('A', 0, 3, 0, 3, 'P'),
-    ('A', 0, 3, 0, 4, 'P'),
-    ('A', 0, 3, 0, 5, 'P'),
-    ('A', 0, 3, 1, 0, 'P'),
-    ('A', 0, 3, 1, 1, 'P'),
-    ('A', 0, 3, 1, 2, 'P'),
-    ('I2', 0, 0, 'V'),
-    ('A', 0, 3, 1, 3, 'P'),
-    ('A', 0, 3, 1, 4, 'P'),
-    ('A', 0, 3, 1, 5, 'P'),
-    ('A', 0, 3, 2, 0, 'P'),
-    ('A', 0, 3, 2, 1, 'P'),
-    ('A', 0, 3, 2, 2, 'P'),
-    ('A', 0, 3, 2, 3, 'P'),
-    ('A', 0, 3, 2, 4, 'P'),
-    ('A', 0, 3, 2, 5, 'P'),
-    ('A', 1, 0, 2, 0, 'P'),
-    ('M1', 0, 0, 'V'),
-    ('A', 1, 0, 2, 1, 'P'),
-    ('A', 1, 0, 2, 2, 'P'),
-    ('Y', 0, 3, 2, 'V'),
-    ('Y', 0, 3, 0, 'S'),
-    ('A', 1, 0, 2, 3, 'P'),
-    ('A', 1, 0, 2, 4, 'P'),
-    ('M2', 0, 0, 'V'),
-    ('A', 1, 0, 2, 5, 'P'),
-    ('A', 1, 1, 0, 0, 'P'),
-    ('W', 1, 0, 'V'),
-    ('W', 1, 2, 'S'),
-    ('A', 1, 1, 0, 1, 'P'),
-    ('A', 1, 1, 0, 2, 'P'),
-    ('A', 1, 1, 0, 3, 'P'),
-    ('A', 1, 1, 0, 4, 'P'),
-    ('W', 2, 3, 'V'),
-    ('A', 1, 1, 0, 5, 'P'),
-    ('A', 1, 1, 1, 0, 'P'),
-    ('A', 1, 1, 1, 1, 'P'),
-    ('A', 1, 1, 1, 2, 'P'),
-    ('M0', 0, 1, 'V'),
-    ('g', 0, 0, 'S'),
-    ('A', 1, 1, 1, 3, 'P'),
-    ('A', 1, 1, 1, 4, 'P'),
-    ('A', 1, 1, 1, 5, 'P'),
-    ('I2', 2, 0, 'S'),
-    ('A', 1, 1, 2, 0, 'P'),
-    ('A', 1, 1, 2, 1, 'P'),
-    ('A', 1, 1, 2, 2, 'P'),
-    ('W', 2, 0, 'V'),
-    ('A', 1, 1, 2, 3, 'P'),
-    ('A', 1, 1, 2, 4, 'P'),
-    ('A', 1, 1, 2, 5, 'P'),
-    ('A', 1, 2, 0, 0, 'P'),
-    ('n', 0, 0, 'V'),
-    ('M1', 0, 1, 'V'),
-    ('A', 1, 2, 0, 1, 'P'),
-    ('A', 1, 2, 0, 2, 'P'),
-    ('A', 1, 2, 0, 3, 'P'),
-    ('W', 2, 1, 'V'),
-    ('A', 1, 2, 0, 4, 'P'),
-    ('A', 1, 2, 0, 5, 'P'),
-    ('A', 1, 2, 1, 0, 'P'),
-    ('A', 1, 2, 1, 1, 'P'),
-    ('M2', 0, 1, 'V'),
-    ('A', 1, 2, 1, 2, 'P'),
-    ('A', 1, 2, 1, 3, 'P'),
-    ('q2', 0, 0, 'V'),
-    ('A', 1, 2, 1, 4, 'P'),
-    ('A', 1, 2, 1, 5, 'P'),
-    ('g', 0, 1, 'S'),
-    ('A', 1, 2, 2, 0, 'P'),
-    ('A', 1, 2, 2, 1, 'P'),
-    ('n', 0, 1, 'S'),
-    ('q2', 1, 0, 'V'),
-    ('A', 1, 2, 2, 2, 'P'),
-    ('n', 0, 2, 'S'),
-    ('A', 1, 2, 2, 3, 'P'),
-    ('n', 0, 3, 'S'),
-    ('A', 1, 2, 2, 4, 'P'),
-    ('Y', 1, 1, 0, 'S'),
-    ('A', 1, 2, 2, 5, 'P'),
-    ('e', 0, 1, 'V'),
-    ('A', 1, 3, 0, 0, 'P'),
-    ('A', 1, 3, 0, 1, 'P'),
-    ('A', 1, 3, 0, 2, 'P'),
-    ('Y', 1, 2, 2, 'S'),
-    ('A', 1, 3, 0, 3, 'P'),
-    ('A', 1, 3, 0, 4, 'P'),
-    ('e', 0, 0, 'V'),
-    ('Y', 1, 0, 2, 'S'),
-    ('A', 1, 3, 0, 5, 'P'),
-    ('A', 1, 3, 1, 0, 'P'),
-    ('A', 1, 3, 1, 1, 'P'),
-    ('Y', 1, 2, 0, 'S'),
-    ('A', 1, 3, 1, 2, 'P'),
-    ('A', 1, 3, 1, 3, 'P'),
-    ('e', 0, 2, 'V'),
-    ('A', 1, 3, 1, 4, 'P'),
-    ('A', 1, 3, 1, 5, 'P'),
-    ('Y', 1, 1, 2, 'S'),
-    ('A', 1, 3, 2, 0, 'P'),
-    ('A', 1, 3, 2, 1, 'P'),
-    ('I2', 3, 0, 'S'),
-    ('eq', 0, 0, 0, 'V'),
-    ('A', 1, 3, 2, 2, 'P'),
-    ('A', 1, 3, 2, 3, 'P'),
-    ('e', 0, 3, 'V'),
-    ('A', 1, 3, 2, 4, 'P'),
-    ('A', 1, 3, 2, 5, 'P'),
-    ('D', 0, 0, 0, 0, 'P'),
-    ('eq', 0, 0, 1, 'V'),
-    ('D', 0, 0, 0, 1, 'P'),
-    ('eq', 0, 1, 2, 'V'),
-    ('D', 0, 0, 1, 0, 'P'),
-    ('e', 0, 4, 'V'),
-    ('D', 0, 0, 1, 1, 'P'),
-    ('D', 0, 0, 2, 0, 'P'),
-    ('eq', 0, 1, 3, 'V'),
-    ('D', 0, 0, 2, 1, 'P'),
-    ('eq', 0, 2, 4, 'V'),
-    ('e', 0, 5, 'V'),
-    ('D', 0, 0, 3, 0, 'P'),
-    ('Y', 1, 3, 0, 'S'),
-    ('D', 0, 0, 3, 1, 'P'),
-    ('D', 0, 0, 4, 0, 'P'),
-    ('I2', 4, 0, 'S'),
-    ('D', 0, 0, 4, 1, 'P'),
-    ('eq', 0, 2, 5, 'V'),
-    ('q2', 2, 0, 'V'),
-    ('D', 0, 0, 5, 0, 'P'),
-    ('D', 0, 0, 5, 1, 'P'),
-    ('q2', 3, 0, 'V'),
-    ('D', 0, 0, 0, 2, 'P'),
-    ('D', 0, 0, 1, 2, 'P'),
-    ('Y', 1, 3, 2, 'V'),
-    ('D', 0, 0, 2, 2, 'P'),
-    ('M0', 1, 0, 'V'),
-    ('D', 0, 0, 3, 2, 'P'),
-    ('D', 0, 0, 4, 2, 'P'),
-    ('D', 0, 0, 5, 2, 'P'),
-    ('I2', 5, 0, 'S'),
-    ('M0', 1, 1, 'V'),
-    ('D', 0, 0, 0, 3, 'P'),
-    ('D', 0, 0, 1, 3, 'P'),
-    ('D', 0, 0, 2, 3, 'P'),
-    ('q2', 4, 0, 'V'),
-    ('D', 0, 0, 3, 3, 'P'),
-    ('D', 0, 0, 4, 3, 'P'),
-    ('M1', 1, 1, 'V'),
-    ('D', 0, 0, 5, 3, 'P'),
-    ('M1', 1, 0, 'V'),
-    ('D', 0, 0, 0, 4, 'P'),
-    ('M2', 1, 1, 'V'),
-    ('D', 0, 0, 1, 4, 'P'),
-    ('M2', 1, 0, 'V'),
-    ('D', 0, 0, 2, 4, 'P'),
-    ('g', 1, 1, 'S'),
-    ('D', 0, 0, 3, 4, 'P'),
-    ('q2', 5, 0, 'V'),
-    ('g', 1, 0, 'S'),
-    ('D', 0, 0, 4, 4, 'P'),
-    ('D', 0, 0, 5, 4, 'P'),
-    ('n', 1, 0, 'S'),
-    ('n', 1, 1, 'V'),
-    ('n', 1, 3, 'V'),
-    ('D', 0, 0, 0, 5, 'P'),
-    ('n', 1, 2, 'V'),
-    ('D', 0, 0, 1, 5, 'P'),
-    ('e', 1, 0, 'V'),
-    ('O', 0, 0, 5, 'S'),
-    ('D', 0, 0, 2, 5, 'P'),
-    ('D', 0, 0, 3, 5, 'P'),
-    ('O', 0, 0, 3, 'S'),
-    ('D', 0, 0, 4, 5, 'P'),
-    ('eq', 1, 0, 0, 'V'),
-    ('D', 0, 0, 5, 5, 'P'),
-    ('e', 1, 1, 'V'),
-    ('O', 0, 0, 1, 'S'),
-    ('D', 1, 0, 0, 0, 'P'),
-    ('D', 1, 0, 0, 1, 'P'),
-    ('O', 0, 0, 2, 'S'),
-    ('D', 1, 0, 0, 2, 'P'),
-    ('eq', 1, 0, 1, 'V'),
-    ('e', 1, 2, 'V'),
-    ('D', 1, 0, 0, 3, 'P'),
-    ('O', 0, 0, 4, 'S'),
-    ('D', 1, 0, 1, 3, 'P'),
-    ('D', 1, 0, 1, 5, 'P'),
-    ('O', 0, 0, 0, 'S'),
-    ('D', 1, 0, 1, 4, 'P'),
-    ('eq', 1, 1, 2, 'V'),
-    ('e', 1, 3, 'V'),
-    ('D', 1, 0, 1, 0, 'P'),
-    ('D', 1, 0, 2, 2, 'P'),
-    ('D', 1, 0, 2, 0, 'P'),
-    ('eq', 1, 1, 3, 'V'),
-    ('D', 1, 0, 2, 1, 'P'),
-    ('e', 1, 4, 'V'),
-    ('D', 1, 0, 2, 5, 'P'),
-    ('D', 1, 0, 3, 5, 'P'),
-    ('D', 1, 0, 3, 4, 'P'),
-    ('eq', 1, 2, 4, 'V'),
-    ('D', 1, 0, 3, 3, 'P'),
-    ('e', 1, 5, 'V'),
-    ('D', 1, 0, 3, 2, 'P'),
-    ('D', 1, 0, 4, 1, 'P'),
-    ('D', 1, 0, 4, 2, 'P'),
-    ('eq', 1, 2, 5, 'V'),
-    ('D', 1, 0, 4, 0, 'P'),
-    ('D', 1, 0, 4, 4, 'P'),
-    ('D', 1, 0, 5, 4, 'P'),
-    ('D', 1, 0, 5, 3, 'P'),
-    ('O', 1, 0, 0, 'S'),
-    ('D', 1, 0, 5, 5, 'P'),
-    ('O', 1, 0, 1, 'V'),
-    ('D', 1, 0, 5, 1, 'P'),
-    ('O', 1, 0, 2, 'S'),
-    ('D', 1, 0, 0, 4, 'P'),
-    ('O', 1, 0, 3, 'V'),
-    ('D', 1, 0, 1, 2, 'P'),
-    ('D', 1, 0, 2, 3, 'P'),
-    ('D', 1, 0, 3, 1, 'P'),
-    ('D', 1, 0, 4, 5, 'P'),
-    ('D', 1, 0, 5, 0, 'P'),
-    ('D', 1, 1, 0, 5, 'P'),
-    ('O', 1, 0, 4, 'S'),
-    ('D', 1, 1, 1, 1, 'P'),
-    ('D', 1, 1, 2, 4, 'P'),
-    ('D', 1, 1, 3, 0, 'P'),
-    ('D', 1, 1, 4, 3, 'P'),
-    ('D', 1, 1, 5, 2, 'P'),
-    ('D', 1, 2, 0, 5, 'P'),
-    ('O', 1, 1, 5, 'S'),
-    ('D', 1, 2, 1, 1, 'P'),
-    ('D', 1, 2, 2, 4, 'P'),
-    ('D', 1, 2, 3, 0, 'P'),
-    ('D', 1, 2, 4, 3, 'P'),
-    ('D', 1, 2, 5, 2, 'P'),
-    ('O', 1, 2, 5, 'V'),
-)
+ORDER = (0, 3, 1, 5, 2, 4)
 
 P = 128
-COLS = ((0, 512), (0, 256), (256, 512))
+PACK = 4
+COPIED_BUFS = 6
+MIX1_BUFS = 8
 F32 = mybir.dt.float32
 BF16 = mybir.dt.bfloat16
 U32 = mybir.dt.uint32
 U8 = mybir.dt.uint8
-FP8X4 = mybir.dt.float8_e4m3fn_x4
 FP8 = mybir.dt.float8_e4m3fn
+FP8X4 = mybir.dt.float8_e4m3fn_x4
 ACT = mybir.ActivationFunctionType
 ALU = mybir.AluOpType
+
+PARTS = ((0, C), (0, C // 2), (C // 2, C))
+
+VECTOR = """
+mix1:01 w1q:01 w1q:00 fetch:01 xq:000 xq:010 xq:030 xq:020 xq:050 xq:040 xq:011 mix1:11 xq:021 w1q:10 xq:001
+w1q:11 xq:101 xq:110 mix1:20 xq:100 w1q:20 mix1:30 xq:111 xq:130 xq:120 xq:121 xq:150 xq:140 w1q:30 w1q:21
+mix1:41 w1q:40 mix1:31 w1q:50 widen:00 widen:03 w1q:31 w1q:41 w1q:51 widen:01 y:012 widen:11 mix2:1 max1:00
+widen:10 mix2:0 w2q:1 max1:01 max2:00 max2:01 max3:00 w2q:0 max3:01 widen:23 gain:00 gain:02 y:112 e:02 e:00
+e:03 eq:00 e:01 e:05 eq:01 eq:02 e:04 eq:05 eq:03 eq:04 w2q:2 max1:10 mix2:4 w2q:3 max1:11 w2q:4 max2:11
+max2:10 max3:11 max3:10 w2q:5 gain:10 gain:12 e:10 eq:10 e:11 eq:11 e:12 store:030 eq:12 e:13 eq:13 e:14
+eq:14 e:15 eq:15 store:100 store:120 store:130 store:152
+"""
+SCALAR = """
+mix1:00 fetch:00 fetch:02 mix1:10 fetch:10 mix1:21 fetch:11 fetch:12 mix1:40 mix1:50 mix1:51 y:000 widen:02
+y:002 y:010 y:001 widen:12 y:011 y:022 widen:13 y:020 y:101 y:032 y:030 y:100 mix2:2 gate:00 gate:01 gain:01
+gain:03 y:102 widen:20 y:120 y:122 y:110 widen:22 widen:21 mix2:3 y:130 y:132 mix2:5 gate:11 gate:10 gain:11
+gain:13 store:050 store:010 store:000 store:020 store:040 store:110 store:140 store:151
+"""
+
+
+def tensor_steps():
+    steps = [("warm", i) for i in range(8)]
+    steps += [("turn", 0, b) for b in range(3)]
+    steps += [("warm", 8)]
+
+    def first(j):
+        return [("conv1", 0, t, q, j) for q in range(3) for t in range(2)]
+
+    def second(j):
+        return [("conv1", 1, 0, q, j) for q in range(2)]
+
+    steps += first(0) + [("turn", 1, 0)] + first(1) + [("turn", 1, 1), ("turn", 1, 2)] + first(2)
+    steps += second(0) + second(1) + second(2)
+    for j in range(3, G):
+        steps += first(j) + second(j)
+
+    for a in range(2):
+        for t in range(4):
+            for q in range(3):
+                for j in range(G):
+                    if ("conv1", a, t, q, j) not in steps:
+                        steps.append(("conv1", a, t, q, j))
+
+    steps += [("conv2", 0, h, j, 0) for h in ORDER for j in range(2)]
+    steps += [("conv2", 0, h, j, 0) for j in range(2, G) for h in ORDER]
+    steps += [("conv2", 1, h, K[h][g], 0) for h in ORDER for g in range(4)]
+    steps += [("conv2", 1, h, K[h][4], 0) for h in ORDER]
+    steps += [("conv2", 1, h, K[h][5], part) for part in (1, 2) for h in ORDER]
+    return steps
+
+
+def parse(text):
+    return [(w.split(":")[0],) + tuple(int(d) for d in w.split(":")[1]) for w in text.split()]
+
+
+def window(q, j):
+    h = [[h for h in range(G) if K[h][g] == j][0] for g in PAIRS[q]]
+    pair = [i for i in range(3) if h[0] in PAIRS[i]][0]
+    return pair, PAIRS[pair].index(h[0])
+
+
+def goal(h, j):
+    return K[h].index(j)
+
+
+def one_by_one(a, t):
+    return (a, t) not in ((0, 0), (0, 1), (1, 0))
 
 
 def tile_dihedralthreegroupblock_kernel(tc, x, w1, b1, ls, w2_bytes, w2_scale, out):
     nc = tc.nc
     with ExitStack() as ctx:
         keep = ctx.enter_context(tc.tile_pool(name="keep", bufs=1))
-        work = ctx.enter_context(tc.tile_pool(name="work", bufs=3))
+        work = ctx.enter_context(tc.tile_pool(name="work", bufs=6))
         psum = ctx.enter_context(tc.psum_pool(name="psum", bufs=1))
         ctx.enter_context(tc.manual_schedule())
 
-        def bank(shape, slot):
-            return psum.tile(shape, F32, name="bank%d" % slot)
-
-        b1_sb = keep.tile([P, 4], BF16, name="b1_sb")
-        ls_sb = keep.tile([P, 4], BF16, name="ls_sb")
-        sc_sb = keep.tile([P, 4], F32, name="sc_sb")
-        ls32 = keep.tile([P, 4], F32, name="ls32")
-        zero = keep.tile([P, C], BF16, name="zero", align_bytes=64)
-        nc.vector.memset(zero[:], 0.0)
-
-        xs = {}
+        x_raw = {}
         w1_raw = {}
         w2_raw = {}
-        for load in LOADS:
-            if load[0] == "x":
-                a, b = load[1:]
-                t = keep.tile([P, 2, C], BF16, name="xs%d_%d" % (a, b), align_bytes=64)
-                nc.sync.dma_start(out=t[:], in_=x[a * P : (a + 1) * P, 2 * b : 2 * b + 2, :])
-                xs[a, b] = t
-            elif load[0] == "w1":
-                j = load[1]
-                t = keep.tile([P, 4, C], BF16, name="w1_raw%d" % j, align_bytes=64)
-                nc.sync.dma_start(out=t[:], in_=w1[j].rearrange("(p t) d -> p t d", t=4))
-                w1_raw[j] = t
-            else:
-                j = load[1]
-                if j == 0:
-                    nc.sync.dma_start(out=sc_sb[:], in_=w2_scale.rearrange("o (p t) z -> p (o t z)", t=4))
-                    nc.sync.dma_start(out=b1_sb[:], in_=b1.rearrange("(p t) -> p t", t=4))
-                    nc.sync.dma_start(out=ls_sb[:], in_=ls.rearrange("(p t) -> p t", t=4))
-                if j % 2 == 0:
-                    w2_raw[j // 2] = keep.tile([P, 4, 2, C], U8, name="w2_raw%d" % (j // 2), align_bytes=64)
-                nc.sync.dma_start(out=w2_raw[j // 2][:, :, j % 2, :], in_=w2_bytes[j].rearrange("(p t) d -> p t d", t=4))
+        b1_sb = keep.tile([P, PACK], BF16, name="b1_sb")
+        ls_bf = keep.tile([P, PACK], BF16, name="ls_bf")
+        ls_sb = keep.tile([P, PACK], F32, name="ls_sb")
+        scale_sb = keep.tile([P, PACK], F32, name="scale_sb")
 
+        def load_w1(j):
+            w1_raw[j] = keep.tile([P, PACK, C], BF16, name="w1_raw%d" % j, align_bytes=64)
+            nc.sync.dma_start(out=w1_raw[j][:], in_=w1[j].rearrange("(p k) d -> p k d", k=PACK))
+
+        def load_x(a):
+            for b in range(3):
+                x_raw[a, b] = keep.tile([P, 2, C], BF16, name="x_raw%d_%d" % (a, b), align_bytes=64)
+                nc.sync.dma_start(out=x_raw[a, b][:], in_=x[a * P : (a + 1) * P, 2 * b : 2 * b + 2, :])
+
+        load_w1(0)
+        load_x(0)
+        load_w1(1)
+        load_x(1)
+        for j in range(2, G):
+            load_w1(j)
+        nc.sync.dma_start(out=scale_sb[:], in_=w2_scale.rearrange("o (p k) z -> p (o k z)", k=PACK))
+        nc.sync.dma_start(out=b1_sb[:], in_=b1.rearrange("(p k) -> p k", k=PACK))
+        nc.sync.dma_start(out=ls_bf[:], in_=ls.rearrange("(p k) -> p k", k=PACK))
+        for b in range(3):
+            w2_raw[b] = keep.tile([P, PACK, 2, C], U8, name="w2_raw%d" % b, align_bytes=64)
+            for i in range(2):
+                nc.sync.dma_start(
+                    out=w2_raw[b][:, :, i, :], in_=w2_bytes[2 * b + i].rearrange("(p k) d -> p k d", k=PACK)
+                )
+
+        zeros = keep.tile([P, C], BF16, name="zeros", align_bytes=64)
+        nc.vector.memset(zeros[:], 0.0)
         ident = keep.tile([P, P], F32, name="ident")
         make_identity(nc, ident[:])
-        warm = keep.tile([P, 1], F32, name="warm")
-        nc.gpsimd.memset(warm[:], 0.0)
-        nc.scalar.activation(out=warm[:], in_=warm[:], func=ACT.Sigmoid)
-        nc.gpsimd.tensor_copy(out=ls32[:], in_=ls_sb[:])
+        spare = keep.tile([P, 1], F32, name="spare")
+        nc.gpsimd.memset(spare[:], 0.0)
+        nc.scalar.activation(out=spare[:], in_=spare[:], func=ACT.Sigmoid)
+        nc.gpsimd.tensor_copy(out=ls_sb[:], in_=ls_bf[:])
 
-        xc = [[keep.tile([P, 3, P], U32, name="xc%d_%d" % (a, q), align_bytes=64) for q in range(3)] for a in range(2)]
-        xsc = [[keep.tile([P, 3, P], U8, name="xsc%d_%d" % (a, q), align_bytes=64) for q in range(3)] for a in range(2)]
-        w1c = [keep.tile([P, C], U32, name="w1c%d" % j, align_bytes=64) for j in range(G)]
-        w1s = [keep.tile([P, C], U8, name="w1s%d" % j, align_bytes=64) for j in range(G)]
-        w2c = [keep.tile([P, C], U32, name="w2c%d" % j, align_bytes=64) for j in range(G)]
-        w2s = [keep.tile([P, C], U8, name="w2s%d" % j, align_bytes=64) for j in range(G)]
+        def mx_tiles(name, shape):
+            codes = keep.tile(shape, U32, name=name + "_codes", align_bytes=64)
+            scales = keep.tile(shape, U8, name=name + "_scales", align_bytes=64)
+            return codes, scales
+
+        x_mx = [[mx_tiles("x%d_%d" % (a, q), [P, 3, P]) for q in range(3)] for a in range(2)]
+        w1_mx = [mx_tiles("w1_%d" % j, [P, C]) for j in range(G)]
+        w2_mx = [mx_tiles("w2_%d" % j, [P, C]) for j in range(G)]
+        e_mx = [[mx_tiles("e%d_%d" % (a, q), [P, 2, P]) for q in range(3)] for a in range(2)]
         y_sb = keep.tile([P, 2, 4, G, P], F32, name="y_sb", align_bytes=64)
-        m3 = keep.tile([P, 2, 4, 3, P], F32, name="m3", align_bytes=64)
-        m_sb = keep.tile([P, 2, 4, P], F32, name="m_sb", align_bytes=64)
-        s_sb = keep.tile([P, 2, 4, P], F32, name="s_sb", align_bytes=64)
-        eg = {}
-        ec = [[keep.tile([P, 2, P], U32, name="ec%d_%d" % (a, q), align_bytes=64) for q in range(3)] for a in range(2)]
-        es = [[keep.tile([P, 2, P], U8, name="es%d_%d" % (a, q), align_bytes=64) for q in range(3)] for a in range(2)]
-        xg = {}
-        tb = {}
+        top3 = keep.tile([P, 2, 4, 3, P], F32, name="top3", align_bytes=64)
+        top = keep.tile([P, 2, 4, P], F32, name="top", align_bytes=64)
+        gate_sb = keep.tile([P, 2, 4, P], F32, name="gate_sb", align_bytes=64)
 
-        def copy(eng, out, in_):
-            if eng == "S":
+        turned = {}
+        x_mixed = {}
+        w1_mixed = {}
+        w2_wide = {}
+        w2_mixed = {}
+        e_mixed = {}
+        copied = {}
+
+        def quantize(mx, index, in_):
+            codes, scales = mx
+            nc.vector.quantize_mx(out=codes[index].bitcast(FP8X4), scales=scales[index], in_=in_)
+
+        def copy(engine, out, in_):
+            if engine == "scalar":
                 nc.scalar.copy(out=out, in_=in_)
             else:
                 nc.vector.tensor_copy(out=out, in_=in_)
 
-        def x_transpose(a, b, slot):
-            t = bank([P, 2, 2, P], slot)
+        closed = list(range(8))
+        opened = []
+        banks = {}
+        passes = {}
+
+        def group_of(step):
+            if step[0] == "conv1":
+                a, t, q = step[1:4]
+                return ("conv1", a, t, 0 if one_by_one(a, t) and q < 2 else q)
+            if step[0] == "conv2":
+                a, h, j, part = step[1:]
+                return ("conv2", a, goal(h, j), part)
+            return ("warm",) if step[0] == "warm" else step
+
+        sizes = {}
+        count = {}
+        tensor = tensor_steps()
+        for step in tensor:
+            sizes[group_of(step)] = sizes.get(group_of(step), 0) + 1
+
+        def reader_of(group):
+            names = {"turn": "fetch", "conv1": "y", "conv2": "store"}
+            return (names[group[0]],) + group[1:] if group[0] in names else None
+
+        def bank_is_free(group):
+            if group in banks:
+                return True
+            same = [g for i, g in enumerate(opened) if closed[i] == closed[len(opened)]]
+            return not same or reader_of(same[-1]) is None or reader_of(same[-1]) in done
+
+        def take_bank(step, shape):
+            group = group_of(step)
+            if group not in banks:
+                banks[group] = psum.tile(shape, F32, name="bank%d" % closed[len(opened)])
+                opened.append(group)
+            passes[group] = passes.get(group, 0) + 1
+            if passes[group] == sizes[group]:
+                closed.append(closed[opened.index(group)])
+            return banks[group]
+
+
+        def warm(engine, i):
+            acc = take_bank(("warm", i), [P, C])
+            nc.tensor.matmul(out=acc[:], lhsT=zeros[:, 0:P], rhs=zeros[:], start=True, stop=True)
+
+        def turn(engine, a, b):
+            acc = take_bank(("turn", a, b), [P, 2, 2, P])
             for i in range(2):
-                words = xs[a, b][:, i, :].bitcast(F32)
+                words = x_raw[a, b][:, i, :].bitcast(F32)
                 for u in range(2):
-                    nc.tensor.transpose(t[:, i, u, :], words[:, u : C // 2 : 2], ident[:])
-            tb[a, b] = t
+                    nc.tensor.transpose(acc[:, i, u, :], words[:, u : C // 2 : 2], ident[:])
 
-        def x_evac(a, b, eng):
-            xg[a, b] = keep.tile([P, 2, P, 4], BF16, name="xg", tag="xg", align_bytes=64, bufs=6)
+        def fetch(engine, a, b):
+            x_mixed[a, b] = keep.tile([P, 2, P, PACK], BF16, name="mixed", align_bytes=64, bufs=6)
+            words = x_mixed[a, b][:].rearrange("p i r k -> p (i r k)").bitcast(F32)
             copy(
-                eng,
-                xg[a, b][:].rearrange("p i n t -> p (i n t)").bitcast(F32).rearrange("p (i r u) -> p i r u", i=2, u=2),
-                tb[a, b][:].rearrange("p i u r -> p i r u"),
+                engine,
+                words.rearrange("p (i r u) -> p i r u", i=2, u=2),
+                banks["turn", a, b][:].rearrange("p i u r -> p i r u"),
             )
 
-        def x_quant(a, h, dup):
+        def xq(engine, a, h, again):
             q = [i for i in range(3) if h in PAIRS[i]][0]
-            slot = 2 if dup else PAIRS[q].index(h)
-            nc.vector.quantize_mx(
-                out=xc[a][q][:, slot, :].bitcast(FP8X4),
-                scales=xsc[a][q][:, slot, :],
-                in_=xg[a, h // 2][:, h % 2].rearrange("p n t -> p (n t)"),
-            )
+            slot = 2 if again else PAIRS[q].index(h)
+            quantize(x_mx[a][q], (slice(0, P), slot), x_mixed[a, h // 2][:, h % 2].rearrange("p r k -> p (r k)"))
 
-        wg = {}
-
-        def w1_inter(j, th, eng):
-            t0, t1 = (0, 4) if th == 2 else (2 * th, 2 * th + 2)
-            g = work.tile([P, t1 - t0, P, 4], BF16, name="wg", align_bytes=64, bufs=8)
-            copy(eng, g[:], w1_raw[j][:].rearrange("p j (m t) -> p t m j", t=4)[:, t0:t1])
-            wg[j, th] = g
-
-        def w1_quant(j, th):
-            cols = slice(0, C) if th == 2 else slice(2 * th * P, 2 * (th + 1) * P)
-            nc.vector.quantize_mx(
-                out=w1c[j][:, cols].bitcast(FP8X4),
-                scales=w1s[j][:, cols],
-                in_=wg[j, th][:].rearrange("p t m j -> p (t m j)"),
-            )
-
-        wide = {}
-        grp = {}
-
-        def w2_widen(b, t, eng):
-            if b not in wide:
-                wide[b] = work.tile([P, 4, 2, C], BF16, name="wide", align_bytes=64, bufs=3)
-            src = w2_raw[b][:, t].rearrange("p j d -> p (j d)").bitcast(FP8)
-            dst = wide[b][:, t].rearrange("p j d -> p (j d)")
-            if eng == "S":
-                nc.scalar.activation(out=dst, in_=src, func=ACT.Copy, scale=sc_sb[:, t : t + 1])
-            else:
-                nc.vector.tensor_scalar(out=dst, in0=src, scalar1=sc_sb[:, t : t + 1], scalar2=None, op0=ALU.mult)
-
-        def w2_inter(j, eng):
-            grp[j] = work.tile([P, C, 4], BF16, name="grp", align_bytes=64, bufs=6)
+        def mix1(engine, j, s):
+            w1_mixed[j, s] = work.tile([P, 2, P, PACK], BF16, name="w1_mixed", align_bytes=64, bufs=MIX1_BUFS)
             copy(
-                eng,
-                grp[j][:].rearrange("p (c i) t -> p c t i", i=4),
-                wide[j // 2][:, :, j % 2, :].rearrange("p t (c i) -> p c t i", i=4),
+                engine,
+                w1_mixed[j, s][:].rearrange("p t m k -> p m k t"),
+                w1_raw[j][:].rearrange("p k (m t) -> p m k t", t=4)[:, :, :, 2 * s : 2 * s + 2],
             )
 
-        def w2_quant(j):
-            nc.vector.quantize_mx(
-                out=w2c[j][:].bitcast(FP8X4), scales=w2s[j][:], in_=grp[j][:].rearrange("p n t -> p (n t)")
-            )
+        def w1q(engine, j, s):
+            cols = slice(2 * s * P, 2 * (s + 1) * P)
+            quantize(w1_mx[j], (slice(0, P), cols), w1_mixed[j, s][:].rearrange("p t m k -> p (t m k)"))
 
-        def window(gp, j):
-            ha, hb = [[h for h in range(G) if K[h][g] == j][0] for g in PAIRS[gp]]
-            for q in range(3):
-                if PAIRS[q] == (ha, hb):
-                    return q, 0
-                if PAIRS[q] == (hb, ha):
-                    return q, 1
-            raise ValueError("no window")
-
-        def conv1(acc, a, t, gp, j, first, last):
-            q, s0 = window(gp, j)
-            cols = slice(t * P, (t + 1) * P)
-            nc.tensor.matmul_mx(
-                out=acc,
-                lhsT=w1c[j][:, cols].bitcast(FP8X4),
-                lhsT_scale=w1s[j][:, cols],
-                rhs=xc[a][q][:, s0 : s0 + 2, :].rearrange("p s n -> p (s n)").bitcast(FP8X4),
-                rhs_scale=xsc[a][q][:, s0 : s0 + 2, :].rearrange("p s n -> p (s n)"),
-                start=first,
-                stop=last,
-            )
-
-        def y_evac(out, in_, t, eng):
-            if eng == "S":
-                nc.scalar.activation(out=out, in_=in_, func=ACT.Identity, bias=b1_sb[:, t : t + 1])
-            else:
-                nc.vector.tensor_scalar(out=out, in0=in_, scalar1=b1_sb[:, t : t + 1], scalar2=None, op0=ALU.add)
-
-        def pool_max0(a, tt):
-            nc.vector.tensor_tensor(out=m3[:, a, tt], in0=y_sb[:, a, tt, 0:3, :], in1=y_sb[:, a, tt, 3:6, :], op=ALU.max)
-
-        def pool_max1(a, tt):
-            nc.vector.tensor_tensor(out=m_sb[:, a, tt], in0=m3[:, a, tt, 0, :], in1=m3[:, a, tt, 1, :], op=ALU.max)
-
-        def pool_max2(a, tt):
-            nc.vector.tensor_tensor(out=m_sb[:, a, tt], in0=m_sb[:, a, tt], in1=m3[:, a, tt, 2, :], op=ALU.max)
-
-        def gate(a, tt):
-            nc.scalar.activation(out=s_sb[:, a, tt], in_=m_sb[:, a, tt], func=ACT.Sigmoid)
-
-        def gain(a, t, eng):
-            if eng == "S":
-                nc.scalar.activation(out=s_sb[:, a, t], in_=s_sb[:, a, t], func=ACT.Copy, scale=ls32[:, t : t + 1])
+        def widen(engine, b, k):
+            if b not in w2_wide:
+                w2_wide[b] = work.tile([P, PACK, 2, C], BF16, name="w2_wide", align_bytes=64, bufs=3)
+            values = w2_raw[b][:, k].rearrange("p i d -> p (i d)").bitcast(FP8)
+            wide = w2_wide[b][:, k].rearrange("p i d -> p (i d)")
+            if engine == "scalar":
+                nc.scalar.activation(out=wide, in_=values, func=ACT.Copy, scale=scale_sb[:, k : k + 1])
             else:
                 nc.vector.tensor_scalar(
-                    out=s_sb[:, a, t], in0=s_sb[:, a, t], scalar1=ls32[:, t : t + 1], scalar2=None, op0=ALU.mult
+                    out=wide, in0=values, scalar1=scale_sb[:, k : k + 1], scalar2=None, op0=ALU.mult
                 )
 
-        def e_mult(a, pos):
-            if (a, pos // 2) not in eg:
-                eg[a, pos // 2] = keep.tile([P, 2, P, 4], BF16, name="eg", tag="xg", align_bytes=64, bufs=6)
+        def mix2(engine, j):
+            w2_mixed[j] = work.tile([P, C, PACK], BF16, name="w2_mixed", align_bytes=64, bufs=6)
+            copy(
+                engine,
+                w2_mixed[j][:].rearrange("p (c i) k -> p c k i", i=4),
+                w2_wide[j // 2][:, :, j % 2, :].rearrange("p k (c i) -> p c k i", i=4),
+            )
+
+        def w2q(engine, j):
+            quantize(w2_mx[j], (slice(0, P), slice(0, C)), w2_mixed[j][:].rearrange("p d k -> p (d k)"))
+
+        def conv1(engine, a, t, q, j):
+            step = ("conv1", a, t, q, j)
+            acc = take_bank(step, [P, C])
+            count[step[:4]] = count.get(step[:4], 0) + 1
+            c0 = 2 * P * q if group_of(step)[3] == 0 else 0
+            pair, slot = window(q, j)
+            rows = (slice(0, P), slice(slot, slot + 2))
+            codes, scales = x_mx[a][pair]
+            nc.tensor.matmul_mx(
+                out=acc[:, c0 : c0 + 2 * P],
+                lhsT=w1_mx[j][0][:, t * P : (t + 1) * P].bitcast(FP8X4),
+                lhsT_scale=w1_mx[j][1][:, t * P : (t + 1) * P],
+                rhs=codes[rows].rearrange("p s r -> p (s r)").bitcast(FP8X4),
+                rhs_scale=scales[rows].rearrange("p s r -> p (s r)"),
+                start=(count[step[:4]] == 1),
+                stop=(count[step[:4]] == G),
+            )
+
+        def y_out(engine, a, t, q):
+            pairs = 2 if one_by_one(a, t) and q == 0 else 1
+            dst = y_sb[:, a, t, 2 * q : 2 * (q + pairs), :].rearrange("p g r -> p (g r)")
+            src = banks["conv1", a, t, q][:, 0 : 2 * P * pairs]
+            if engine == "scalar":
+                nc.scalar.activation(out=dst, in_=src, func=ACT.Identity, bias=b1_sb[:, t : t + 1])
+            else:
+                nc.vector.tensor_scalar(out=dst, in0=src, scalar1=b1_sb[:, t : t + 1], scalar2=None, op0=ALU.add)
+
+        def max1(engine, a, s):
+            t = slice(2 * s, 2 * s + 2)
+            nc.vector.tensor_tensor(out=top3[:, a, t], in0=y_sb[:, a, t, 0:3, :], in1=y_sb[:, a, t, 3:6, :], op=ALU.max)
+
+        def max2(engine, a, s):
+            t = slice(2 * s, 2 * s + 2)
+            nc.vector.tensor_tensor(out=top[:, a, t], in0=top3[:, a, t, 0, :], in1=top3[:, a, t, 1, :], op=ALU.max)
+
+        def max3(engine, a, s):
+            t = slice(2 * s, 2 * s + 2)
+            nc.vector.tensor_tensor(out=top[:, a, t], in0=top[:, a, t], in1=top3[:, a, t, 2, :], op=ALU.max)
+
+        def gate(engine, a, s):
+            t = slice(2 * s, 2 * s + 2)
+            nc.scalar.activation(out=gate_sb[:, a, t], in_=top[:, a, t], func=ACT.Sigmoid)
+
+        def gain(engine, a, t):
+            g = gate_sb[:, a, t]
+            if engine == "scalar":
+                nc.scalar.activation(out=g, in_=g, func=ACT.Copy, scale=ls_sb[:, t : t + 1])
+            else:
+                nc.vector.tensor_scalar(out=g, in0=g, scalar1=ls_sb[:, t : t + 1], scalar2=None, op0=ALU.mult)
+
+        def gated(engine, a, i):
+            if (a, i // 2) not in e_mixed:
+                e_mixed[a, i // 2] = keep.tile([P, 2, P, PACK], BF16, name="mixed", align_bytes=64, bufs=6)
             nc.vector.tensor_tensor(
-                out=eg[a, pos // 2][:, pos % 2].rearrange("p (c i) t -> p c t i", i=4),
-                in0=y_sb[:, a, :, pos, :].rearrange("p t (c i) -> p c t i", i=4),
-                in1=s_sb[:, a].rearrange("p t (c i) -> p c t i", i=4),
+                out=e_mixed[a, i // 2][:, i % 2].rearrange("p (c r) t -> p c t r", r=4),
+                in0=y_sb[:, a, :, i, :].rearrange("p t (c r) -> p c t r", r=4),
+                in1=gate_sb[:, a].rearrange("p t (c r) -> p c t r", r=4),
                 op=ALU.mult,
             )
 
-        def e_quant(a, q, i0, i1):
-            nc.vector.quantize_mx(
-                out=ec[a][q][:, i0:i1, :].rearrange("p s n -> p (s n)").bitcast(FP8X4),
-                scales=es[a][q][:, i0:i1, :].rearrange("p s n -> p (s n)"),
-                in_=eg[a, q][:, i0:i1].rearrange("p s n t -> p (s n t)"),
-            )
+        def eq(engine, a, i):
+            quantize(e_mx[a][i // 2], (slice(0, P), i % 2), e_mixed[a, i // 2][:, i % 2].rearrange("p r t -> p (r t)"))
 
-        def conv2(acc, a, h, j, c0, c1, first, last):
-            i = POS.index(h)
+        def conv2(engine, a, h, j, part):
+            step = ("conv2", a, h, j, part)
+            acc = take_bank(step, [P, C])
+            group = group_of(step)
+            c0, c1 = PARTS[part]
+            i = ORDER.index(h)
+            codes, scales = e_mx[a][i // 2]
             nc.tensor.matmul_mx(
-                out=acc,
-                lhsT=ec[a][i // 2][:, i % 2, :].bitcast(FP8X4),
-                lhsT_scale=es[a][i // 2][:, i % 2, :],
-                rhs=w2c[j][:, c0:c1].bitcast(FP8X4),
-                rhs_scale=w2s[j][:, c0:c1],
-                start=first,
-                stop=last,
+                out=acc[:, 0 : c1 - c0],
+                lhsT=codes[:, i % 2, :].bitcast(FP8X4),
+                lhsT_scale=scales[:, i % 2, :],
+                rhs=w2_mx[j][0][:, c0:c1].bitcast(FP8X4),
+                rhs_scale=w2_mx[j][1][:, c0:c1],
+                start=(passes[group] == 1),
+                stop=(passes[group] == G),
             )
 
-        def store(acc, a, g, c0, c1, eng):
-            o = work.tile([P, c1 - c0], F32, name="o_sb", bufs=6)
-            copy(eng, o[:], acc[:, 0 : c1 - c0])
-            nc.sync.dma_start(out=out[a * P : (a + 1) * P, g, c0:c1], in_=o[:])
+        def store(engine, a, g, part):
+            width = PARTS[part][1] - PARTS[part][0]
+            copied[a, g, part] = work.tile([P, width], F32, name="copied", bufs=COPIED_BUFS)
+            copy(engine, copied[a, g, part][:], banks["conv2", a, g, part][:, 0:width])
 
-        banks = {}
-        count = {}
+        def send(engine, a, g, part):
+            c0, c1 = PARTS[part]
+            nc.sync.dma_start(out=out[a * P : (a + 1) * P, g, c0:c1], in_=copied[a, g, part][:])
 
-        def group(key, bank_key, c0, c1):
-            if bank_key not in banks:
-                banks[bank_key] = bank([P, C], SLOTS[bank_key])
-            count[key] = count.get(key, 0) + 1
-            return banks[bank_key][:, c0:c1], count[key] == 1, count[key] == G
+        def needs(step):
+            name, args = step[0], step[1:]
+            if name == "fetch":
+                return [("turn",) + args]
+            if name == "xq":
+                return [("fetch", args[0], args[1] // 2)]
+            if name == "mix1":
+                return [("w1q",) + key for key in list(w1_mixed)[-MIX1_BUFS:][:1]] if len(w1_mixed) >= MIX1_BUFS else []
+            if name == "w1q":
+                return [("mix1",) + args]
+            if name == "mix2":
+                return [("widen", args[0] // 2, k) for k in range(PACK)]
+            if name == "w2q":
+                return [("mix2",) + args]
+            if name == "conv1":
+                a, t, q, j = args
+                pair, slot = window(q, j)
+                return [("w1q", j, t // 2), ("xq", a, PAIRS[pair][0], slot), ("xq", a, PAIRS[pair][1], 0)]
+            if name == "y":
+                return members[("conv1",) + args]
+            if name == "max1":
+                a, s = args
+                return [("y",) + key[1:] for key in members if key[0] == "conv1" and key[1] == a and key[2] // 2 == s]
+            if name in ("max2", "max3", "gate"):
+                return [({"max2": "max1", "max3": "max2", "gate": "max3"}[name],) + args]
+            if name == "gain":
+                return [("gate", args[0], args[1] // 2)]
+            if name == "e":
+                return [("gain", args[0], t) for t in range(4)]
+            if name == "eq":
+                return [("e",) + args]
+            if name == "conv2":
+                a, h, j, part = args
+                return [("eq", a, ORDER.index(h)), ("w2q", j)]
+            if name == "store":
+                turn_to_send = sends.index(("send",) + args)
+                return members[("conv2",) + args] + sends[: max(0, turn_to_send - COPIED_BUFS + 1)]
+            if name == "send":
+                return [("store",) + args]
+            return []
 
-        for step in PROGRAM:
-            kind, arg, eng = step[0], step[1:-1], step[-1]
-            if kind == "Z":
-                if "Z" not in banks:
-                    banks["Z"] = bank([P, C], SLOTS["Z",])
-                nc.tensor.matmul(out=banks["Z"][:], lhsT=zero[:, 0:P], rhs=zero[:], start=True, stop=True)
-            elif kind == "T":
-                x_transpose(arg[0], arg[1], SLOTS[("T",) + arg])
-            elif kind == "E":
-                x_evac(arg[0], arg[1], eng)
-            elif kind == "Q":
-                x_quant(arg[0], arg[1], arg[2] == 1)
-            elif kind == "I":
-                w1_inter(arg[0], arg[1], eng)
-            elif kind == "q":
-                w1_quant(arg[0], arg[1])
-            elif kind == "W":
-                w2_widen(arg[0], arg[1], eng)
-            elif kind == "I2":
-                w2_inter(arg[0], eng)
-            elif kind == "q2":
-                w2_quant(arg[0])
-            elif kind == "A":
-                a, t, gp, j = arg
-                if (a, t) in YMERGE and gp < 2:
-                    acc, first, last = group(step[:4], ("A", a, t, 0), 256 * gp, 256 * gp + 256)
-                else:
-                    acc, first, last = group(step[:4], step[:4], 0, 256)
-                conv1(acc, a, t, gp, j, first, last)
-            elif kind == "Y":
-                a, t, gp = arg
-                w = 2 if (a, t) in YMERGE and gp == 0 else 1
-                y_evac(
-                    y_sb[:, a, t, 2 * gp : 2 * gp + 2 * w, :].rearrange("p g n -> p (g n)"),
-                    banks["A", a, t, gp][:, 0 : 256 * w],
-                    t,
-                    eng,
-                )
-            elif kind in ("M0", "M1", "M2", "g"):
-                f = {"M0": pool_max0, "M1": pool_max1, "M2": pool_max2, "g": gate}[kind]
-                f(arg[0], slice(0, 4) if arg[1] == 2 else slice(2 * arg[1], 2 * arg[1] + 2))
-            elif kind == "n":
-                gain(arg[0], arg[1], eng)
-            elif kind == "e":
-                e_mult(arg[0], arg[1])
-            elif kind == "eq":
-                if len(arg) == 2:
-                    e_quant(arg[0], arg[1], 0, 2)
-                else:
-                    e_quant(arg[0], arg[1], arg[2] % 2, arg[2] % 2 + 1)
-            elif kind == "D":
-                a, dh, pos, j = arg
-                h = POS[pos]
-                g = [gg for gg in range(G) if K[h][gg] == j][0]
-                c0, c1 = COLS[dh]
-                acc, first, last = group(("D", a, dh, g), ("D", a, dh, g), 0, c1 - c0)
-                conv2(acc, a, h, j, c0, c1, first, last)
-            elif kind == "O":
-                a, dh, g = arg
-                store(banks["D", a, dh, g], a, g, *COLS[dh], eng)
+        members = {}
+        for step in tensor:
+            members.setdefault(group_of(step), []).append(step)
+        closing = {members[group][-1]: group for group in members}
+        sends = [("send",) + closing[step][1:] for step in tensor if step in closing and step[0] == "conv2"]
+
+        actions = {
+            "warm": warm, "turn": turn, "fetch": fetch, "xq": xq, "mix1": mix1, "w1q": w1q, "widen": widen,
+            "mix2": mix2, "w2q": w2q, "conv1": conv1, "y": y_out, "max1": max1, "max2": max2, "max3": max3,
+            "gate": gate, "gain": gain, "e": gated, "eq": eq, "conv2": conv2, "store": store, "send": send,
+        }
+        vector, scalar = parse(VECTOR), parse(SCALAR)
+        queues = {
+            "tensor": tensor,
+            "vector": vector,
+            "scalar": scalar,
+            "sync": sends,
+        }
+        done = set()
+        place = {engine: 0 for engine in queues}
+        while any(place[engine] < len(queues[engine]) for engine in queues):
+            moved = sum(place.values())
+            for engine in queues:
+                while place[engine] < len(queues[engine]):
+                    step = queues[engine][place[engine]]
+                    if any(need not in done for need in needs(step)):
+                        break
+                    if engine == "tensor" and not bank_is_free(group_of(step)):
+                        break
+                    actions[step[0]](engine, *step[1:])
+                    done.add(step)
+                    place[engine] += 1
+            assert sum(place.values()) > moved, "no queue can go on"

from contextlib import ExitStack

import concourse.mybir as mybir
from concourse.masks import make_identity

N, G, C = 256, 6, 512
FLOPS = 2 * 2 * N * G * C * G * C

K = (
    (0, 1, 2, 3, 4, 5),
    (2, 0, 1, 5, 3, 4),
    (1, 2, 0, 4, 5, 3),
    (3, 5, 4, 0, 2, 1),
    (4, 3, 5, 1, 0, 2),
    (5, 4, 3, 2, 1, 0),
)
PAIRS = ((0, 3), (1, 5), (2, 4))
ORDER = (0, 3, 1, 5, 2, 4)

P = 128
PACK = 4
COPIED_BUFS = 6
MIX1_BUFS = 8
F32 = mybir.dt.float32
BF16 = mybir.dt.bfloat16
U32 = mybir.dt.uint32
U8 = mybir.dt.uint8
FP8 = mybir.dt.float8_e4m3fn
FP8X4 = mybir.dt.float8_e4m3fn_x4
ACT = mybir.ActivationFunctionType
ALU = mybir.AluOpType

PARTS = ((0, C), (0, C // 2), (C // 2, C))

VECTOR = """
mix1:01 w1q:01 w1q:00 fetch:01 xq:000 xq:010 xq:030 xq:020 xq:050 xq:040 xq:011 mix1:11 xq:021 w1q:10 xq:001
w1q:11 xq:101 xq:110 mix1:20 xq:100 w1q:20 mix1:30 xq:111 xq:130 xq:120 xq:121 xq:150 xq:140 w1q:30 w1q:21
mix1:41 w1q:40 mix1:31 w1q:50 widen:00 widen:03 w1q:31 w1q:41 w1q:51 widen:01 y:012 widen:11 mix2:1 max1:00
widen:10 mix2:0 w2q:1 max1:01 max2:00 max2:01 max3:00 w2q:0 max3:01 widen:23 gain:00 gain:02 y:112 e:02 e:00
e:03 eq:00 e:01 e:05 eq:01 eq:02 e:04 eq:05 eq:03 eq:04 w2q:2 max1:10 mix2:4 w2q:3 max1:11 w2q:4 max2:11
max2:10 max3:11 max3:10 w2q:5 gain:10 gain:12 e:10 eq:10 e:11 eq:11 e:12 store:030 eq:12 e:13 eq:13 e:14
eq:14 e:15 eq:15 store:100 store:120 store:130 store:152
"""
SCALAR = """
mix1:00 fetch:00 fetch:02 mix1:10 fetch:10 mix1:21 fetch:11 fetch:12 mix1:40 mix1:50 mix1:51 y:000 widen:02
y:002 y:010 y:001 widen:12 y:011 y:022 widen:13 y:020 y:101 y:032 y:030 y:100 mix2:2 gate:00 gate:01 gain:01
gain:03 y:102 widen:20 y:120 y:122 y:110 widen:22 widen:21 mix2:3 y:130 y:132 mix2:5 gate:11 gate:10 gain:11
gain:13 store:050 store:010 store:000 store:020 store:040 store:110 store:140 store:151
"""


def tensor_steps():
    steps = [("warm", i) for i in range(8)]
    steps += [("turn", 0, b) for b in range(3)]
    steps += [("warm", 8)]

    def first(j):
        return [("conv1", 0, t, q, j) for q in range(3) for t in range(2)]

    def second(j):
        return [("conv1", 1, 0, q, j) for q in range(2)]

    steps += first(0) + [("turn", 1, 0)] + first(1) + [("turn", 1, 1), ("turn", 1, 2)] + first(2)
    steps += second(0) + second(1) + second(2)
    for j in range(3, G):
        steps += first(j) + second(j)

    for a in range(2):
        for t in range(4):
            for q in range(3):
                for j in range(G):
                    if ("conv1", a, t, q, j) not in steps:
                        steps.append(("conv1", a, t, q, j))

    steps += [("conv2", 0, h, j, 0) for h in ORDER for j in range(2)]
    steps += [("conv2", 0, h, j, 0) for j in range(2, G) for h in ORDER]
    steps += [("conv2", 1, h, K[h][g], 0) for h in ORDER for g in range(4)]
    steps += [("conv2", 1, h, K[h][4], 0) for h in ORDER]
    steps += [("conv2", 1, h, K[h][5], part) for part in (1, 2) for h in ORDER]
    return steps


def parse(text):
    return [(w.split(":")[0],) + tuple(int(d) for d in w.split(":")[1]) for w in text.split()]


def window(q, j):
    h = [[h for h in range(G) if K[h][g] == j][0] for g in PAIRS[q]]
    pair = [i for i in range(3) if h[0] in PAIRS[i]][0]
    return pair, PAIRS[pair].index(h[0])


def goal(h, j):
    return K[h].index(j)


def one_by_one(a, t):
    return (a, t) not in ((0, 0), (0, 1), (1, 0))


def tile_dihedralthreegroupblock_kernel(tc, x, w1, b1, ls, w2_bytes, w2_scale, out):
    nc = tc.nc
    with ExitStack() as ctx:
        keep = ctx.enter_context(tc.tile_pool(name="keep", bufs=1))
        work = ctx.enter_context(tc.tile_pool(name="work", bufs=6))
        psum = ctx.enter_context(tc.psum_pool(name="psum", bufs=1))
        ctx.enter_context(tc.manual_schedule())

        x_raw = {}
        w1_raw = {}
        w2_raw = {}
        b1_sb = keep.tile([P, PACK], BF16, name="b1_sb")
        ls_bf = keep.tile([P, PACK], BF16, name="ls_bf")
        ls_sb = keep.tile([P, PACK], F32, name="ls_sb")
        scale_sb = keep.tile([P, PACK], F32, name="scale_sb")

        def load_w1(j):
            w1_raw[j] = keep.tile([P, PACK, C], BF16, name="w1_raw%d" % j, align_bytes=64)
            nc.sync.dma_start(out=w1_raw[j][:], in_=w1[j].rearrange("(p k) d -> p k d", k=PACK))

        def load_x(a):
            for b in range(3):
                x_raw[a, b] = keep.tile([P, 2, C], BF16, name="x_raw%d_%d" % (a, b), align_bytes=64)
                nc.sync.dma_start(out=x_raw[a, b][:], in_=x[a * P : (a + 1) * P, 2 * b : 2 * b + 2, :])

        load_w1(0)
        load_x(0)
        load_w1(1)
        load_x(1)
        for j in range(2, G):
            load_w1(j)
        nc.sync.dma_start(out=scale_sb[:], in_=w2_scale.rearrange("o (p k) z -> p (o k z)", k=PACK))
        nc.sync.dma_start(out=b1_sb[:], in_=b1.rearrange("(p k) -> p k", k=PACK))
        nc.sync.dma_start(out=ls_bf[:], in_=ls.rearrange("(p k) -> p k", k=PACK))
        for b in range(3):
            w2_raw[b] = keep.tile([P, PACK, 2, C], U8, name="w2_raw%d" % b, align_bytes=64)
            for i in range(2):
                nc.sync.dma_start(
                    out=w2_raw[b][:, :, i, :], in_=w2_bytes[2 * b + i].rearrange("(p k) d -> p k d", k=PACK)
                )

        zeros = keep.tile([P, C], BF16, name="zeros", align_bytes=64)
        nc.vector.memset(zeros[:], 0.0)
        ident = keep.tile([P, P], F32, name="ident")
        make_identity(nc, ident[:])
        spare = keep.tile([P, 1], F32, name="spare")
        nc.gpsimd.memset(spare[:], 0.0)
        nc.scalar.activation(out=spare[:], in_=spare[:], func=ACT.Sigmoid)
        nc.gpsimd.tensor_copy(out=ls_sb[:], in_=ls_bf[:])

        def mx_tiles(name, shape):
            codes = keep.tile(shape, U32, name=name + "_codes", align_bytes=64)
            scales = keep.tile(shape, U8, name=name + "_scales", align_bytes=64)
            return codes, scales

        x_mx = [[mx_tiles("x%d_%d" % (a, q), [P, 3, P]) for q in range(3)] for a in range(2)]
        w1_mx = [mx_tiles("w1_%d" % j, [P, C]) for j in range(G)]
        w2_mx = [mx_tiles("w2_%d" % j, [P, C]) for j in range(G)]
        e_mx = [[mx_tiles("e%d_%d" % (a, q), [P, 2, P]) for q in range(3)] for a in range(2)]
        y_sb = keep.tile([P, 2, 4, G, P], F32, name="y_sb", align_bytes=64)
        top3 = keep.tile([P, 2, 4, 3, P], F32, name="top3", align_bytes=64)
        top = keep.tile([P, 2, 4, P], F32, name="top", align_bytes=64)
        gate_sb = keep.tile([P, 2, 4, P], F32, name="gate_sb", align_bytes=64)

        turned = {}
        x_mixed = {}
        w1_mixed = {}
        w2_wide = {}
        w2_mixed = {}
        e_mixed = {}
        copied = {}

        def quantize(mx, index, in_):
            codes, scales = mx
            nc.vector.quantize_mx(out=codes[index].bitcast(FP8X4), scales=scales[index], in_=in_)

        def copy(engine, out, in_):
            if engine == "scalar":
                nc.scalar.copy(out=out, in_=in_)
            else:
                nc.vector.tensor_copy(out=out, in_=in_)

        closed = list(range(8))
        opened = []
        banks = {}
        passes = {}

        def group_of(step):
            if step[0] == "conv1":
                a, t, q = step[1:4]
                return ("conv1", a, t, 0 if one_by_one(a, t) and q < 2 else q)
            if step[0] == "conv2":
                a, h, j, part = step[1:]
                return ("conv2", a, goal(h, j), part)
            return ("warm",) if step[0] == "warm" else step

        sizes = {}
        count = {}
        tensor = tensor_steps()
        for step in tensor:
            sizes[group_of(step)] = sizes.get(group_of(step), 0) + 1

        def reader_of(group):
            names = {"turn": "fetch", "conv1": "y", "conv2": "store"}
            return (names[group[0]],) + group[1:] if group[0] in names else None

        def bank_is_free(group):
            if group in banks:
                return True
            same = [g for i, g in enumerate(opened) if closed[i] == closed[len(opened)]]
            return not same or reader_of(same[-1]) is None or reader_of(same[-1]) in done

        def take_bank(step, shape):
            group = group_of(step)
            if group not in banks:
                banks[group] = psum.tile(shape, F32, name="bank%d" % closed[len(opened)])
                opened.append(group)
            passes[group] = passes.get(group, 0) + 1
            if passes[group] == sizes[group]:
                closed.append(closed[opened.index(group)])
            return banks[group]


        def warm(engine, i):
            acc = take_bank(("warm", i), [P, C])
            nc.tensor.matmul(out=acc[:], lhsT=zeros[:, 0:P], rhs=zeros[:], start=True, stop=True)

        def turn(engine, a, b):
            acc = take_bank(("turn", a, b), [P, 2, 2, P])
            for i in range(2):
                words = x_raw[a, b][:, i, :].bitcast(F32)
                for u in range(2):
                    nc.tensor.transpose(acc[:, i, u, :], words[:, u : C // 2 : 2], ident[:])

        def fetch(engine, a, b):
            x_mixed[a, b] = keep.tile([P, 2, P, PACK], BF16, name="mixed", align_bytes=64, bufs=6)
            words = x_mixed[a, b][:].rearrange("p i r k -> p (i r k)").bitcast(F32)
            copy(
                engine,
                words.rearrange("p (i r u) -> p i r u", i=2, u=2),
                banks["turn", a, b][:].rearrange("p i u r -> p i r u"),
            )

        def xq(engine, a, h, again):
            q = [i for i in range(3) if h in PAIRS[i]][0]
            slot = 2 if again else PAIRS[q].index(h)
            quantize(x_mx[a][q], (slice(0, P), slot), x_mixed[a, h // 2][:, h % 2].rearrange("p r k -> p (r k)"))

        def mix1(engine, j, s):
            w1_mixed[j, s] = work.tile([P, 2, P, PACK], BF16, name="w1_mixed", align_bytes=64, bufs=MIX1_BUFS)
            copy(
                engine,
                w1_mixed[j, s][:].rearrange("p t m k -> p m k t"),
                w1_raw[j][:].rearrange("p k (m t) -> p m k t", t=4)[:, :, :, 2 * s : 2 * s + 2],
            )

        def w1q(engine, j, s):
            cols = slice(2 * s * P, 2 * (s + 1) * P)
            quantize(w1_mx[j], (slice(0, P), cols), w1_mixed[j, s][:].rearrange("p t m k -> p (t m k)"))

        def widen(engine, b, k):
            if b not in w2_wide:
                w2_wide[b] = work.tile([P, PACK, 2, C], BF16, name="w2_wide", align_bytes=64, bufs=3)
            values = w2_raw[b][:, k].rearrange("p i d -> p (i d)").bitcast(FP8)
            wide = w2_wide[b][:, k].rearrange("p i d -> p (i d)")
            if engine == "scalar":
                nc.scalar.activation(out=wide, in_=values, func=ACT.Copy, scale=scale_sb[:, k : k + 1])
            else:
                nc.vector.tensor_scalar(
                    out=wide, in0=values, scalar1=scale_sb[:, k : k + 1], scalar2=None, op0=ALU.mult
                )

        def mix2(engine, j):
            w2_mixed[j] = work.tile([P, C, PACK], BF16, name="w2_mixed", align_bytes=64, bufs=6)
            copy(
                engine,
                w2_mixed[j][:].rearrange("p (c i) k -> p c k i", i=4),
                w2_wide[j // 2][:, :, j % 2, :].rearrange("p k (c i) -> p c k i", i=4),
            )

        def w2q(engine, j):
            quantize(w2_mx[j], (slice(0, P), slice(0, C)), w2_mixed[j][:].rearrange("p d k -> p (d k)"))

        def conv1(engine, a, t, q, j):
            step = ("conv1", a, t, q, j)
            acc = take_bank(step, [P, C])
            count[step[:4]] = count.get(step[:4], 0) + 1
            c0 = 2 * P * q if group_of(step)[3] == 0 else 0
            pair, slot = window(q, j)
            rows = (slice(0, P), slice(slot, slot + 2))
            codes, scales = x_mx[a][pair]
            nc.tensor.matmul_mx(
                out=acc[:, c0 : c0 + 2 * P],
                lhsT=w1_mx[j][0][:, t * P : (t + 1) * P].bitcast(FP8X4),
                lhsT_scale=w1_mx[j][1][:, t * P : (t + 1) * P],
                rhs=codes[rows].rearrange("p s r -> p (s r)").bitcast(FP8X4),
                rhs_scale=scales[rows].rearrange("p s r -> p (s r)"),
                start=(count[step[:4]] == 1),
                stop=(count[step[:4]] == G),
            )

        def y_out(engine, a, t, q):
            pairs = 2 if one_by_one(a, t) and q == 0 else 1
            dst = y_sb[:, a, t, 2 * q : 2 * (q + pairs), :].rearrange("p g r -> p (g r)")
            src = banks["conv1", a, t, q][:, 0 : 2 * P * pairs]
            if engine == "scalar":
                nc.scalar.activation(out=dst, in_=src, func=ACT.Identity, bias=b1_sb[:, t : t + 1])
            else:
                nc.vector.tensor_scalar(out=dst, in0=src, scalar1=b1_sb[:, t : t + 1], scalar2=None, op0=ALU.add)

        def max1(engine, a, s):
            t = slice(2 * s, 2 * s + 2)
            nc.vector.tensor_tensor(out=top3[:, a, t], in0=y_sb[:, a, t, 0:3, :], in1=y_sb[:, a, t, 3:6, :], op=ALU.max)

        def max2(engine, a, s):
            t = slice(2 * s, 2 * s + 2)
            nc.vector.tensor_tensor(out=top[:, a, t], in0=top3[:, a, t, 0, :], in1=top3[:, a, t, 1, :], op=ALU.max)

        def max3(engine, a, s):
            t = slice(2 * s, 2 * s + 2)
            nc.vector.tensor_tensor(out=top[:, a, t], in0=top[:, a, t], in1=top3[:, a, t, 2, :], op=ALU.max)

        def gate(engine, a, s):
            t = slice(2 * s, 2 * s + 2)
            nc.scalar.activation(out=gate_sb[:, a, t], in_=top[:, a, t], func=ACT.Sigmoid)

        def gain(engine, a, t):
            g = gate_sb[:, a, t]
            if engine == "scalar":
                nc.scalar.activation(out=g, in_=g, func=ACT.Copy, scale=ls_sb[:, t : t + 1])
            else:
                nc.vector.tensor_scalar(out=g, in0=g, scalar1=ls_sb[:, t : t + 1], scalar2=None, op0=ALU.mult)

        def gated(engine, a, i):
            if (a, i // 2) not in e_mixed:
                e_mixed[a, i // 2] = keep.tile([P, 2, P, PACK], BF16, name="mixed", align_bytes=64, bufs=6)
            nc.vector.tensor_tensor(
                out=e_mixed[a, i // 2][:, i % 2].rearrange("p (c r) t -> p c t r", r=4),
                in0=y_sb[:, a, :, i, :].rearrange("p t (c r) -> p c t r", r=4),
                in1=gate_sb[:, a].rearrange("p t (c r) -> p c t r", r=4),
                op=ALU.mult,
            )

        def eq(engine, a, i):
            quantize(e_mx[a][i // 2], (slice(0, P), i % 2), e_mixed[a, i // 2][:, i % 2].rearrange("p r t -> p (r t)"))

        def conv2(engine, a, h, j, part):
            step = ("conv2", a, h, j, part)
            acc = take_bank(step, [P, C])
            group = group_of(step)
            c0, c1 = PARTS[part]
            i = ORDER.index(h)
            codes, scales = e_mx[a][i // 2]
            nc.tensor.matmul_mx(
                out=acc[:, 0 : c1 - c0],
                lhsT=codes[:, i % 2, :].bitcast(FP8X4),
                lhsT_scale=scales[:, i % 2, :],
                rhs=w2_mx[j][0][:, c0:c1].bitcast(FP8X4),
                rhs_scale=w2_mx[j][1][:, c0:c1],
                start=(passes[group] == 1),
                stop=(passes[group] == G),
            )

        def store(engine, a, g, part):
            width = PARTS[part][1] - PARTS[part][0]
            copied[a, g, part] = work.tile([P, width], F32, name="copied", bufs=COPIED_BUFS)
            copy(engine, copied[a, g, part][:], banks["conv2", a, g, part][:, 0:width])

        def send(engine, a, g, part):
            c0, c1 = PARTS[part]
            nc.sync.dma_start(out=out[a * P : (a + 1) * P, g, c0:c1], in_=copied[a, g, part][:])

        def needs(step):
            name, args = step[0], step[1:]
            if name == "fetch":
                return [("turn",) + args]
            if name == "xq":
                return [("fetch", args[0], args[1] // 2)]
            if name == "mix1":
                return [("w1q",) + key for key in list(w1_mixed)[-MIX1_BUFS:][:1]] if len(w1_mixed) >= MIX1_BUFS else []
            if name == "w1q":
                return [("mix1",) + args]
            if name == "mix2":
                return [("widen", args[0] // 2, k) for k in range(PACK)]
            if name == "w2q":
                return [("mix2",) + args]
            if name == "conv1":
                a, t, q, j = args
                pair, slot = window(q, j)
                return [("w1q", j, t // 2), ("xq", a, PAIRS[pair][0], slot), ("xq", a, PAIRS[pair][1], 0)]
            if name == "y":
                return members[("conv1",) + args]
            if name == "max1":
                a, s = args
                return [("y",) + key[1:] for key in members if key[0] == "conv1" and key[1] == a and key[2] // 2 == s]
            if name in ("max2", "max3", "gate"):
                return [({"max2": "max1", "max3": "max2", "gate": "max3"}[name],) + args]
            if name == "gain":
                return [("gate", args[0], args[1] // 2)]
            if name == "e":
                return [("gain", args[0], t) for t in range(4)]
            if name == "eq":
                return [("e",) + args]
            if name == "conv2":
                a, h, j, part = args
                return [("eq", a, ORDER.index(h)), ("w2q", j)]
            if name == "store":
                turn_to_send = sends.index(("send",) + args)
                return members[("conv2",) + args] + sends[: max(0, turn_to_send - COPIED_BUFS + 1)]
            if name == "send":
                return [("store",) + args]
            return []

        members = {}
        for step in tensor:
            members.setdefault(group_of(step), []).append(step)
        closing = {members[group][-1]: group for group in members}
        sends = [("send",) + closing[step][1:] for step in tensor if step in closing and step[0] == "conv2"]

        actions = {
            "warm": warm, "turn": turn, "fetch": fetch, "xq": xq, "mix1": mix1, "w1q": w1q, "widen": widen,
            "mix2": mix2, "w2q": w2q, "conv1": conv1, "y": y_out, "max1": max1, "max2": max2, "max3": max3,
            "gate": gate, "gain": gain, "e": gated, "eq": eq, "conv2": conv2, "store": store, "send": send,
        }
        vector, scalar = parse(VECTOR), parse(SCALAR)
        queues = {
            "tensor": tensor,
            "vector": vector,
            "scalar": scalar,
            "sync": sends,
        }
        done = set()
        place = {engine: 0 for engine in queues}
        while any(place[engine] < len(queues[engine]) for engine in queues):
            moved = sum(place.values())
            for engine in queues:
                while place[engine] < len(queues[engine]):
                    step = queues[engine][place[engine]]
                    if any(need not in done for need in needs(step)):
                        break
                    if engine == "tensor" and not bank_is_free(group_of(step)):
                        break
                    actions[step[0]](engine, *step[1:])
                    done.add(step)
                    place[engine] += 1
            assert sum(place.values()) > moved, "no queue can go on"
